import numpy as np
import ml_dtypes


def mxq(x, axis, fmt="e4m3"):
    dtype, down = {"e4m3": (ml_dtypes.float8_e4m3fn, 7), "e5m2": (ml_dtypes.float8_e5m2, 14)}[fmt]
    v = np.moveaxis(np.asarray(x, np.float32).astype(ml_dtypes.bfloat16).astype(np.float64), axis, -1)
    blocks = v.reshape(v.shape[:-1] + (-1, 32))
    amax = np.abs(blocks).max(-1, keepdims=True)
    byte = np.maximum(np.where(amax > 0, np.frexp(amax)[1] - 1 + 127, 0) - down, 1)
    scale = np.exp2(byte - 127.0)
    codes = (blocks / scale).astype(np.float32).astype(dtype).astype(np.float64)
    return np.moveaxis((codes * scale).reshape(v.shape), -1, axis)


WIDE = False


def mx_kscale(k):
    if not WIDE:
        return np.ones(k)
    levels = np.array([10, -10, 5, -5, 0])
    if k % 512:
        return np.exp2(np.random.permutation(np.resize(levels, k // 32))).repeat(32)
    a = np.empty((k // 512, 16))
    for p in range(k // 512):
        a[p, :8] = np.random.permutation(np.resize(levels, 8))
        for g in range(8):
            far = levels[np.abs(levels - a[p, g]) >= 10]
            a[p, g + 8] = far[np.random.randint(len(far))]
    return np.exp2(a.ravel()).repeat(32)


def f64(x):
    return np.asarray(x).astype(np.float64)


def striped(idx):
    return np.tile(idx.reshape(-1, 16).T, (8, 1)).astype(np.uint16)


def unstriped(offs):
    return offs[:16].T.reshape(-1).astype(np.int64)


E2M1 = np.array([0.0, 0.5, 1.0, 1.5, 2.0, 3.0, 4.0, 6.0, -0.0, -0.5, -1.0, -1.5, -2.0, -3.0, -4.0, -6.0])


def pack_weight(w, fmt):
    k, n = w.shape
    w = f64(np.asarray(w, np.float32).astype(ml_dtypes.bfloat16)).reshape(k // 32, 32, n)
    amax = np.abs(w).max(1)
    if fmt == "e4m3":
        byte = np.frexp(amax)[1] - 1 + 127 - 7
    else:
        mant, ex = np.frexp(amax / 6.0)
        byte = np.where(mant > 0.5, ex, ex - 1) + 127
    byte = np.clip(np.where(amax > 0, byte, 1), 1, 254)
    scaled = (w * np.exp2(127.0 - byte)[:, None, :]).reshape(k, n).astype(np.float32)
    by_word = np.ascontiguousarray(scaled.reshape(k // 512, 128, 4, n).transpose(0, 1, 3, 2))
    if fmt == "e4m3":
        words = by_word.astype(ml_dtypes.float8_e4m3fn).view(np.uint8)
    else:
        c = by_word.astype(ml_dtypes.float4_e2m1fn).view(np.uint8) & 0xF
        words = (c[..., 0::2] | (c[..., 1::2] << 4)).reshape(k // 512, 128, 2 * n)
    return np.ascontiguousarray(words), np.ascontiguousarray(byte.astype(np.uint8).reshape(k // 512, 16, n))


def unpack_weight(words, scales, fmt):
    g, _, n = scales.shape
    words = np.ascontiguousarray(words).reshape(g, 128, n, -1)
    if fmt == "e4m3":
        vals = words.view(ml_dtypes.float8_e4m3fn).astype(np.float64)
    else:
        nib = np.empty((g, 128, n, 4), np.uint8)
        nib[..., 0::2] = words & 0xF
        nib[..., 1::2] = words >> 4
        vals = E2M1[nib]
    vals = vals * np.repeat(np.exp2(scales.astype(np.float64) - 127.0), 8, axis=1)[..., None]
    return vals.transpose(0, 1, 3, 2).reshape(g * 512, n)


def gelu(v):
    return 0.5 * v * (1.0 + np.tanh(np.sqrt(2.0 / np.pi) * (v + 0.044715 * v**3)))


def bf(x):
    return np.asarray(x, np.float32).astype(ml_dtypes.bfloat16)

def planes(Y):
    n, m = Y.shape
    b = f64(bf(Y)).reshape(n // 32, 32, m)
    amax = np.abs(b).max(1)
    byte = np.clip(np.where(amax > 0, np.frexp(amax)[1] - 1 + 127 - 7, 1), 1, 254)
    codes = (b * np.exp2(127.0 - byte)[:, None, :]).reshape(n, m).astype(np.float32).astype(ml_dtypes.float8_e4m3fn).view(np.uint8)
    words = codes.reshape(n // 512, 128, 4, m).transpose(0, 1, 3, 2)
    return np.ascontiguousarray(words), np.ascontiguousarray(byte.astype(np.uint8).reshape(n // 512, 16, m))


K, T, S, H, P, N = 1024, 4096, 1024, 1024, 512, 1024

def setup_inputs():
    n = np.random.standard_normal
    s = mx_kscale(K)[:, None]
    u = mx_kscale(H)[:, None]
    gain = np.exp(0.8 * n(N))
    tab_words, tab_scales = pack_weight(n((K, T)) * s, "e4m3")
    w1 = n((K, H)) / np.sqrt(K) / s * u.T
    wc_words, wc_scales = pack_weight(n((K, H)) / np.sqrt(K) / s, "e2m1")
    w2_words, w2_scales = pack_weight(n((H, N)) / np.sqrt(H) * gain[None, :] / u, "e4m3")
    return {
        "tab_words": tab_words, "tab_scales": tab_scales,
        "offs": striped(np.random.permutation(T)[:S]),
        "pos1": striped(np.random.permutation(S)[:P]),
        "pos2": striped(np.random.permutation(S)[:P]),
        "w1": w1.astype(np.float32),
        "wc_words": wc_words, "wc_scales": wc_scales,
        "w2_words": w2_words, "w2_scales": w2_scales,
        "b2": (0.4 * gain * n(N)).astype(np.float32),
    }

def reference(tab_words, tab_scales, offs, pos1, pos2, w1, wc_words, wc_scales, w2_words, w2_scales, b2):
    v = unpack_weight(tab_words, tab_scales, "e4m3")[:, unstriped(offs)]
    wc = unpack_weight(wc_words, wc_scales, "e2m1")
    w2 = unpack_weight(w2_words, w2_scales, "e4m3")
    load = mxq(f64(w1), 0, "e4m3").T @ v
    cap = wc.T @ v
    h = load / (1.0 + np.abs(cap))
    a = h[:, unstriped(pos1)]
    b = h[:, unstriped(pos2)]
    z = np.maximum(a, b)
    y = (w2.T @ mxq(z, 0, "e4m3")) + f64(b2)[:, None]
    words, scales = planes(y)
    return y, words, scales

@@ -1,0 +1,294 @@
+from contextlib import ExitStack
+
+import concourse.mybir as mybir
+
+K, T, S, H, PAIRS, N = 1024, 4096, 1024, 1024, 512, 1024
+FLOPS = 2 * K * H * S * 2 + 2 * H * N * PAIRS
+
+F32 = mybir.dt.float32
+BF16 = mybir.dt.bfloat16
+I32 = mybir.dt.int32
+U32 = mybir.dt.uint32
+U16 = mybir.dt.uint16
+U8 = mybir.dt.uint8
+FP8X4 = mybir.dt.float8_e4m3fn_x4
+FP4X4 = mybir.dt.float4_e2m1fn_x4
+ACT = mybir.ActivationFunctionType
+ALU = mybir.AluOpType
+
+P = 128
+BANK = 512
+HALF = PAIRS // 2
+
+
+def tile_list_flow_congestion_routing_kernel(
+    tc, tab_words, tab_scales, offs, pos1, pos2, w1, wc_words, wc_scales, w2_words, w2_scales, b2, out_0, out_1, out_2
+):
+    nc = tc.nc
+    with ExitStack() as ctx:
+        sb = ctx.enter_context(tc.tile_pool(name="sb", bufs=1))
+        ps = ctx.enter_context(tc.psum_pool(name="ps", bufs=1))
+
+        def tile(shape, dtype, name):
+            return sb.tile(shape, dtype, name=name, align_bytes=64)
+
+        offs_sb = sb.tile([P, S // 16], U16, name="offs_sb")
+        pos1_sb = sb.tile([P, PAIRS // 16], U16, name="pos1_sb")
+        pos2_sb = sb.tile([P, PAIRS // 16], U16, name="pos2_sb")
+        banks = [ps.tile([P, BANK], F32, name="bank%d" % i) for i in range(8)]
+
+        tab_w = [tile([P, T], I32, "tab_w%d" % a) for a in range(2)]
+        tab_s = tile([P, T], U8, "tab_s")
+        v_w = [[tile([P, BANK], U32, "v_w%d%d" % (a, s)) for s in range(2)] for a in range(2)]
+        v_s = [tile([P, S], U8, "v_s%d" % a) for a in range(2)]
+        wc_raw = tile([P, 2, H // 2], I32, "wc_raw")
+        wcs_raw = tile([P, 2, H], U8, "wcs_raw")
+        wc_w = [tile([P, 2, BANK], U16, "wc_w%d" % b) for b in range(2)]
+        wc_s = [tile([P, 2, BANK], U8, "wc_s%d" % b) for b in range(2)]
+        w1_raw = [[tile([P, 4, BANK], F32, "w1_raw%d%d" % (b, a)) for a in range(2)] for b in range(2)]
+        w1_bf = [tile([P, 4 * BANK], BF16, "w1_bf%d" % a) for a in range(2)]
+        w1_w = [[tile([P, BANK], U32, "w1_w%d%d" % (b, a)) for a in range(2)] for b in range(2)]
+        w1_s = [[tile([P, BANK], U8, "w1_s%d%d" % (b, a)) for a in range(2)] for b in range(2)]
+        w2_raw = tile([P, 2, N], I32, "w2_raw")
+        w2s_raw = tile([P, N], U8, "w2s_raw")
+        w2_w = [tile([P, N], I32, "w2_w%d" % b) for b in range(2)]
+        w2_s = tile([P, N], U8, "w2_s")
+        bias = tile([P, 2, 4], F32, "bias")
+        warm = tile([P, 8], F32, "warm")
+
+        nc.vector.memset(tab_s[:].bitcast(I32), 0)
+        nc.vector.memset(wcs_raw[:].bitcast(I32), 0)
+        nc.vector.memset(v_s[1][:].bitcast(I32), 0)
+        nc.vector.memset(w2s_raw[:].bitcast(I32), 0)
+        nc.vector.memset(warm[:], 1.0)
+        nc.scalar.activation(out=warm[:], in_=warm[:], func=ACT.Abs_reciprocal_sqrt)
+
+        def load_table(a):
+            nc.sync.dma_start(out=tab_w[a][:], in_=tab_words[a].rearrange("p t i -> p (t i)").bitcast(I32))
+
+        def load_w1(b, a):
+            rows = w1[BANK * a : BANK * (a + 1), BANK * b : BANK * (b + 1)]
+            nc.sync.dma_start(out=w1_raw[b][a][:], in_=rows.rearrange("(p j) c -> p j c", j=4))
+
+        load_table(0)
+        nc.sync.dma_start(offs_sb[:], offs)
+        for q in range(4):
+            nc.gpsimd.dma_start(
+                out=tab_s[32 * q : 32 * q + 8, :].bitcast(I32), in_=tab_scales[:, 4 * q : 4 * q + 4, :].bitcast(I32)
+            )
+        nc.sync.dma_start(out=wc_raw[:], in_=wc_words.rearrange("a p c -> p a c").bitcast(I32))
+        load_table(1)
+        for q in range(4):
+            nc.gpsimd.dma_start(
+                out=wcs_raw[32 * q : 32 * q + 4, :, :].bitcast(I32),
+                in_=wc_scales[:, 4 * q : 4 * q + 4, :].rearrange("a r c -> r a c").bitcast(I32),
+            )
+        load_w1(0, 0)
+        load_w1(0, 1)
+
+        nc.vector.tensor_copy(v_s[0][:], tab_s[:].indirect(offs_sb[:]))
+        nc.gpsimd.dma_start(out=v_s[1][0:112, :].bitcast(I32), in_=v_s[0][4:116, :].bitcast(I32))
+
+        nc.sync.dma_start(pos1_sb[:], pos1)
+        nc.sync.dma_start(pos2_sb[:], pos2)
+        load_w1(1, 0)
+        load_w1(1, 1)
+        nc.sync.dma_start(out=w2_raw[:], in_=w2_words.rearrange("b p n i -> p b (n i)").bitcast(I32))
+        for q in range(4):
+            nc.sync.dma_start(
+                out=w2s_raw[32 * q : 32 * q + 8, :].bitcast(I32), in_=w2_scales[:, 4 * q : 4 * q + 4, :].bitcast(I32)
+            )
+        nc.sync.dma_start(out=bias[:], in_=b2.rearrange("(g p t) -> p g t", g=2, t=4))
+
+        def gather_words(a, s):
+            nc.vector.tensor_copy(v_w[a][s][:], tab_w[a][:].bitcast(U32).indirect(offs_sb[:, 32 * s : 32 * (s + 1)]))
+
+        def deal_wc(b):
+            cols = slice(BANK * b, BANK * (b + 1))
+            nc.vector.tensor_copy(
+                out=wc_w[b][:].rearrange("p a (t c i) -> p a c t i", t=4, i=8),
+                in_=wc_raw[:].bitcast(U16)[:, :, cols].rearrange("p a (c i t) -> p a c t i", t=4, i=8),
+            )
+            nc.vector.tensor_copy(
+                out=wc_s[b][:].rearrange("p a (t c i) -> p a c t i", t=4, i=16),
+                in_=wcs_raw[:, :, cols].rearrange("p a (c i t) -> p a c t i", t=4, i=16),
+            )
+
+        def round_w1(b, a):
+            out = w1_bf[a][:].rearrange("p (t m j) -> p m t j", t=4, j=4)
+            in_ = w1_raw[b][a][:].rearrange("p j (m t) -> p m t j", t=4)
+            if b == 0:
+                nc.vector.tensor_copy(out=out, in_=in_)
+            else:
+                nc.scalar.copy(out=out, in_=in_)
+
+        def quantize_w1(b, a):
+            nc.vector.quantize_mx(out=w1_w[b][a][:].bitcast(FP8X4), scales=w1_s[b][a][:], in_=w1_bf[a][:])
+
+        def deal_w2():
+            for b in range(2):
+                nc.vector.tensor_copy(
+                    out=w2_w[b][:].rearrange("p (g t c i) -> p g c t i", g=2, t=4, i=4),
+                    in_=w2_raw[:, b, :].rearrange("p (g c i t) -> p g c t i", g=2, t=4, i=4),
+                )
+            nc.vector.tensor_copy(
+                out=w2_s[:].rearrange("p (g t c i) -> p g c t i", g=2, t=4, i=16),
+                in_=w2s_raw[:].rearrange("p (g c i t) -> p g c t i", g=2, t=4, i=16),
+            )
+
+        gather_words(0, 0)
+        gather_words(0, 1)
+        deal_wc(0)
+        gather_words(1, 0)
+        gather_words(1, 1)
+        deal_wc(1)
+        round_w1(0, 0)
+        quantize_w1(0, 0)
+        round_w1(0, 1)
+        quantize_w1(0, 1)
+
+        damp = [tile([P, S], F32, "damp%d" % i) for i in range(4)]
+        h = [tile([P, S], F32, "h%d" % i) for i in range(2)]
+        first = tile([P, 4, PAIRS], F32, "first")
+        second = tile([P, 4, PAIRS], F32, "second")
+        z_bf = [tile([P, 4 * HALF], BF16, "z_bf%d" % i) for i in range(4)]
+        z_w = [tile([P, HALF], U32, "z_w%d" % i) for i in range(4)]
+        z_s = [tile([P, HALF], U8, "z_s%d" % i) for i in range(4)]
+
+        def cap_stage(u):
+            b, t = divmod(u, 4)
+            cols = slice(P * t, P * (t + 1))
+            d = damp[u % 4]
+            for s in range(2):
+                for a in range(2):
+                    nc.tensor.matmul_mx(
+                        out=banks[(2 * u + s) % 4][:],
+                        lhsT=wc_w[b][:, a, cols].bitcast(FP4X4),
+                        lhsT_scale=wc_s[b][:, a, cols],
+                        rhs=v_w[a][s][:].bitcast(FP8X4),
+                        rhs_scale=v_s[a][:, BANK * s : BANK * (s + 1)],
+                        start=(a == 0),
+                        stop=(a == 1),
+                    )
+            halves = [d[:, BANK * s : BANK * (s + 1)] for s in range(2)]
+            for s in range(2):
+                nc.scalar.activation(out=halves[s], in_=banks[(2 * u + s) % 4][:], func=ACT.Abs)
+            for s in range(2):
+                nc.scalar.activation(out=halves[s], in_=halves[s], func=ACT.Abs_reciprocal_sqrt, bias=1.0)
+            for s in range(2):
+                nc.scalar.activation(out=halves[s], in_=halves[s], func=ACT.Square)
+
+        def load_stage(u):
+            b, t = divmod(u, 4)
+            cols = slice(P * t, P * (t + 1))
+            for s in range(2):
+                for a in range(2):
+                    nc.tensor.matmul_mx(
+                        out=banks[4 + (2 * u + s) % 4][:],
+                        lhsT=w1_w[b][a][:, cols].bitcast(FP8X4),
+                        lhsT_scale=w1_s[b][a][:, cols],
+                        rhs=v_w[a][s][:].bitcast(FP8X4),
+                        rhs_scale=v_s[a][:, BANK * s : BANK * (s + 1)],
+                        start=(a == 0),
+                        stop=(a == 1),
+                    )
+            for s in range(2):
+                cols_s = slice(BANK * s, BANK * (s + 1))
+                nc.vector.tensor_tensor(
+                    out=h[u % 2][:, cols_s], in0=banks[4 + (2 * u + s) % 4][:], in1=damp[u % 4][:, cols_s], op=ALU.mult
+                )
+
+        def pick(u, lo, hi):
+            t = u % 4
+            whole = lo == 0 and hi == PAIRS
+            for dst, pos in ((first, pos1_sb), (second, pos2_sb)):
+                lst = pos[:] if whole else pos[:, lo // 16 : hi // 16]
+                nc.vector.tensor_copy(dst[:, t, lo:hi], h[u % 2][:].indirect(lst))
+
+        def make_z(b, s):
+            cols = slice(HALF * s, HALF * (s + 1))
+            nc.vector.tensor_tensor(
+                out=z_bf[2 * b + s][:].rearrange("p (c i t) -> p c t i", t=4, i=4),
+                in0=first[:, :, cols].rearrange("p t (c i) -> p c t i", i=4),
+                in1=second[:, :, cols].rearrange("p t (c i) -> p c t i", i=4),
+                op=ALU.max,
+            )
+
+        def quantize_z(b, s):
+            i = 2 * b + s
+            nc.vector.quantize_mx(out=z_w[i][:].bitcast(FP8X4), scales=z_s[i][:], in_=z_bf[i][:])
+
+        def y_passes(b, s):
+            for g in range(2):
+                for t in range(4):
+                    cols = slice(BANK * g + P * t, BANK * g + P * (t + 1))
+                    bank = banks[4 * s + 2 * g + t // 2]
+                    nc.tensor.matmul_mx(
+                        out=bank[:, HALF * (t % 2) : HALF * (t % 2 + 1)],
+                        lhsT=w2_w[b][:, cols].bitcast(FP8X4),
+                        lhsT_scale=w2_s[4 * b : P, cols],
+                        rhs=z_w[2 * b + s][:].bitcast(FP8X4),
+                        rhs_scale=z_s[2 * b + s][:],
+                        start=(b == 0 and t % 2 == 0),
+                        stop=(b == 1 and t % 2 == 1),
+                    )
+
+        cap_stage(0)
+        for u in range(8):
+            if u + 1 < 8:
+                cap_stage(u + 1)
+            load_stage(u)
+            if u < 7:
+                pick(u, 0, PAIRS)
+            if u == 1:
+                for a in range(2):
+                    round_w1(1, a)
+                    quantize_w1(1, a)
+            if u == 3:
+                for s in range(2):
+                    make_z(0, s)
+                for s in range(2):
+                    quantize_z(0, s)
+            if u == 4:
+                deal_w2()
+
+        y = [[tile([P, 4, HALF], F32, "y%d%d" % (s, g)) for g in range(2)] for s in range(2)]
+        y_bf = [[tile([P, 4 * HALF], BF16, "y_bf%d%d" % (s, g)) for g in range(2)] for s in range(2)]
+        y_w = [[tile([P, HALF], I32, "y_w%d%d" % (s, g)) for g in range(2)] for s in range(2)]
+        y_s = tile([P, 2, PAIRS], U8, "y_s")
+
+        def finish(s, g):
+            cols = slice(HALF * s, HALF * (s + 1))
+            for t in range(4):
+                bank = banks[4 * s + 2 * g + t // 2]
+                nc.scalar.activation(
+                    out=y[s][g][:, t, :],
+                    in_=bank[:, HALF * (t % 2) : HALF * (t % 2 + 1)],
+                    func=ACT.Identity,
+                    bias=bias[:, g, t : t + 1],
+                )
+            rows = out_0[BANK * g : BANK * (g + 1), cols]
+            nc.sync.dma_start(out=rows.rearrange("(p t) j -> p t j", t=4), in_=y[s][g][:])
+            nc.vector.tensor_copy(
+                out=y_bf[s][g][:].rearrange("p (c i t) -> p c t i", t=4, i=4),
+                in_=y[s][g][:].rearrange("p t (c i) -> p c t i", i=4),
+            )
+            nc.vector.quantize_mx(out=y_w[s][g][:].bitcast(FP8X4), scales=y_s[:, g, cols], in_=y_bf[s][g][:])
+            nc.sync.dma_start(out=out_1[g].rearrange("p m t -> p (m t)").bitcast(I32)[:, cols], in_=y_w[s][g][:])
+
+        for s in range(2):
+            y_passes(0, s)
+        for s in range(2):
+            pick(7, HALF * s, HALF * (s + 1))
+            make_z(1, s)
+            quantize_z(1, s)
+            y_passes(1, s)
+        for s in range(2):
+            for g in range(2):
+                finish(s, g)
+        for q in range(4):
+            queue = nc.sync if q % 2 == 0 else nc.scalar
+            queue.dma_start(
+                out=out_2[:, 4 * q : 4 * q + 4, :].rearrange("g r m -> r g m").bitcast(I32),
+                in_=y_s[32 * q : 32 * q + 4, :, :].bitcast(I32),
+            )

@@ -29,76 +29,82 @@ def tile_list_flow_congestion_routing_kernel(
         sb = ctx.enter_context(tc.tile_pool(name="sb", bufs=1))
         ps = ctx.enter_context(tc.psum_pool(name="ps", bufs=1))
 
-        def tile(shape, dtype, name):
-            return sb.tile(shape, dtype, name=name, align_bytes=64)
+        def tile(shape, dtype, name, tag=None):
+            return sb.tile(shape, dtype, name=name, tag=tag or name, align_bytes=64)
 
         offs_sb = sb.tile([P, S // 16], U16, name="offs_sb")
         pos1_sb = sb.tile([P, PAIRS // 16], U16, name="pos1_sb")
         pos2_sb = sb.tile([P, PAIRS // 16], U16, name="pos2_sb")
         banks = [ps.tile([P, BANK], F32, name="bank%d" % i) for i in range(8)]
 
-        tab_w = [tile([P, T], I32, "tab_w%d" % a) for a in range(2)]
-        tab_s = tile([P, T], U8, "tab_s")
+        tab_s = tile([P, T], U8, "tab_s", "stage2")
+        tab_w = [tile([P, T], I32, "tab_w%d" % a, "stage%d" % (a + 1)) for a in range(2)]
+        picked_s = tile([P, S], U8, "picked_s")
         v_w = [[tile([P, BANK], U32, "v_w%d%d" % (a, s)) for s in range(2)] for a in range(2)]
         v_s = [tile([P, S], U8, "v_s%d" % a) for a in range(2)]
-        wc_raw = tile([P, 2, H // 2], I32, "wc_raw")
+        wc_raw = tile([P, 2, H // 2], I32, "wc_raw", "stage0")
         wcs_raw = tile([P, 2, H], U8, "wcs_raw")
         wc_w = [tile([P, 2, BANK], U16, "wc_w%d" % b) for b in range(2)]
         wc_s = [tile([P, 2, BANK], U8, "wc_s%d" % b) for b in range(2)]
-        w1_raw = [[tile([P, 4, BANK], F32, "w1_raw%d%d" % (b, a)) for a in range(2)] for b in range(2)]
-        w1_bf = [tile([P, 4 * BANK], BF16, "w1_bf%d" % a) for a in range(2)]
+        w1_raw = [[tile([P, 4, BANK], F32, "w1_raw%d%d" % (b, a), "stage%d" % (1 - a)) for a in range(2)] for b in range(2)]
+        w1_bf_both = tile([P, 8 * BANK], BF16, "w1_bf", "stage2")
+        w1_bf = [w1_bf_both[:, 4 * BANK * a : 4 * BANK * (a + 1)] for a in range(2)]
         w1_w = [[tile([P, BANK], U32, "w1_w%d%d" % (b, a)) for a in range(2)] for b in range(2)]
         w1_s = [[tile([P, BANK], U8, "w1_s%d%d" % (b, a)) for a in range(2)] for b in range(2)]
-        w2_raw = tile([P, 2, N], I32, "w2_raw")
-        w2s_raw = tile([P, N], U8, "w2s_raw")
+        w2_raw = tile([P, 2, N], I32, "w2_raw", "stage1")
+        w2s_raw = tile([P, N], U8, "w2s_raw", "stage0")
         w2_w = [tile([P, N], I32, "w2_w%d" % b) for b in range(2)]
-        w2_s = tile([P, N], U8, "w2_s")
-        bias = tile([P, 2, 4], F32, "bias")
+        bias = tile([P, 2, 4], F32, "bias", "stage2")
         warm = tile([P, 8], F32, "warm")
 
-        nc.vector.memset(tab_s[:].bitcast(I32), 0)
         nc.vector.memset(wcs_raw[:].bitcast(I32), 0)
-        nc.vector.memset(v_s[1][:].bitcast(I32), 0)
-        nc.vector.memset(w2s_raw[:].bitcast(I32), 0)
-        nc.vector.memset(warm[:], 1.0)
+        nc.gpsimd.memset(warm[:], 1.0)
+        for q in range(4):
+            engine = nc.vector if q < 2 else nc.gpsimd
+            engine.memset(tab_s[32 * q : 32 * q + 24, :].bitcast(I32), 0)
+        for a in range(2):
+            nc.gpsimd.memset(v_s[a][:].bitcast(I32), 0)
         nc.scalar.activation(out=warm[:], in_=warm[:], func=ACT.Abs_reciprocal_sqrt)
 
         def load_table(a):
             nc.sync.dma_start(out=tab_w[a][:], in_=tab_words[a].rearrange("p t i -> p (t i)").bitcast(I32))
 
-        def load_w1(b, a):
-            rows = w1[BANK * a : BANK * (a + 1), BANK * b : BANK * (b + 1)]
-            nc.sync.dma_start(out=w1_raw[b][a][:], in_=rows.rearrange("(p j) c -> p j c", j=4))
+        def load_w1(b, a, lo=0, hi=BANK):
+            rows = w1[BANK * a : BANK * (a + 1), BANK * b + lo : BANK * b + hi]
+            nc.sync.dma_start(out=w1_raw[b][a][:, :, lo:hi], in_=rows.rearrange("(p j) c -> p j c", j=4))
 
-        load_table(0)
         nc.sync.dma_start(offs_sb[:], offs)
         for q in range(4):
-            nc.gpsimd.dma_start(
-                out=tab_s[32 * q : 32 * q + 8, :].bitcast(I32), in_=tab_scales[:, 4 * q : 4 * q + 4, :].bitcast(I32)
+            nc.sync.dma_start(
+                out=tab_s[32 * q + 24 : 32 * q + 32, :].bitcast(I32), in_=tab_scales[:, 4 * q : 4 * q + 4, :].bitcast(I32)
             )
+        nc.sync.dma_start(pos1_sb[:], pos1)
+        nc.sync.dma_start(pos2_sb[:], pos2)
+        load_table(0)
         nc.sync.dma_start(out=wc_raw[:], in_=wc_words.rearrange("a p c -> p a c").bitcast(I32))
-        load_table(1)
         for q in range(4):
-            nc.gpsimd.dma_start(
+            nc.sync.dma_start(
                 out=wcs_raw[32 * q : 32 * q + 4, :, :].bitcast(I32),
                 in_=wc_scales[:, 4 * q : 4 * q + 4, :].rearrange("a r c -> r a c").bitcast(I32),
             )
-        load_w1(0, 0)
-        load_w1(0, 1)
 
-        nc.vector.tensor_copy(v_s[0][:], tab_s[:].indirect(offs_sb[:]))
-        nc.gpsimd.dma_start(out=v_s[1][0:112, :].bitcast(I32), in_=v_s[0][4:116, :].bitcast(I32))
-
-        nc.sync.dma_start(pos1_sb[:], pos1)
-        nc.sync.dma_start(pos2_sb[:], pos2)
-        load_w1(1, 0)
-        load_w1(1, 1)
-        nc.sync.dma_start(out=w2_raw[:], in_=w2_words.rearrange("b p n i -> p b (n i)").bitcast(I32))
-        for q in range(4):
-            nc.sync.dma_start(
-                out=w2s_raw[32 * q : 32 * q + 8, :].bitcast(I32), in_=w2_scales[:, 4 * q : 4 * q + 4, :].bitcast(I32)
+        nc.vector.tensor_copy(picked_s[:], tab_s[:].indirect(offs_sb[:]))
+        for a in range(2):
+            nc.scalar.dma_start(
+                out=v_s[a][0:100, :].bitcast(I32), in_=picked_s[24 + 4 * a : 124 + 4 * a, :].bitcast(I32)
             )
-        nc.sync.dma_start(out=bias[:], in_=b2.rearrange("(g p t) -> p g t", g=2, t=4))
+        load_table(1)
+
+        def load_w2():
+            nc.sync.dma_start(out=w2_raw[:], in_=w2_words.rearrange("b p n i -> p b (n i)").bitcast(I32))
+
+        def load_w2_scales():
+            nc.gpsimd.memset(w2s_raw[:].bitcast(I32), 0)
+            for q in range(4):
+                nc.sync.dma_start(
+                    out=w2s_raw[32 * q : 32 * q + 8, :].bitcast(I32),
+                    in_=w2_scales[:, 4 * q : 4 * q + 4, :].bitcast(I32),
+                )
 
         def gather_words(a, s):
             nc.vector.tensor_copy(v_w[a][s][:], tab_w[a][:].bitcast(U32).indirect(offs_sb[:, 32 * s : 32 * (s + 1)]))
@@ -106,51 +112,71 @@ def tile_list_flow_congestion_routing_kernel(
         def deal_wc(b):
             cols = slice(BANK * b, BANK * (b + 1))
             nc.vector.tensor_copy(
-                out=wc_w[b][:].rearrange("p a (t c i) -> p a c t i", t=4, i=8),
-                in_=wc_raw[:].bitcast(U16)[:, :, cols].rearrange("p a (c i t) -> p a c t i", t=4, i=8),
+                out=wc_w[b][:].rearrange("p a (t m) -> p a m t", t=4),
+                in_=wc_raw[:].bitcast(U16)[:, :, cols].rearrange("p a (m t) -> p a m t", t=4),
             )
             nc.vector.tensor_copy(
-                out=wc_s[b][:].rearrange("p a (t c i) -> p a c t i", t=4, i=16),
-                in_=wcs_raw[:, :, cols].rearrange("p a (c i t) -> p a c t i", t=4, i=16),
+                out=wc_s[b][:].rearrange("p a (t m) -> p a m t", t=4),
+                in_=wcs_raw[:, :, cols].rearrange("p a (m t) -> p a m t", t=4),
             )
 
-        def round_w1(b, a):
-            out = w1_bf[a][:].rearrange("p (t m j) -> p m t j", t=4, j=4)
-            in_ = w1_raw[b][a][:].rearrange("p j (m t) -> p m t j", t=4)
+        def round_w1(b, a, lo=0, hi=BANK):
+            out = w1_bf[a].rearrange("p (t m j) -> p m j t", t=4, j=4)[:, lo // 4 : hi // 4, :, :]
+            in_ = w1_raw[b][a][:, :, lo:hi].rearrange("p j (m t) -> p m j t", t=4)
             if b == 0:
                 nc.vector.tensor_copy(out=out, in_=in_)
             else:
                 nc.scalar.copy(out=out, in_=in_)
 
-        def quantize_w1(b, a):
-            nc.vector.quantize_mx(out=w1_w[b][a][:].bitcast(FP8X4), scales=w1_s[b][a][:], in_=w1_bf[a][:])
+        def quantize_w1(b, a, lo=0, hi=BANK):
+            nc.vector.quantize_mx(
+                out=w1_w[b][a][:, lo:hi].bitcast(FP8X4), scales=w1_s[b][a][:, lo:hi], in_=w1_bf[a][:, 4 * lo : 4 * hi]
+            )
 
-        def deal_w2():
+        def deal_w2_words():
             for b in range(2):
                 nc.vector.tensor_copy(
-                    out=w2_w[b][:].rearrange("p (g t c i) -> p g c t i", g=2, t=4, i=4),
-                    in_=w2_raw[:, b, :].rearrange("p (g c i t) -> p g c t i", g=2, t=4, i=4),
+                    out=w2_w[b][:].rearrange("p (g t m) -> p g m t", g=2, t=4),
+                    in_=w2_raw[:, b, :].rearrange("p (g m t) -> p g m t", g=2, t=4),
                 )
+
+        def deal_w2_scales():
             nc.vector.tensor_copy(
-                out=w2_s[:].rearrange("p (g t c i) -> p g c t i", g=2, t=4, i=16),
-                in_=w2s_raw[:].rearrange("p (g c i t) -> p g c t i", g=2, t=4, i=16),
+                out=w2_s[:].rearrange("p (g t m) -> p g m t", g=2, t=4),
+                in_=w2s_raw[:].rearrange("p (g m t) -> p g m t", g=2, t=4),
             )
 
         gather_words(0, 0)
         gather_words(0, 1)
+        load_w1(0, 0)
         deal_wc(0)
+        deal_wc(1)
+        load_w1(0, 1, 0, HALF)
+        load_w1(0, 1, HALF, BANK)
         gather_words(1, 0)
         gather_words(1, 1)
-        deal_wc(1)
         round_w1(0, 0)
+        load_w1(1, 0)
         quantize_w1(0, 0)
-        round_w1(0, 1)
-        quantize_w1(0, 1)
+        round_w1(0, 1, 0, HALF)
+        round_w1(0, 1, HALF, BANK)
+        load_w1(1, 1)
+        quantize_w1(0, 1, 0, P)
+        quantize_w1(0, 1, P, HALF)
+        quantize_w1(0, 1, HALF, BANK)
 
-        damp = [tile([P, S], F32, "damp%d" % i) for i in range(4)]
-        h = [tile([P, S], F32, "h%d" % i) for i in range(2)]
-        first = tile([P, 4, PAIRS], F32, "first")
-        second = tile([P, 4, PAIRS], F32, "second")
+        h = [tile([P, S], F32, "h%d" % i) for i in range(3)]
+        w2_s = tile([P, N], U8, "w2_s", "h0")
+        first = [tile([P, 4, PAIRS], F32, "first%d" % b) for b in range(2)]
+        second = [tile([P, 4, PAIRS], F32, "second%d" % b) for b in range(2)]
+        damp = []
+        for u in range(8):
+            if u in (0, 4, 7):
+                own = tile([P, S], F32, "damp%d" % u)
+                damp.append([own[:, BANK * s : BANK * (s + 1)] for s in range(2)])
+            else:
+                b, t = divmod(u - 1, 4)
+                damp.append([first[b][:, t, :], second[b][:, t, :]])
         z_bf = [tile([P, 4 * HALF], BF16, "z_bf%d" % i) for i in range(4)]
         z_w = [tile([P, HALF], U32, "z_w%d" % i) for i in range(4)]
         z_s = [tile([P, HALF], U8, "z_s%d" % i) for i in range(4)]
@@ -158,21 +184,20 @@ def tile_list_flow_congestion_routing_kernel(
         def cap_stage(u):
             b, t = divmod(u, 4)
             cols = slice(P * t, P * (t + 1))
-            d = damp[u % 4]
             for s in range(2):
-                for a in range(2):
+                for a in (1, 0):
                     nc.tensor.matmul_mx(
-                        out=banks[(2 * u + s) % 4][:],
+                        out=banks[2 * (u % 4) + s][:],
                         lhsT=wc_w[b][:, a, cols].bitcast(FP4X4),
                         lhsT_scale=wc_s[b][:, a, cols],
                         rhs=v_w[a][s][:].bitcast(FP8X4),
                         rhs_scale=v_s[a][:, BANK * s : BANK * (s + 1)],
-                        start=(a == 0),
-                        stop=(a == 1),
+                        start=(a == 1),
+                        stop=(a == 0),
                     )
-            halves = [d[:, BANK * s : BANK * (s + 1)] for s in range(2)]
+            halves = damp[u]
             for s in range(2):
-                nc.scalar.activation(out=halves[s], in_=banks[(2 * u + s) % 4][:], func=ACT.Abs)
+                nc.scalar.activation(out=halves[s], in_=banks[2 * (u % 4) + s][:], func=ACT.Abs)
             for s in range(2):
                 nc.scalar.activation(out=halves[s], in_=halves[s], func=ACT.Abs_reciprocal_sqrt, bias=1.0)
             for s in range(2):
@@ -182,35 +207,33 @@ def tile_list_flow_congestion_routing_kernel(
             b, t = divmod(u, 4)
             cols = slice(P * t, P * (t + 1))
             for s in range(2):
-                for a in range(2):
+                for a in (1, 0):
                     nc.tensor.matmul_mx(
-                        out=banks[4 + (2 * u + s) % 4][:],
+                        out=banks[2 * ((u - 1) % 4) + s][:],
                         lhsT=w1_w[b][a][:, cols].bitcast(FP8X4),
                         lhsT_scale=w1_s[b][a][:, cols],
                         rhs=v_w[a][s][:].bitcast(FP8X4),
                         rhs_scale=v_s[a][:, BANK * s : BANK * (s + 1)],
-                        start=(a == 0),
-                        stop=(a == 1),
+                        start=(a == 1),
+                        stop=(a == 0),
                     )
             for s in range(2):
                 cols_s = slice(BANK * s, BANK * (s + 1))
                 nc.vector.tensor_tensor(
-                    out=h[u % 2][:, cols_s], in0=banks[4 + (2 * u + s) % 4][:], in1=damp[u % 4][:, cols_s], op=ALU.mult
+                    out=h[u % 3][:, cols_s], in0=banks[2 * ((u - 1) % 4) + s][:], in1=damp[u][s], op=ALU.mult
                 )
 
-        def pick(u, lo, hi):
-            t = u % 4
-            whole = lo == 0 and hi == PAIRS
-            for dst, pos in ((first, pos1_sb), (second, pos2_sb)):
-                lst = pos[:] if whole else pos[:, lo // 16 : hi // 16]
-                nc.vector.tensor_copy(dst[:, t, lo:hi], h[u % 2][:].indirect(lst))
+        def pick(u, which, lo=0, hi=PAIRS):
+            b, t = divmod(u, 4)
+            dst, pos = ((first, pos1_sb), (second, pos2_sb))[which]
+            nc.vector.tensor_copy(dst[b][:, t, lo:hi], h[u % 3][:].indirect(pos[:, lo // 16 : hi // 16]))
 
         def make_z(b, s):
             cols = slice(HALF * s, HALF * (s + 1))
             nc.vector.tensor_tensor(
                 out=z_bf[2 * b + s][:].rearrange("p (c i t) -> p c t i", t=4, i=4),
-                in0=first[:, :, cols].rearrange("p t (c i) -> p c t i", i=4),
-                in1=second[:, :, cols].rearrange("p t (c i) -> p c t i", i=4),
+                in0=first[b][:, :, cols].rearrange("p t (c i) -> p c t i", i=4),
+                in1=second[b][:, :, cols].rearrange("p t (c i) -> p c t i", i=4),
                 op=ALU.max,
             )
 
@@ -222,7 +245,7 @@ def tile_list_flow_congestion_routing_kernel(
             for g in range(2):
                 for t in range(4):
                     cols = slice(BANK * g + P * t, BANK * g + P * (t + 1))
-                    bank = banks[4 * s + 2 * g + t // 2]
+                    bank = banks[2 * (0, 3, 1, 2)[2 * s + g] + t // 2]
                     nc.tensor.matmul_mx(
                         out=bank[:, HALF * (t % 2) : HALF * (t % 2 + 1)],
                         lhsT=w2_w[b][:, cols].bitcast(FP8X4),
@@ -233,24 +256,34 @@ def tile_list_flow_congestion_routing_kernel(
                         stop=(b == 1 and t % 2 == 1),
                     )
 
-        cap_stage(0)
+        for u in range(3):
+            cap_stage(u)
         for u in range(8):
-            if u + 1 < 8:
-                cap_stage(u + 1)
             load_stage(u)
-            if u < 7:
-                pick(u, 0, PAIRS)
-            if u == 1:
+            if u + 3 < 8:
+                cap_stage(u + 3)
+            if u == 0:
                 for a in range(2):
-                    round_w1(1, a)
+                    for lo in (0, HALF):
+                        round_w1(1, a, lo, lo + HALF)
                     quantize_w1(1, a)
+                load_w2()
+                load_w2_scales()
+                nc.sync.dma_start(out=bias[:], in_=b2.rearrange("(g p t) -> p g t", g=2, t=4))
+            if u in (1, 2, 3, 5, 6):
+                for which in range(2):
+                    pick(u - 1, which)
+            if u in (3, 6):
+                for which in range(2):
+                    pick(u, which)
             if u == 3:
                 for s in range(2):
                     make_z(0, s)
                 for s in range(2):
                     quantize_z(0, s)
             if u == 4:
-                deal_w2()
+                deal_w2_words()
+        deal_w2_scales()
 
         y = [[tile([P, 4, HALF], F32, "y%d%d" % (s, g)) for g in range(2)] for s in range(2)]
         y_bf = [[tile([P, 4 * HALF], BF16, "y_bf%d%d" % (s, g)) for g in range(2)] for s in range(2)]
@@ -260,7 +293,7 @@ def tile_list_flow_congestion_routing_kernel(
         def finish(s, g):
             cols = slice(HALF * s, HALF * (s + 1))
             for t in range(4):
-                bank = banks[4 * s + 2 * g + t // 2]
+                bank = banks[2 * (0, 3, 1, 2)[2 * s + g] + t // 2]
                 nc.scalar.activation(
                     out=y[s][g][:, t, :],
                     in_=bank[:, HALF * (t % 2) : HALF * (t % 2 + 1)],
@@ -279,7 +312,8 @@ def tile_list_flow_congestion_routing_kernel(
         for s in range(2):
             y_passes(0, s)
         for s in range(2):
-            pick(7, HALF * s, HALF * (s + 1))
+            for which in range(2):
+                pick(7, which, HALF * s, HALF * (s + 1))
             make_z(1, s)
             quantize_z(1, s)
             y_passes(1, s)

@@ -17,8 +17,17 @@ ACT = mybir.ActivationFunctionType
 ALU = mybir.AluOpType
 
 P = 128
+QUAD = 32
+GROUP = 512
 BANK = 512
 HALF = PAIRS // 2
+SLICES = H // P
+AHEAD = 3
+H_RING = 3
+SCALE_ROW = 24
+PLANE_ROWS = 100
+OWN_DAMP = (0, 4, 7)
+Y_BANKS = (0, 3, 1, 2)
 
 
 def tile_list_flow_congestion_routing_kernel(
@@ -29,8 +38,8 @@ def tile_list_flow_congestion_routing_kernel(
         sb = ctx.enter_context(tc.tile_pool(name="sb", bufs=1))
         ps = ctx.enter_context(tc.psum_pool(name="ps", bufs=1))
 
-        def tile(shape, dtype, name, tag=None):
-            return sb.tile(shape, dtype, name=name, tag=tag or name, align_bytes=64)
+        def tile(shape, dtype, name, buffer=None):
+            return sb.tile(shape, dtype, name=name, tag=buffer or name, align_bytes=64)
 
         offs_sb = sb.tile([P, S // 16], U16, name="offs_sb")
         pos1_sb = sb.tile([P, PAIRS // 16], U16, name="pos1_sb")
@@ -44,39 +53,48 @@ def tile_list_flow_congestion_routing_kernel(
         v_s = [tile([P, S], U8, "v_s%d" % a) for a in range(2)]
         wc_raw = tile([P, 2, H // 2], I32, "wc_raw", "stage0")
         wcs_raw = tile([P, 2, H], U8, "wcs_raw")
-        wc_w = [tile([P, 2, BANK], U16, "wc_w%d" % b) for b in range(2)]
-        wc_s = [tile([P, 2, BANK], U8, "wc_s%d" % b) for b in range(2)]
-        w1_raw = [[tile([P, 4, BANK], F32, "w1_raw%d%d" % (b, a), "stage%d" % (1 - a)) for a in range(2)] for b in range(2)]
-        w1_bf_both = tile([P, 8 * BANK], BF16, "w1_bf", "stage2")
-        w1_bf = [w1_bf_both[:, 4 * BANK * a : 4 * BANK * (a + 1)] for a in range(2)]
-        w1_w = [[tile([P, BANK], U32, "w1_w%d%d" % (b, a)) for a in range(2)] for b in range(2)]
-        w1_s = [[tile([P, BANK], U8, "w1_s%d%d" % (b, a)) for a in range(2)] for b in range(2)]
+        wc_w = [tile([P, 2, GROUP], U16, "wc_w%d" % b) for b in range(2)]
+        wc_s = [tile([P, 2, GROUP], U8, "wc_s%d" % b) for b in range(2)]
+        w1_raw = [
+            [tile([P, 4, GROUP], F32, "w1_raw%d%d" % (b, a), "stage%d" % (1 - a)) for a in range(2)] for b in range(2)
+        ]
+        w1_bf_both = tile([P, 8 * GROUP], BF16, "w1_bf", "stage2")
+        w1_bf = [w1_bf_both[:, 4 * GROUP * a : 4 * GROUP * (a + 1)] for a in range(2)]
+        w1_w = [[tile([P, GROUP], U32, "w1_w%d%d" % (b, a)) for a in range(2)] for b in range(2)]
+        w1_s = [[tile([P, GROUP], U8, "w1_s%d%d" % (b, a)) for a in range(2)] for b in range(2)]
         w2_raw = tile([P, 2, N], I32, "w2_raw", "stage1")
         w2s_raw = tile([P, N], U8, "w2s_raw", "stage0")
-        w2_w = [tile([P, N], I32, "w2_w%d" % b) for b in range(2)]
+        w2_w = tile([P, 2, N], I32, "w2_w")
         bias = tile([P, 2, 4], F32, "bias", "stage2")
-        warm = tile([P, 8], F32, "warm")
 
         nc.vector.memset(wcs_raw[:].bitcast(I32), 0)
-        nc.gpsimd.memset(warm[:], 1.0)
         for q in range(4):
             engine = nc.vector if q < 2 else nc.gpsimd
-            engine.memset(tab_s[32 * q : 32 * q + 24, :].bitcast(I32), 0)
+            engine.memset(tab_s[QUAD * q : QUAD * q + SCALE_ROW, :].bitcast(I32), 0)
         for a in range(2):
             nc.gpsimd.memset(v_s[a][:].bitcast(I32), 0)
-        nc.scalar.activation(out=warm[:], in_=warm[:], func=ACT.Abs_reciprocal_sqrt)
 
         def load_table(a):
             nc.sync.dma_start(out=tab_w[a][:], in_=tab_words[a].rearrange("p t i -> p (t i)").bitcast(I32))
 
-        def load_w1(b, a, lo=0, hi=BANK):
-            rows = w1[BANK * a : BANK * (a + 1), BANK * b + lo : BANK * b + hi]
+        def load_w1(b, a, lo=0, hi=GROUP):
+            rows = w1[GROUP * a : GROUP * (a + 1), GROUP * b + lo : GROUP * b + hi]
             nc.sync.dma_start(out=w1_raw[b][a][:, :, lo:hi], in_=rows.rearrange("(p j) c -> p j c", j=4))
+
+        def load_w2():
+            nc.sync.dma_start(out=w2_raw[:], in_=w2_words.rearrange("b p n i -> p b (n i)").bitcast(I32))
+            nc.vector.memset(w2s_raw[:].bitcast(I32), 0)
+            for q in range(4):
+                nc.sync.dma_start(
+                    out=w2s_raw[QUAD * q : QUAD * q + 8, :].bitcast(I32),
+                    in_=w2_scales[:, 4 * q : 4 * q + 4, :].bitcast(I32),
+                )
 
         nc.sync.dma_start(offs_sb[:], offs)
         for q in range(4):
             nc.sync.dma_start(
-                out=tab_s[32 * q + 24 : 32 * q + 32, :].bitcast(I32), in_=tab_scales[:, 4 * q : 4 * q + 4, :].bitcast(I32)
+                out=tab_s[QUAD * q + SCALE_ROW : QUAD * (q + 1), :].bitcast(I32),
+                in_=tab_scales[:, 4 * q : 4 * q + 4, :].bitcast(I32),
             )
         nc.sync.dma_start(pos1_sb[:], pos1)
         nc.sync.dma_start(pos2_sb[:], pos2)
@@ -84,33 +102,24 @@ def tile_list_flow_congestion_routing_kernel(
         nc.sync.dma_start(out=wc_raw[:], in_=wc_words.rearrange("a p c -> p a c").bitcast(I32))
         for q in range(4):
             nc.sync.dma_start(
-                out=wcs_raw[32 * q : 32 * q + 4, :, :].bitcast(I32),
+                out=wcs_raw[QUAD * q : QUAD * q + 4, :, :].bitcast(I32),
                 in_=wc_scales[:, 4 * q : 4 * q + 4, :].rearrange("a r c -> r a c").bitcast(I32),
             )
 
         nc.vector.tensor_copy(picked_s[:], tab_s[:].indirect(offs_sb[:]))
         for a in range(2):
+            top = SCALE_ROW + 4 * a
             nc.scalar.dma_start(
-                out=v_s[a][0:100, :].bitcast(I32), in_=picked_s[24 + 4 * a : 124 + 4 * a, :].bitcast(I32)
+                out=v_s[a][0:PLANE_ROWS, :].bitcast(I32), in_=picked_s[top : top + PLANE_ROWS, :].bitcast(I32)
             )
         load_table(1)
 
-        def load_w2():
-            nc.sync.dma_start(out=w2_raw[:], in_=w2_words.rearrange("b p n i -> p b (n i)").bitcast(I32))
-
-        def load_w2_scales():
-            nc.gpsimd.memset(w2s_raw[:].bitcast(I32), 0)
-            for q in range(4):
-                nc.sync.dma_start(
-                    out=w2s_raw[32 * q : 32 * q + 8, :].bitcast(I32),
-                    in_=w2_scales[:, 4 * q : 4 * q + 4, :].bitcast(I32),
-                )
-
         def gather_words(a, s):
-            nc.vector.tensor_copy(v_w[a][s][:], tab_w[a][:].bitcast(U32).indirect(offs_sb[:, 32 * s : 32 * (s + 1)]))
+            entries = offs_sb[:, BANK // 16 * s : BANK // 16 * (s + 1)]
+            nc.vector.tensor_copy(v_w[a][s][:], tab_w[a][:].bitcast(U32).indirect(entries))
 
         def deal_wc(b):
-            cols = slice(BANK * b, BANK * (b + 1))
+            cols = slice(GROUP * b, GROUP * (b + 1))
             nc.vector.tensor_copy(
                 out=wc_w[b][:].rearrange("p a (t m) -> p a m t", t=4),
                 in_=wc_raw[:].bitcast(U16)[:, :, cols].rearrange("p a (m t) -> p a m t", t=4),
@@ -120,25 +129,22 @@ def tile_list_flow_congestion_routing_kernel(
                 in_=wcs_raw[:, :, cols].rearrange("p a (m t) -> p a m t", t=4),
             )
 
-        def round_w1(b, a, lo=0, hi=BANK):
-            out = w1_bf[a].rearrange("p (t m j) -> p m j t", t=4, j=4)[:, lo // 4 : hi // 4, :, :]
-            in_ = w1_raw[b][a][:, :, lo:hi].rearrange("p j (m t) -> p m j t", t=4)
-            if b == 0:
-                nc.vector.tensor_copy(out=out, in_=in_)
-            else:
-                nc.scalar.copy(out=out, in_=in_)
+        def round_w1(copy, b, a, lo=0, hi=GROUP):
+            copy(
+                out=w1_bf[a].rearrange("p (t m j) -> p m j t", t=4, j=4)[:, lo // 4 : hi // 4, :, :],
+                in_=w1_raw[b][a][:, :, lo:hi].rearrange("p j (m t) -> p m j t", t=4),
+            )
 
-        def quantize_w1(b, a, lo=0, hi=BANK):
+        def quantize_w1(b, a, lo=0, hi=GROUP):
             nc.vector.quantize_mx(
                 out=w1_w[b][a][:, lo:hi].bitcast(FP8X4), scales=w1_s[b][a][:, lo:hi], in_=w1_bf[a][:, 4 * lo : 4 * hi]
             )
 
         def deal_w2_words():
-            for b in range(2):
-                nc.vector.tensor_copy(
-                    out=w2_w[b][:].rearrange("p (g t m) -> p g m t", g=2, t=4),
-                    in_=w2_raw[:, b, :].rearrange("p (g m t) -> p g m t", g=2, t=4),
-                )
+            nc.vector.tensor_copy(
+                out=w2_w[:].rearrange("p b (g t m) -> p (b g) m t", g=2, t=4),
+                in_=w2_raw[:].rearrange("p b (g m t) -> p (b g) m t", g=2, t=4),
+            )
 
         def deal_w2_scales():
             nc.vector.tensor_copy(
@@ -151,178 +157,174 @@ def tile_list_flow_congestion_routing_kernel(
         load_w1(0, 0)
         deal_wc(0)
         deal_wc(1)
-        load_w1(0, 1, 0, HALF)
-        load_w1(0, 1, HALF, BANK)
+        load_w1(0, 1, 0, GROUP // 2)
+        load_w1(0, 1, GROUP // 2, GROUP)
         gather_words(1, 0)
         gather_words(1, 1)
-        round_w1(0, 0)
+        round_w1(nc.vector.tensor_copy, 0, 0)
         load_w1(1, 0)
-        quantize_w1(0, 0)
-        round_w1(0, 1, 0, HALF)
-        round_w1(0, 1, HALF, BANK)
+        round_w1(nc.vector.tensor_copy, 0, 1, 0, GROUP // 2)
+        quantize_w1(0, 0, 0, P)
+        round_w1(nc.vector.tensor_copy, 0, 1, GROUP // 2, GROUP)
         load_w1(1, 1)
         quantize_w1(0, 1, 0, P)
-        quantize_w1(0, 1, P, HALF)
-        quantize_w1(0, 1, HALF, BANK)
+        for lo, hi in ((P, 2 * P), (2 * P, GROUP)):
+            for a in range(2):
+                quantize_w1(0, a, lo, hi)
 
-        h = [tile([P, S], F32, "h%d" % i) for i in range(3)]
+        h = [tile([P, S], F32, "h%d" % i) for i in range(H_RING)]
         w2_s = tile([P, N], U8, "w2_s", "h0")
-        first = [tile([P, 4, PAIRS], F32, "first%d" % b) for b in range(2)]
+        first_flat = [tile([P, 4 * PAIRS + HALF * b], F32, "first%d" % b) for b in range(2)]
+        first = [first_flat[b][:, 0 : 4 * PAIRS].rearrange("p (t j) -> p t j", t=4) for b in range(2)]
         second = [tile([P, 4, PAIRS], F32, "second%d" % b) for b in range(2)]
         damp = []
-        for u in range(8):
-            if u in (0, 4, 7):
+        for u in range(SLICES):
+            if u in OWN_DAMP:
                 own = tile([P, S], F32, "damp%d" % u)
                 damp.append([own[:, BANK * s : BANK * (s + 1)] for s in range(2)])
             else:
                 b, t = divmod(u - 1, 4)
                 damp.append([first[b][:, t, :], second[b][:, t, :]])
-        z_bf = [tile([P, 4 * HALF], BF16, "z_bf%d" % i) for i in range(4)]
-        z_w = [tile([P, HALF], U32, "z_w%d" % i) for i in range(4)]
-        z_s = [tile([P, HALF], U8, "z_s%d" % i) for i in range(4)]
+        z_bf = tile([P, 4 * PAIRS], BF16, "z_bf")
+        z_bf_early = first_flat[1][:, 4 * PAIRS - HALF : 4 * PAIRS + HALF].bitcast(BF16)
+        z_w = [tile([P, PAIRS], U32, "z_w%d" % b) for b in range(2)]
+        z_s = [tile([P, PAIRS], U8, "z_s%d" % b) for b in range(2)]
+
+        def first_product(pair, words, scales):
+            for s in range(2):
+                for a in (1, 0):
+                    nc.tensor.matmul_mx(
+                        out=banks[2 * pair + s][:],
+                        lhsT=words(a),
+                        lhsT_scale=scales(a),
+                        rhs=v_w[a][s][:].bitcast(FP8X4),
+                        rhs_scale=v_s[a][:, BANK * s : BANK * (s + 1)],
+                        start=(a == 1),
+                        stop=(a == 0),
+                    )
 
         def cap_stage(u):
             b, t = divmod(u, 4)
             cols = slice(P * t, P * (t + 1))
+            pair = u % 4
+            first_product(pair, lambda a: wc_w[b][:, a, cols].bitcast(FP4X4), lambda a: wc_s[b][:, a, cols])
             for s in range(2):
-                for a in (1, 0):
-                    nc.tensor.matmul_mx(
-                        out=banks[2 * (u % 4) + s][:],
-                        lhsT=wc_w[b][:, a, cols].bitcast(FP4X4),
-                        lhsT_scale=wc_s[b][:, a, cols],
-                        rhs=v_w[a][s][:].bitcast(FP8X4),
-                        rhs_scale=v_s[a][:, BANK * s : BANK * (s + 1)],
-                        start=(a == 1),
-                        stop=(a == 0),
-                    )
-            halves = damp[u]
+                nc.scalar.activation(out=damp[u][s], in_=banks[2 * pair + s][:], func=ACT.Abs)
             for s in range(2):
-                nc.scalar.activation(out=halves[s], in_=banks[2 * (u % 4) + s][:], func=ACT.Abs)
+                nc.scalar.activation(out=damp[u][s], in_=damp[u][s], func=ACT.Abs_reciprocal_sqrt, bias=1.0)
             for s in range(2):
-                nc.scalar.activation(out=halves[s], in_=halves[s], func=ACT.Abs_reciprocal_sqrt, bias=1.0)
-            for s in range(2):
-                nc.scalar.activation(out=halves[s], in_=halves[s], func=ACT.Square)
+                nc.scalar.activation(out=damp[u][s], in_=damp[u][s], func=ACT.Square)
 
         def load_stage(u):
             b, t = divmod(u, 4)
             cols = slice(P * t, P * (t + 1))
+            pair = (u - 1) % 4
+            first_product(pair, lambda a: w1_w[b][a][:, cols].bitcast(FP8X4), lambda a: w1_s[b][a][:, cols])
             for s in range(2):
-                for a in (1, 0):
-                    nc.tensor.matmul_mx(
-                        out=banks[2 * ((u - 1) % 4) + s][:],
-                        lhsT=w1_w[b][a][:, cols].bitcast(FP8X4),
-                        lhsT_scale=w1_s[b][a][:, cols],
-                        rhs=v_w[a][s][:].bitcast(FP8X4),
-                        rhs_scale=v_s[a][:, BANK * s : BANK * (s + 1)],
-                        start=(a == 1),
-                        stop=(a == 0),
-                    )
-            for s in range(2):
-                cols_s = slice(BANK * s, BANK * (s + 1))
                 nc.vector.tensor_tensor(
-                    out=h[u % 3][:, cols_s], in0=banks[2 * ((u - 1) % 4) + s][:], in1=damp[u][s], op=ALU.mult
+                    out=h[u % H_RING][:, BANK * s : BANK * (s + 1)],
+                    in0=banks[2 * pair + s][:],
+                    in1=damp[u][s],
+                    op=ALU.mult,
                 )
 
-        def pick(u, which, lo=0, hi=PAIRS):
+        def pick(u, lo=0, hi=PAIRS):
             b, t = divmod(u, 4)
-            dst, pos = ((first, pos1_sb), (second, pos2_sb))[which]
-            nc.vector.tensor_copy(dst[b][:, t, lo:hi], h[u % 3][:].indirect(pos[:, lo // 16 : hi // 16]))
+            for picked, pos in ((first, pos1_sb), (second, pos2_sb)):
+                nc.vector.tensor_copy(picked[b][:, t, lo:hi], h[u % H_RING][:].indirect(pos[:, lo // 16 : hi // 16]))
 
-        def make_z(b, s):
-            cols = slice(HALF * s, HALF * (s + 1))
+        def make_z(b, cols, rounded):
             nc.vector.tensor_tensor(
-                out=z_bf[2 * b + s][:].rearrange("p (c i t) -> p c t i", t=4, i=4),
+                out=rounded.rearrange("p (c i t) -> p c t i", t=4, i=4),
                 in0=first[b][:, :, cols].rearrange("p t (c i) -> p c t i", i=4),
                 in1=second[b][:, :, cols].rearrange("p t (c i) -> p c t i", i=4),
                 op=ALU.max,
             )
+            nc.vector.quantize_mx(out=z_w[b][:, cols].bitcast(FP8X4), scales=z_s[b][:, cols], in_=rounded)
 
-        def quantize_z(b, s):
-            i = 2 * b + s
-            nc.vector.quantize_mx(out=z_w[i][:].bitcast(FP8X4), scales=z_s[i][:], in_=z_bf[i][:])
+        def y_psum(s, g, t):
+            return banks[2 * Y_BANKS[2 * s + g] + t // 2][:, HALF * (t % 2) : HALF * (t % 2 + 1)]
 
         def y_passes(b, s):
             for g in range(2):
                 for t in range(4):
-                    cols = slice(BANK * g + P * t, BANK * g + P * (t + 1))
-                    bank = banks[2 * (0, 3, 1, 2)[2 * s + g] + t // 2]
+                    cols = slice(GROUP * g + P * t, GROUP * g + P * (t + 1))
                     nc.tensor.matmul_mx(
-                        out=bank[:, HALF * (t % 2) : HALF * (t % 2 + 1)],
-                        lhsT=w2_w[b][:, cols].bitcast(FP8X4),
+                        out=y_psum(s, g, t),
+                        lhsT=w2_w[:, b, cols].bitcast(FP8X4),
                         lhsT_scale=w2_s[4 * b : P, cols],
-                        rhs=z_w[2 * b + s][:].bitcast(FP8X4),
-                        rhs_scale=z_s[2 * b + s][:],
+                        rhs=z_w[b][:, HALF * s : HALF * (s + 1)].bitcast(FP8X4),
+                        rhs_scale=z_s[b][:, HALF * s : HALF * (s + 1)],
                         start=(b == 0 and t % 2 == 0),
                         stop=(b == 1 and t % 2 == 1),
                     )
 
-        for u in range(3):
+        for u in range(AHEAD):
             cap_stage(u)
-        for u in range(8):
+        for u in range(SLICES):
             load_stage(u)
-            if u + 3 < 8:
-                cap_stage(u + 3)
+            if u + AHEAD < SLICES:
+                cap_stage(u + AHEAD)
             if u == 0:
                 for a in range(2):
-                    for lo in (0, HALF):
-                        round_w1(1, a, lo, lo + HALF)
+                    for lo in (0, GROUP // 2):
+                        round_w1(nc.scalar.copy, 1, a, lo, lo + GROUP // 2)
                     quantize_w1(1, a)
                 load_w2()
-                load_w2_scales()
                 nc.sync.dma_start(out=bias[:], in_=b2.rearrange("(g p t) -> p g t", g=2, t=4))
-            if u in (1, 2, 3, 5, 6):
-                for which in range(2):
-                    pick(u - 1, which)
-            if u in (3, 6):
-                for which in range(2):
-                    pick(u, which)
+            if u not in OWN_DAMP:
+                pick(u - 1)
+            if u + 1 in OWN_DAMP:
+                pick(u)
             if u == 3:
-                for s in range(2):
-                    make_z(0, s)
-                for s in range(2):
-                    quantize_z(0, s)
+                make_z(0, slice(0, PAIRS), z_bf[:])
             if u == 4:
                 deal_w2_words()
-        deal_w2_scales()
+            if u == SLICES - 2:
+                deal_w2_scales()
 
         y = [[tile([P, 4, HALF], F32, "y%d%d" % (s, g)) for g in range(2)] for s in range(2)]
         y_bf = [[tile([P, 4 * HALF], BF16, "y_bf%d%d" % (s, g)) for g in range(2)] for s in range(2)]
-        y_w = [[tile([P, HALF], I32, "y_w%d%d" % (s, g)) for g in range(2)] for s in range(2)]
+        y_w = [tile([P, PAIRS], I32, "y_w%d" % g) for g in range(2)]
         y_s = tile([P, 2, PAIRS], U8, "y_s")
 
-        def finish(s, g):
-            cols = slice(HALF * s, HALF * (s + 1))
-            for t in range(4):
-                bank = banks[2 * (0, 3, 1, 2)[2 * s + g] + t // 2]
-                nc.scalar.activation(
-                    out=y[s][g][:, t, :],
-                    in_=bank[:, HALF * (t % 2) : HALF * (t % 2 + 1)],
-                    func=ACT.Identity,
-                    bias=bias[:, g, t : t + 1],
+        def finish(s, g, round_copies):
+            width = HALF // len(round_copies)
+            for piece, round_copy in enumerate(round_copies):
+                lo = width * piece
+                for t in range(4):
+                    nc.scalar.activation(
+                        out=y[s][g][:, t, lo : lo + width],
+                        in_=y_psum(s, g, t)[:, lo : lo + width],
+                        func=ACT.Identity,
+                        bias=bias[:, g, t : t + 1],
+                    )
+                rounded = y_bf[s][g][:, 4 * lo : 4 * (lo + width)]
+                round_copy(
+                    out=rounded.rearrange("p (c i t) -> p c t i", t=4, i=4),
+                    in_=y[s][g][:, :, lo : lo + width].rearrange("p t (c i) -> p c t i", i=4),
                 )
-            rows = out_0[BANK * g : BANK * (g + 1), cols]
-            nc.sync.dma_start(out=rows.rearrange("(p t) j -> p t j", t=4), in_=y[s][g][:])
-            nc.vector.tensor_copy(
-                out=y_bf[s][g][:].rearrange("p (c i t) -> p c t i", t=4, i=4),
-                in_=y[s][g][:].rearrange("p t (c i) -> p c t i", i=4),
-            )
-            nc.vector.quantize_mx(out=y_w[s][g][:].bitcast(FP8X4), scales=y_s[:, g, cols], in_=y_bf[s][g][:])
-            nc.sync.dma_start(out=out_1[g].rearrange("p m t -> p (m t)").bitcast(I32)[:, cols], in_=y_w[s][g][:])
+                cols = slice(HALF * s + lo, HALF * s + lo + width)
+                nc.vector.quantize_mx(out=y_w[g][:, cols].bitcast(FP8X4), scales=y_s[:, g, cols], in_=rounded)
+            rows = out_0[GROUP * g : GROUP * (g + 1), HALF * s : HALF * (s + 1)].rearrange("(p t) j -> p t j", t=4)
+            for t in (0, 2):
+                nc.sync.dma_start(out=rows[:, t : t + 2, :], in_=y[s][g][:, t : t + 2, :])
 
         for s in range(2):
             y_passes(0, s)
-        for s in range(2):
-            for which in range(2):
-                pick(7, which, HALF * s, HALF * (s + 1))
-            make_z(1, s)
-            quantize_z(1, s)
+        for s, rounded in enumerate((z_bf_early, z_bf[:, 0 : 4 * HALF])):
+            pick(SLICES - 1, HALF * s, HALF * (s + 1))
+            make_z(1, slice(HALF * s, HALF * (s + 1)), rounded)
             y_passes(1, s)
-        for s in range(2):
-            for g in range(2):
-                finish(s, g)
+        finish(0, 0, [nc.vector.tensor_copy])
+        finish(0, 1, [nc.vector.tensor_copy])
+        finish(1, 0, [nc.vector.tensor_copy])
+        finish(1, 1, [nc.vector.tensor_copy, nc.scalar.copy])
+        for g in range(2):
+            nc.sync.dma_start(out=out_1[g].rearrange("p m t -> p (m t)").bitcast(I32), in_=y_w[g][:])
         for q in range(4):
             queue = nc.sync if q % 2 == 0 else nc.scalar
             queue.dma_start(
                 out=out_2[:, 4 * q : 4 * q + 4, :].rearrange("g r m -> r g m").bitcast(I32),
-                in_=y_s[32 * q : 32 * q + 4, :, :].bitcast(I32),
+                in_=y_s[QUAD * q : QUAD * q + 4, :, :].bitcast(I32),
             )

@@ -36,36 +36,41 @@ def tile_list_flow_congestion_routing_kernel(
     nc = tc.nc
     with ExitStack() as ctx:
         sb = ctx.enter_context(tc.tile_pool(name="sb", bufs=1))
+        shared = ctx.enter_context(tc.tile_pool(name="shared", bufs=1))
         ps = ctx.enter_context(tc.psum_pool(name="ps", bufs=1))
 
         def tile(shape, dtype, name, buffer=None):
             return sb.tile(shape, dtype, name=name, tag=buffer or name, align_bytes=64)
+
+        def placed(shape, dtype, name, offset):
+            return shared.tile(shape, dtype, name=name, align_bytes=64, offset=offset)
 
         offs_sb = sb.tile([P, S // 16], U16, name="offs_sb")
         pos1_sb = sb.tile([P, PAIRS // 16], U16, name="pos1_sb")
         pos2_sb = sb.tile([P, PAIRS // 16], U16, name="pos2_sb")
         banks = [ps.tile([P, BANK], F32, name="bank%d" % i) for i in range(8)]
 
-        tab_s = tile([P, T], U8, "tab_s", "stage2")
+        tab_s = placed([P, T], U8, "tab_s", 7168)
         tab_w = [tile([P, T], I32, "tab_w%d" % a, "stage%d" % (a + 1)) for a in range(2)]
         picked_s = tile([P, S], U8, "picked_s")
         v_w = [[tile([P, BANK], U32, "v_w%d%d" % (a, s)) for s in range(2)] for a in range(2)]
         v_s = [tile([P, S], U8, "v_s%d" % a) for a in range(2)]
-        wc_raw = tile([P, 2, H // 2], I32, "wc_raw", "stage0")
+        wc_raw = tile([P, 2, H // 2], I32, "wc_raw")
         wcs_raw = tile([P, 2, H], U8, "wcs_raw")
         wc_w = [tile([P, 2, GROUP], U16, "wc_w%d" % b) for b in range(2)]
-        wc_s = [tile([P, 2, GROUP], U8, "wc_s%d" % b) for b in range(2)]
+        wc_s_both = placed([P, 2, 2, GROUP], U8, "wc_s", 8192)
+        wc_s = [wc_s_both[:, b, :, :] for b in range(2)]
         w1_raw = [
-            [tile([P, 4, GROUP], F32, "w1_raw%d%d" % (b, a), "stage%d" % (1 - a)) for a in range(2)] for b in range(2)
+            [placed([P, 4, GROUP], F32, "w1_raw0%d" % a, 10240 * a) for a in range(2)],
+            [tile([P, 4, GROUP], F32, "w1_raw1%d" % a, "stage%d" % (a + 1)) for a in range(2)],
         ]
-        w1_bf_both = tile([P, 8 * GROUP], BF16, "w1_bf", "stage2")
-        w1_bf = [w1_bf_both[:, 4 * GROUP * a : 4 * GROUP * (a + 1)] for a in range(2)]
+        w1_bf = [[tile([P, 4 * GROUP], BF16, "w1_bf0%d" % a) for a in range(2)]]
         w1_w = [[tile([P, GROUP], U32, "w1_w%d%d" % (b, a)) for a in range(2)] for b in range(2)]
         w1_s = [[tile([P, GROUP], U8, "w1_s%d%d" % (b, a)) for a in range(2)] for b in range(2)]
-        w2_raw = tile([P, 2, N], I32, "w2_raw", "stage1")
-        w2s_raw = tile([P, N], U8, "w2s_raw", "stage0")
+        w2_raw = placed([P, 2, N], I32, "w2_raw", 10240)
+        w2s_raw = wcs_raw[:, 0, :]
         w2_w = tile([P, 2, N], I32, "w2_w")
-        bias = tile([P, 2, 4], F32, "bias", "stage2")
+        bias = placed([P, 2, 4], F32, "bias", 10240)
 
         nc.vector.memset(wcs_raw[:].bitcast(I32), 0)
         for q in range(4):
@@ -83,10 +88,9 @@ def tile_list_flow_congestion_routing_kernel(
 
         def load_w2():
             nc.sync.dma_start(out=w2_raw[:], in_=w2_words.rearrange("b p n i -> p b (n i)").bitcast(I32))
-            nc.vector.memset(w2s_raw[:].bitcast(I32), 0)
             for q in range(4):
                 nc.sync.dma_start(
-                    out=w2s_raw[QUAD * q : QUAD * q + 8, :].bitcast(I32),
+                    out=wcs_raw[QUAD * q : QUAD * q + 8, 0, :].bitcast(I32),
                     in_=w2_scales[:, 4 * q : 4 * q + 4, :].bitcast(I32),
                 )
 
@@ -96,48 +100,52 @@ def tile_list_flow_congestion_routing_kernel(
                 out=tab_s[QUAD * q + SCALE_ROW : QUAD * (q + 1), :].bitcast(I32),
                 in_=tab_scales[:, 4 * q : 4 * q + 4, :].bitcast(I32),
             )
+        nc.sync.dma_start(out=wc_raw[:], in_=wc_words.rearrange("a p c -> p a c").bitcast(I32))
+        load_table(0)
         nc.sync.dma_start(pos1_sb[:], pos1)
         nc.sync.dma_start(pos2_sb[:], pos2)
-        load_table(0)
-        nc.sync.dma_start(out=wc_raw[:], in_=wc_words.rearrange("a p c -> p a c").bitcast(I32))
         for q in range(4):
             nc.sync.dma_start(
                 out=wcs_raw[QUAD * q : QUAD * q + 4, :, :].bitcast(I32),
                 in_=wc_scales[:, 4 * q : 4 * q + 4, :].rearrange("a r c -> r a c").bitcast(I32),
             )
 
+        load_table(1)
+
         nc.vector.tensor_copy(picked_s[:], tab_s[:].indirect(offs_sb[:]))
         for a in range(2):
             top = SCALE_ROW + 4 * a
-            nc.scalar.dma_start(
+            nc.sync.dma_start(
                 out=v_s[a][0:PLANE_ROWS, :].bitcast(I32), in_=picked_s[top : top + PLANE_ROWS, :].bitcast(I32)
             )
-        load_table(1)
 
         def gather_words(a, s):
             entries = offs_sb[:, BANK // 16 * s : BANK // 16 * (s + 1)]
             nc.vector.tensor_copy(v_w[a][s][:], tab_w[a][:].bitcast(U32).indirect(entries))
 
-        def deal_wc(b):
+        def deal_wc_words(b):
             cols = slice(GROUP * b, GROUP * (b + 1))
             nc.vector.tensor_copy(
                 out=wc_w[b][:].rearrange("p a (t m) -> p a m t", t=4),
                 in_=wc_raw[:].bitcast(U16)[:, :, cols].rearrange("p a (m t) -> p a m t", t=4),
             )
+
+        def deal_wc_scales(b):
+            cols = slice(GROUP * b, GROUP * (b + 1))
             nc.vector.tensor_copy(
-                out=wc_s[b][:].rearrange("p a (t m) -> p a m t", t=4),
+                out=wc_s[b].rearrange("p a (t m) -> p a m t", t=4),
                 in_=wcs_raw[:, :, cols].rearrange("p a (m t) -> p a m t", t=4),
             )
 
         def round_w1(copy, b, a, lo=0, hi=GROUP):
             copy(
-                out=w1_bf[a].rearrange("p (t m j) -> p m j t", t=4, j=4)[:, lo // 4 : hi // 4, :, :],
+                out=w1_bf[b][a][:].rearrange("p (t m j) -> p m j t", t=4, j=4)[:, lo // 4 : hi // 4, :, :],
                 in_=w1_raw[b][a][:, :, lo:hi].rearrange("p j (m t) -> p m j t", t=4),
             )
 
         def quantize_w1(b, a, lo=0, hi=GROUP):
             nc.vector.quantize_mx(
-                out=w1_w[b][a][:, lo:hi].bitcast(FP8X4), scales=w1_s[b][a][:, lo:hi], in_=w1_bf[a][:, 4 * lo : 4 * hi]
+                out=w1_w[b][a][:, lo:hi].bitcast(FP8X4), scales=w1_s[b][a][:, lo:hi], in_=w1_bf[b][a][:, 4 * lo : 4 * hi]
             )
 
         def deal_w2_words():
@@ -149,24 +157,26 @@ def tile_list_flow_congestion_routing_kernel(
         def deal_w2_scales():
             nc.vector.tensor_copy(
                 out=w2_s[:].rearrange("p (g t m) -> p g m t", g=2, t=4),
-                in_=w2s_raw[:].rearrange("p (g m t) -> p g m t", g=2, t=4),
+                in_=w2s_raw.rearrange("p (g m t) -> p g m t", g=2, t=4),
             )
 
-        gather_words(0, 0)
-        gather_words(0, 1)
         load_w1(0, 0)
-        deal_wc(0)
-        deal_wc(1)
         load_w1(0, 1, 0, GROUP // 2)
         load_w1(0, 1, GROUP // 2, GROUP)
+        for b in range(2):
+            deal_wc_words(b)
+        gather_words(0, 0)
+        gather_words(0, 1)
+        load_w1(1, 0)
+        for b in range(2):
+            deal_wc_scales(b)
         gather_words(1, 0)
         gather_words(1, 1)
+        load_w1(1, 1)
         round_w1(nc.vector.tensor_copy, 0, 0)
-        load_w1(1, 0)
         round_w1(nc.vector.tensor_copy, 0, 1, 0, GROUP // 2)
         quantize_w1(0, 0, 0, P)
         round_w1(nc.vector.tensor_copy, 0, 1, GROUP // 2, GROUP)
-        load_w1(1, 1)
         quantize_w1(0, 1, 0, P)
         for lo, hi in ((P, 2 * P), (2 * P, GROUP)):
             for a in range(2):
@@ -185,7 +195,7 @@ def tile_list_flow_congestion_routing_kernel(
             else:
                 b, t = divmod(u - 1, 4)
                 damp.append([first[b][:, t, :], second[b][:, t, :]])
-        z_bf = tile([P, 4 * PAIRS], BF16, "z_bf")
+        z_bf = tile([P, 4 * PAIRS], BF16, "z_bf", "w1_bf01")
         z_bf_early = first_flat[1][:, 4 * PAIRS - HALF : 4 * PAIRS + HALF].bitcast(BF16)
         z_w = [tile([P, PAIRS], U32, "z_w%d" % b) for b in range(2)]
         z_s = [tile([P, PAIRS], U8, "z_s%d" % b) for b in range(2)]
@@ -266,6 +276,7 @@ def tile_list_flow_congestion_routing_kernel(
             if u + AHEAD < SLICES:
                 cap_stage(u + AHEAD)
             if u == 0:
+                w1_bf.append([tile([P, 4 * GROUP], BF16, "w1_bf10", "damp0"), w1_bf[0][1]])
                 for a in range(2):
                     for lo in (0, GROUP // 2):
                         round_w1(nc.scalar.copy, 1, a, lo, lo + GROUP // 2)

@@ -26,7 +26,8 @@ AHEAD = 3
 H_RING = 3
 SCALE_ROW = 24
 PLANE_ROWS = 100
-OWN_DAMP = (0, 4, 7)
+OWN_DAMP = (0, 4, 5, 6, 7)
+ON_GPSIMD = (4, 5, 6)
 Y_BANKS = (0, 3, 1, 2)
 
 
@@ -64,7 +65,7 @@ def tile_list_flow_congestion_routing_kernel(
             [placed([P, 4, GROUP], F32, "w1_raw0%d" % a, 10240 * a) for a in range(2)],
             [tile([P, 4, GROUP], F32, "w1_raw1%d" % a, "stage%d" % (a + 1)) for a in range(2)],
         ]
-        w1_bf = [[tile([P, 4 * GROUP], BF16, "w1_bf0%d" % a) for a in range(2)]]
+        w1_bf = [[tile([P, 4 * GROUP], BF16, "w1_bf%d%d" % (b, a)) for a in range(2)] for b in range(2)]
         w1_w = [[tile([P, GROUP], U32, "w1_w%d%d" % (b, a)) for a in range(2)] for b in range(2)]
         w1_s = [[tile([P, GROUP], U8, "w1_s%d%d" % (b, a)) for a in range(2)] for b in range(2)]
         w2_raw = placed([P, 2, N], I32, "w2_raw", 10240)
@@ -143,6 +144,9 @@ def tile_list_flow_congestion_routing_kernel(
                 in_=w1_raw[b][a][:, :, lo:hi].rearrange("p j (m t) -> p m j t", t=4),
             )
 
+        def gpsimd_round(out, in_):
+            nc.gpsimd.tensor_scalar(out=out, in0=in_, scalar1=1.0, scalar2=0.0, op0=ALU.mult, op1=ALU.add)
+
         def quantize_w1(b, a, lo=0, hi=GROUP):
             nc.vector.quantize_mx(
                 out=w1_w[b][a][:, lo:hi].bitcast(FP8X4), scales=w1_s[b][a][:, lo:hi], in_=w1_bf[b][a][:, 4 * lo : 4 * hi]
@@ -182,11 +186,14 @@ def tile_list_flow_congestion_routing_kernel(
             for a in range(2):
                 quantize_w1(0, a, lo, hi)
 
-        h = [tile([P, S], F32, "h%d" % i) for i in range(H_RING)]
+        ring = [tile([P, S], F32, "h%d" % i) for i in range(H_RING)]
+        h = [ring[u % H_RING] for u in range(SLICES)]
+        h[3] = tile([P, S], F32, "h3", "w1_bf11")
         w2_s = tile([P, N], U8, "w2_s", "h0")
         first_flat = [tile([P, 4 * PAIRS + HALF * b], F32, "first%d" % b) for b in range(2)]
         first = [first_flat[b][:, 0 : 4 * PAIRS].rearrange("p (t j) -> p t j", t=4) for b in range(2)]
         second = [tile([P, 4, PAIRS], F32, "second%d" % b) for b in range(2)]
+        load_sb = [tile([P, BANK], F32, "load_sb%d" % s) for s in range(4)]
         damp = []
         for u in range(SLICES):
             if u in OWN_DAMP:
@@ -195,7 +202,7 @@ def tile_list_flow_congestion_routing_kernel(
             else:
                 b, t = divmod(u - 1, 4)
                 damp.append([first[b][:, t, :], second[b][:, t, :]])
-        z_bf = tile([P, 4 * PAIRS], BF16, "z_bf", "w1_bf01")
+        z_bf = tile([P, 4 * PAIRS], BF16, "z_bf")
         z_bf_early = first_flat[1][:, 4 * PAIRS - HALF : 4 * PAIRS + HALF].bitcast(BF16)
         z_w = [tile([P, PAIRS], U32, "z_w%d" % b) for b in range(2)]
         z_s = [tile([P, PAIRS], U8, "z_s%d" % b) for b in range(2)]
@@ -231,17 +238,23 @@ def tile_list_flow_congestion_routing_kernel(
             pair = (u - 1) % 4
             first_product(pair, lambda a: w1_w[b][a][:, cols].bitcast(FP8X4), lambda a: w1_s[b][a][:, cols])
             for s in range(2):
-                nc.vector.tensor_tensor(
-                    out=h[u % H_RING][:, BANK * s : BANK * (s + 1)],
-                    in0=banks[2 * pair + s][:],
-                    in1=damp[u][s],
-                    op=ALU.mult,
-                )
+                if u in ON_GPSIMD:
+                    nc.scalar.copy(out=load_sb[2 * (u % 2) + s][:], in_=banks[2 * pair + s][:])
+                    nc.gpsimd.tensor_tensor(
+                        out=h[u][:, BANK * s : BANK * (s + 1)], in0=load_sb[2 * (u % 2) + s][:], in1=damp[u][s], op=ALU.mult
+                    )
+                else:
+                    nc.vector.tensor_tensor(
+                        out=h[u][:, BANK * s : BANK * (s + 1)],
+                        in0=banks[2 * pair + s][:],
+                        in1=damp[u][s],
+                        op=ALU.mult,
+                    )
 
         def pick(u, lo=0, hi=PAIRS):
             b, t = divmod(u, 4)
             for picked, pos in ((first, pos1_sb), (second, pos2_sb)):
-                nc.vector.tensor_copy(picked[b][:, t, lo:hi], h[u % H_RING][:].indirect(pos[:, lo // 16 : hi // 16]))
+                nc.vector.tensor_copy(picked[b][:, t, lo:hi], h[u][:].indirect(pos[:, lo // 16 : hi // 16]))
 
         def make_z(b, cols, rounded):
             nc.vector.tensor_tensor(
@@ -273,13 +286,17 @@ def tile_list_flow_congestion_routing_kernel(
             cap_stage(u)
         for u in range(SLICES):
             load_stage(u)
-            if u + AHEAD < SLICES:
+            if u < 2:
                 cap_stage(u + AHEAD)
+            if u in ON_GPSIMD:
+                cap_stage(u + 1)
             if u == 0:
-                w1_bf.append([tile([P, 4 * GROUP], BF16, "w1_bf10", "damp0"), w1_bf[0][1]])
                 for a in range(2):
-                    for lo in (0, GROUP // 2):
-                        round_w1(nc.scalar.copy, 1, a, lo, lo + GROUP // 2)
+                    for t in range(4):
+                        gpsimd_round(
+                            out=w1_bf[1][a][:].rearrange("p (t m j) -> p t m j", t=4, j=4)[:, t, :, :],
+                            in_=w1_raw[1][a][:].rearrange("p j (m t) -> p t m j", t=4)[:, t, :, :],
+                        )
                     quantize_w1(1, a)
                 load_w2()
                 nc.sync.dma_start(out=bias[:], in_=b2.rearrange("(g p t) -> p g t", g=2, t=4))

@@ -65,12 +65,13 @@ def tile_list_flow_congestion_routing_kernel(
             [placed([P, 4, GROUP], F32, "w1_raw0%d" % a, 10240 * a) for a in range(2)],
             [tile([P, 4, GROUP], F32, "w1_raw1%d" % a, "stage%d" % (a + 1)) for a in range(2)],
         ]
-        w1_bf = [[tile([P, 4 * GROUP], BF16, "w1_bf%d%d" % (b, a)) for a in range(2)] for b in range(2)]
+        w1_bf = [[tile([P, 4 * GROUP], BF16, "w1_bf%d" % a) for a in range(2)]]
+        w1_bf.append(w1_bf[0][::-1])
         w1_w = [[tile([P, GROUP], U32, "w1_w%d%d" % (b, a)) for a in range(2)] for b in range(2)]
         w1_s = [[tile([P, GROUP], U8, "w1_s%d%d" % (b, a)) for a in range(2)] for b in range(2)]
         w2_raw = placed([P, 2, N], I32, "w2_raw", 10240)
         w2s_raw = wcs_raw[:, 0, :]
-        w2_w = tile([P, 2, N], I32, "w2_w")
+        w2_w = tile([P, 2, N], I32, "w2_w", "stage2")
         bias = placed([P, 2, 4], F32, "bias", 10240)
 
         nc.vector.memset(wcs_raw[:].bitcast(I32), 0)
@@ -188,7 +189,7 @@ def tile_list_flow_congestion_routing_kernel(
 
         ring = [tile([P, S], F32, "h%d" % i) for i in range(H_RING)]
         h = [ring[u % H_RING] for u in range(SLICES)]
-        h[3] = tile([P, S], F32, "h3", "w1_bf11")
+        h[3] = tile([P, S], F32, "h3", "w1_bf0")
         w2_s = tile([P, N], U8, "w2_s", "h0")
         first_flat = [tile([P, 4 * PAIRS + HALF * b], F32, "first%d" % b) for b in range(2)]
         first = [first_flat[b][:, 0 : 4 * PAIRS].rearrange("p (t j) -> p t j", t=4) for b in range(2)]
@@ -204,7 +205,7 @@ def tile_list_flow_congestion_routing_kernel(
                 damp.append([first[b][:, t, :], second[b][:, t, :]])
         z_bf = tile([P, 4 * PAIRS], BF16, "z_bf")
         z_bf_early = first_flat[1][:, 4 * PAIRS - HALF : 4 * PAIRS + HALF].bitcast(BF16)
-        z_w = [tile([P, PAIRS], U32, "z_w%d" % b) for b in range(2)]
+        z_w = [tile([P, PAIRS], U32, "z_w0", "load_sb1"), tile([P, PAIRS], U32, "z_w1")]
         z_s = [tile([P, PAIRS], U8, "z_s%d" % b) for b in range(2)]
 
         def first_product(pair, words, scales):
@@ -256,13 +257,15 @@ def tile_list_flow_congestion_routing_kernel(
             for picked, pos in ((first, pos1_sb), (second, pos2_sb)):
                 nc.vector.tensor_copy(picked[b][:, t, lo:hi], h[u][:].indirect(pos[:, lo // 16 : hi // 16]))
 
-        def make_z(b, cols, rounded):
+        def maximum(b, cols, rounded):
             nc.vector.tensor_tensor(
                 out=rounded.rearrange("p (c i t) -> p c t i", t=4, i=4),
                 in0=first[b][:, :, cols].rearrange("p t (c i) -> p c t i", i=4),
                 in1=second[b][:, :, cols].rearrange("p t (c i) -> p c t i", i=4),
                 op=ALU.max,
             )
+
+        def quantize_z(b, cols, rounded):
             nc.vector.quantize_mx(out=z_w[b][:, cols].bitcast(FP8X4), scales=z_s[b][:, cols], in_=rounded)
 
         def y_psum(s, g, t):
@@ -305,10 +308,11 @@ def tile_list_flow_congestion_routing_kernel(
             if u + 1 in OWN_DAMP:
                 pick(u)
             if u == 3:
-                make_z(0, slice(0, PAIRS), z_bf[:])
+                maximum(0, slice(0, PAIRS), z_bf[:])
             if u == 4:
                 deal_w2_words()
             if u == SLICES - 2:
+                quantize_z(0, slice(0, PAIRS), z_bf[:])
                 deal_w2_scales()
 
         y = [[tile([P, 4, HALF], F32, "y%d%d" % (s, g)) for g in range(2)] for s in range(2)]
@@ -342,7 +346,8 @@ def tile_list_flow_congestion_routing_kernel(
             y_passes(0, s)
         for s, rounded in enumerate((z_bf_early, z_bf[:, 0 : 4 * HALF])):
             pick(SLICES - 1, HALF * s, HALF * (s + 1))
-            make_z(1, slice(HALF * s, HALF * (s + 1)), rounded)
+            maximum(1, slice(HALF * s, HALF * (s + 1)), rounded)
+            quantize_z(1, slice(HALF * s, HALF * (s + 1)), rounded)
             y_passes(1, s)
         finish(0, 0, [nc.vector.tensor_copy])
         finish(0, 1, [nc.vector.tensor_copy])

@@ -24,6 +24,7 @@ HALF = PAIRS // 2
 SLICES = H // P
 AHEAD = 3
 H_RING = 3
+TAB1_AT = 10240
 SCALE_ROW = 24
 PLANE_ROWS = 100
 OWN_DAMP = (0, 4, 5, 6, 7)
@@ -52,7 +53,7 @@ def tile_list_flow_congestion_routing_kernel(
         banks = [ps.tile([P, BANK], F32, name="bank%d" % i) for i in range(8)]
 
         tab_s = placed([P, T], U8, "tab_s", 7168)
-        tab_w = [tile([P, T], I32, "tab_w%d" % a, "stage%d" % (a + 1)) for a in range(2)]
+        tab_w = [tile([P, T], I32, "tab_w0", "stage1"), placed([P, T], I32, "tab_w1", TAB1_AT)]
         picked_s = tile([P, S], U8, "picked_s")
         v_w = [[tile([P, BANK], U32, "v_w%d%d" % (a, s)) for s in range(2)] for a in range(2)]
         v_s = [tile([P, S], U8, "v_s%d" % a) for a in range(2)]
@@ -62,22 +63,21 @@ def tile_list_flow_congestion_routing_kernel(
         wc_s_both = placed([P, 2, 2, GROUP], U8, "wc_s", 8192)
         wc_s = [wc_s_both[:, b, :, :] for b in range(2)]
         w1_raw = [
-            [placed([P, 4, GROUP], F32, "w1_raw0%d" % a, 10240 * a) for a in range(2)],
-            [tile([P, 4, GROUP], F32, "w1_raw1%d" % a, "stage%d" % (a + 1)) for a in range(2)],
+            [placed([P, 4, GROUP], F32, "w1_raw00", 0), tile([P, 4, GROUP], F32, "w1_raw01", "wc_raw")],
+            [tile([P, 4, GROUP], F32, "w1_raw10", "stage1"), placed([P, 4, GROUP], F32, "w1_raw11", TAB1_AT)],
         ]
         w1_bf = [[tile([P, 4 * GROUP], BF16, "w1_bf%d" % a) for a in range(2)]]
         w1_bf.append(w1_bf[0][::-1])
         w1_w = [[tile([P, GROUP], U32, "w1_w%d%d" % (b, a)) for a in range(2)] for b in range(2)]
         w1_s = [[tile([P, GROUP], U8, "w1_s%d%d" % (b, a)) for a in range(2)] for b in range(2)]
-        w2_raw = placed([P, 2, N], I32, "w2_raw", 10240)
+        w2_raw = tile([P, 2, N], I32, "w2_raw", "wc_raw")
         w2s_raw = wcs_raw[:, 0, :]
-        w2_w = tile([P, 2, N], I32, "w2_w", "stage2")
-        bias = placed([P, 2, 4], F32, "bias", 10240)
+        w2_w = placed([P, 2, N], I32, "w2_w", TAB1_AT)
+        bias = tile([P, 2, 4], F32, "bias", "wc_raw")
 
         nc.vector.memset(wcs_raw[:].bitcast(I32), 0)
-        for q in range(4):
-            engine = nc.vector if q < 2 else nc.gpsimd
-            engine.memset(tab_s[QUAD * q : QUAD * q + SCALE_ROW, :].bitcast(I32), 0)
+        nc.gpsimd.memset(tab_s[QUAD : 2 * QUAD, :].bitcast(I32), 0)
+        nc.vector.memset(tab_s[2 * QUAD : P, :].bitcast(I32), 0)
         for a in range(2):
             nc.gpsimd.memset(v_s[a][:].bitcast(I32), 0)
 
@@ -97,28 +97,25 @@ def tile_list_flow_congestion_routing_kernel(
                 )
 
         nc.sync.dma_start(offs_sb[:], offs)
-        for q in range(4):
-            nc.sync.dma_start(
-                out=tab_s[QUAD * q + SCALE_ROW : QUAD * (q + 1), :].bitcast(I32),
-                in_=tab_scales[:, 4 * q : 4 * q + 4, :].bitcast(I32),
-            )
+        nc.sync.dma_start(out=tab_s[0:QUAD, :].bitcast(I32), in_=tab_scales.rearrange("a q t -> (a q) t").bitcast(I32))
         nc.sync.dma_start(out=wc_raw[:], in_=wc_words.rearrange("a p c -> p a c").bitcast(I32))
-        load_table(0)
         nc.sync.dma_start(pos1_sb[:], pos1)
         nc.sync.dma_start(pos2_sb[:], pos2)
+        load_table(0)
         for q in range(4):
             nc.sync.dma_start(
                 out=wcs_raw[QUAD * q : QUAD * q + 4, :, :].bitcast(I32),
                 in_=wc_scales[:, 4 * q : 4 * q + 4, :].rearrange("a r c -> r a c").bitcast(I32),
             )
 
-        load_table(1)
 
         nc.vector.tensor_copy(picked_s[:], tab_s[:].indirect(offs_sb[:]))
-        for a in range(2):
-            top = SCALE_ROW + 4 * a
+        for i in range(8):
+            a, q = divmod(i, 4)
+            if i == 2:
+                load_table(1)
             nc.sync.dma_start(
-                out=v_s[a][0:PLANE_ROWS, :].bitcast(I32), in_=picked_s[top : top + PLANE_ROWS, :].bitcast(I32)
+                out=v_s[a][QUAD * q : QUAD * q + 4, :].bitcast(I32), in_=picked_s[4 * i : 4 * i + 4, :].bitcast(I32)
             )
 
         def gather_words(a, s):
@@ -295,10 +292,10 @@ def tile_list_flow_congestion_routing_kernel(
                 cap_stage(u + 1)
             if u == 0:
                 for a in range(2):
-                    for t in range(4):
+                    for lo in range(0, P, P // 4):
                         gpsimd_round(
-                            out=w1_bf[1][a][:].rearrange("p (t m j) -> p t m j", t=4, j=4)[:, t, :, :],
-                            in_=w1_raw[1][a][:].rearrange("p j (m t) -> p t m j", t=4)[:, t, :, :],
+                            out=w1_bf[1][a][:].rearrange("p (t m j) -> p m t j", t=4, j=4)[:, lo : lo + P // 4, :, :],
+                            in_=w1_raw[1][a][:].rearrange("p j (m t) -> p m t j", t=4)[:, lo : lo + P // 4, :, :],
                         )
                     quantize_w1(1, a)
                 load_w2()

@@ -73,10 +73,10 @@ def tile_list_flow_congestion_routing_kernel(
         w2_raw = tile([P, 2, N], I32, "w2_raw", "wc_raw")
         w2s_raw = wcs_raw[:, 0, :]
         w2_w = placed([P, 2, N], I32, "w2_w", TAB1_AT)
-        bias = tile([P, 2, 4], F32, "bias", "wc_raw")
+        bias = placed([P, 2, 4], F32, "bias", 0)
 
-        nc.vector.memset(wcs_raw[:].bitcast(I32), 0)
-        nc.gpsimd.memset(tab_s[QUAD : 2 * QUAD, :].bitcast(I32), 0)
+        nc.gpsimd.memset(wcs_raw[:].bitcast(I32), 0)
+        nc.vector.memset(tab_s[QUAD : 2 * QUAD, :].bitcast(I32), 0)
         nc.vector.memset(tab_s[2 * QUAD : P, :].bitcast(I32), 0)
         for a in range(2):
             nc.gpsimd.memset(v_s[a][:].bitcast(I32), 0)
@@ -101,18 +101,18 @@ def tile_list_flow_congestion_routing_kernel(
         nc.sync.dma_start(out=wc_raw[:], in_=wc_words.rearrange("a p c -> p a c").bitcast(I32))
         nc.sync.dma_start(pos1_sb[:], pos1)
         nc.sync.dma_start(pos2_sb[:], pos2)
-        load_table(0)
         for q in range(4):
             nc.sync.dma_start(
                 out=wcs_raw[QUAD * q : QUAD * q + 4, :, :].bitcast(I32),
                 in_=wc_scales[:, 4 * q : 4 * q + 4, :].rearrange("a r c -> r a c").bitcast(I32),
             )
 
+        load_table(0)
 
         nc.vector.tensor_copy(picked_s[:], tab_s[:].indirect(offs_sb[:]))
         for i in range(8):
             a, q = divmod(i, 4)
-            if i == 2:
+            if i == 4:
                 load_table(1)
             nc.sync.dma_start(
                 out=v_s[a][QUAD * q : QUAD * q + 4, :].bitcast(I32), in_=picked_s[4 * i : 4 * i + 4, :].bitcast(I32)
@@ -157,10 +157,12 @@ def tile_list_flow_congestion_routing_kernel(
             )
 
         def deal_w2_scales():
-            nc.vector.tensor_copy(
-                out=w2_s[:].rearrange("p (g t m) -> p g m t", g=2, t=4),
-                in_=w2s_raw.rearrange("p (g m t) -> p g m t", g=2, t=4),
-            )
+            for g in range(2):
+                for t in range(4):
+                    nc.gpsimd.tensor_copy(
+                        out=w2_s[:, GROUP * g + P * t : GROUP * g + P * (t + 1)],
+                        in_=w2s_raw[:, GROUP * g : GROUP * (g + 1)].rearrange("p (m t) -> p m t", t=4)[:, :, t],
+                    )
 
         load_w1(0, 0)
         load_w1(0, 1, 0, GROUP // 2)
@@ -187,7 +189,7 @@ def tile_list_flow_congestion_routing_kernel(
         ring = [tile([P, S], F32, "h%d" % i) for i in range(H_RING)]
         h = [ring[u % H_RING] for u in range(SLICES)]
         h[3] = tile([P, S], F32, "h3", "w1_bf0")
-        w2_s = tile([P, N], U8, "w2_s", "h0")
+        w2_s = tile([P, N], U8, "w2_s", "wc_raw")
         first_flat = [tile([P, 4 * PAIRS + HALF * b], F32, "first%d" % b) for b in range(2)]
         first = [first_flat[b][:, 0 : 4 * PAIRS].rearrange("p (t j) -> p t j", t=4) for b in range(2)]
         second = [tile([P, 4, PAIRS], F32, "second%d" % b) for b in range(2)]
@@ -205,24 +207,24 @@ def tile_list_flow_congestion_routing_kernel(
         z_w = [tile([P, PAIRS], U32, "z_w0", "load_sb1"), tile([P, PAIRS], U32, "z_w1")]
         z_s = [tile([P, PAIRS], U8, "z_s%d" % b) for b in range(2)]
 
-        def first_product(pair, words, scales):
+        def first_product(pair, words, scales, order):
             for s in range(2):
-                for a in (1, 0):
+                for a in order:
                     nc.tensor.matmul_mx(
                         out=banks[2 * pair + s][:],
                         lhsT=words(a),
                         lhsT_scale=scales(a),
                         rhs=v_w[a][s][:].bitcast(FP8X4),
                         rhs_scale=v_s[a][:, BANK * s : BANK * (s + 1)],
-                        start=(a == 1),
-                        stop=(a == 0),
+                        start=(a == order[0]),
+                        stop=(a == order[1]),
                     )
 
         def cap_stage(u):
             b, t = divmod(u, 4)
             cols = slice(P * t, P * (t + 1))
             pair = u % 4
-            first_product(pair, lambda a: wc_w[b][:, a, cols].bitcast(FP4X4), lambda a: wc_s[b][:, a, cols])
+            first_product(pair, lambda a: wc_w[b][:, a, cols].bitcast(FP4X4), lambda a: wc_s[b][:, a, cols], (0, 1))
             for s in range(2):
                 nc.scalar.activation(out=damp[u][s], in_=banks[2 * pair + s][:], func=ACT.Abs)
             for s in range(2):
@@ -234,7 +236,7 @@ def tile_list_flow_congestion_routing_kernel(
             b, t = divmod(u, 4)
             cols = slice(P * t, P * (t + 1))
             pair = (u - 1) % 4
-            first_product(pair, lambda a: w1_w[b][a][:, cols].bitcast(FP8X4), lambda a: w1_s[b][a][:, cols])
+            first_product(pair, lambda a: w1_w[b][a][:, cols].bitcast(FP8X4), lambda a: w1_s[b][a][:, cols], (1, 0))
             for s in range(2):
                 if u in ON_GPSIMD:
                     nc.scalar.copy(out=load_sb[2 * (u % 2) + s][:], in_=banks[2 * pair + s][:])
@@ -306,11 +308,11 @@ def tile_list_flow_congestion_routing_kernel(
                 pick(u)
             if u == 3:
                 maximum(0, slice(0, PAIRS), z_bf[:])
-            if u == 4:
+            if u == 2:
                 deal_w2_words()
+                deal_w2_scales()
             if u == SLICES - 2:
                 quantize_z(0, slice(0, PAIRS), z_bf[:])
-                deal_w2_scales()
 
         y = [[tile([P, 4, HALF], F32, "y%d%d" % (s, g)) for g in range(2)] for s in range(2)]
         y_bf = [[tile([P, 4 * HALF], BF16, "y_bf%d%d" % (s, g)) for g in range(2)] for s in range(2)]

@@ -56,7 +56,8 @@ def tile_list_flow_congestion_routing_kernel(
         tab_w = [tile([P, T], I32, "tab_w0", "stage1"), placed([P, T], I32, "tab_w1", TAB1_AT)]
         picked_s = tile([P, S], U8, "picked_s")
         v_w = [[tile([P, BANK], U32, "v_w%d%d" % (a, s)) for s in range(2)] for a in range(2)]
-        v_s = [tile([P, S], U8, "v_s%d" % a) for a in range(2)]
+        v_s_both = tile([P, 2, S], U8, "v_s")
+        v_s = [v_s_both[:, a, :] for a in range(2)]
         wc_raw = tile([P, 2, H // 2], I32, "wc_raw")
         wcs_raw = tile([P, 2, H], U8, "wcs_raw")
         wc_w = [tile([P, 2, GROUP], U16, "wc_w%d" % b) for b in range(2)]
@@ -71,15 +72,21 @@ def tile_list_flow_congestion_routing_kernel(
         w1_w = [[tile([P, GROUP], U32, "w1_w%d%d" % (b, a)) for a in range(2)] for b in range(2)]
         w1_s = [[tile([P, GROUP], U8, "w1_s%d%d" % (b, a)) for a in range(2)] for b in range(2)]
         w2_raw = tile([P, 2, N], I32, "w2_raw", "wc_raw")
-        w2s_raw = wcs_raw[:, 0, :]
+        w2s_raw = tile([P, GROUP], U8, "w2s_raw")
+        w2s_dealt = tile([P, GROUP], U8, "w2s_dealt")
+        w2_s = tile([P, 2, 2, GROUP], U8, "w2_s")
         w2_w = placed([P, 2, N], I32, "w2_w", TAB1_AT)
         bias = placed([P, 2, 4], F32, "bias", 0)
 
+        warm = tile([P, 2], F32, "warm")
+        nc.vector.memset(warm[:, 0:1], 0.0)
+        nc.scalar.activation(out=warm[:, 1:2], in_=warm[:, 0:1], func=ACT.Abs_reciprocal_sqrt, bias=1.0)
         nc.gpsimd.memset(wcs_raw[:].bitcast(I32), 0)
         nc.vector.memset(tab_s[QUAD : 2 * QUAD, :].bitcast(I32), 0)
         nc.vector.memset(tab_s[2 * QUAD : P, :].bitcast(I32), 0)
-        for a in range(2):
-            nc.gpsimd.memset(v_s[a][:].bitcast(I32), 0)
+        nc.gpsimd.memset(v_s_both[:].bitcast(I32), 0)
+        nc.gpsimd.memset(w2s_raw[2 * QUAD : P, :].bitcast(I32), 0)
+        nc.gpsimd.memset(w2_s[:].bitcast(I32), 0)
 
         def load_table(a):
             nc.sync.dma_start(out=tab_w[a][:], in_=tab_words[a].rearrange("p t i -> p (t i)").bitcast(I32))
@@ -90,17 +97,10 @@ def tile_list_flow_congestion_routing_kernel(
 
         def load_w2():
             nc.sync.dma_start(out=w2_raw[:], in_=w2_words.rearrange("b p n i -> p b (n i)").bitcast(I32))
-            for q in range(4):
-                nc.sync.dma_start(
-                    out=wcs_raw[QUAD * q : QUAD * q + 8, 0, :].bitcast(I32),
-                    in_=w2_scales[:, 4 * q : 4 * q + 4, :].bitcast(I32),
-                )
 
         nc.sync.dma_start(offs_sb[:], offs)
-        nc.sync.dma_start(out=tab_s[0:QUAD, :].bitcast(I32), in_=tab_scales.rearrange("a q t -> (a q) t").bitcast(I32))
+        nc.sync.dma_start(out=tab_s[0:QUAD, :].bitcast(I32), in_=tab_scales.rearrange("a q t -> q a t").bitcast(I32))
         nc.sync.dma_start(out=wc_raw[:], in_=wc_words.rearrange("a p c -> p a c").bitcast(I32))
-        nc.sync.dma_start(pos1_sb[:], pos1)
-        nc.sync.dma_start(pos2_sb[:], pos2)
         for q in range(4):
             nc.sync.dma_start(
                 out=wcs_raw[QUAD * q : QUAD * q + 4, :, :].bitcast(I32),
@@ -108,15 +108,16 @@ def tile_list_flow_congestion_routing_kernel(
             )
 
         load_table(0)
+        nc.sync.dma_start(pos1_sb[:], pos1)
+        nc.sync.dma_start(pos2_sb[:], pos2)
 
         nc.vector.tensor_copy(picked_s[:], tab_s[:].indirect(offs_sb[:]))
-        for i in range(8):
-            a, q = divmod(i, 4)
-            if i == 4:
-                load_table(1)
+        for q in range(4):
             nc.sync.dma_start(
-                out=v_s[a][QUAD * q : QUAD * q + 4, :].bitcast(I32), in_=picked_s[4 * i : 4 * i + 4, :].bitcast(I32)
+                out=v_s_both[QUAD * q : QUAD * q + 4, :, :].bitcast(I32),
+                in_=picked_s[8 * q : 8 * q + 8, :].bitcast(I32),
             )
+        load_table(1)
 
         def gather_words(a, s):
             entries = offs_sb[:, BANK // 16 * s : BANK // 16 * (s + 1)]
@@ -157,23 +158,29 @@ def tile_list_flow_congestion_routing_kernel(
             )
 
         def deal_w2_scales():
-            for g in range(2):
-                for t in range(4):
-                    nc.gpsimd.tensor_copy(
-                        out=w2_s[:, GROUP * g + P * t : GROUP * g + P * (t + 1)],
-                        in_=w2s_raw[:, GROUP * g : GROUP * (g + 1)].rearrange("p (m t) -> p m t", t=4)[:, :, t],
-                    )
+            nc.vector.tensor_copy(
+                out=w2s_dealt[:].rearrange("p (t m) -> p m t", t=4), in_=w2s_raw[:].rearrange("p (m t) -> p m t", t=4)
+            )
+            for q in range(4):
+                nc.sync.dma_start(
+                    out=w2_s[QUAD * q : QUAD * q + 4, :, :, :].rearrange("r g b c -> r (g b c)").bitcast(I32),
+                    in_=w2s_dealt[16 * q : 16 * q + 16, :].bitcast(I32),
+                )
 
         load_w1(0, 0)
         load_w1(0, 1, 0, GROUP // 2)
         load_w1(0, 1, GROUP // 2, GROUP)
-        for b in range(2):
-            deal_wc_words(b)
+        nc.sync.dma_start(
+            out=w2s_raw[0 : 2 * QUAD, :].bitcast(I32),
+            in_=w2_scales.rearrange("b q (g c) -> (q g) b c", g=2).bitcast(I32),
+        )
+        deal_wc_words(0)
+        deal_wc_scales(0)
+        deal_wc_words(1)
         gather_words(0, 0)
         gather_words(0, 1)
         load_w1(1, 0)
-        for b in range(2):
-            deal_wc_scales(b)
+        deal_wc_scales(1)
         gather_words(1, 0)
         gather_words(1, 1)
         load_w1(1, 1)
@@ -189,7 +196,6 @@ def tile_list_flow_congestion_routing_kernel(
         ring = [tile([P, S], F32, "h%d" % i) for i in range(H_RING)]
         h = [ring[u % H_RING] for u in range(SLICES)]
         h[3] = tile([P, S], F32, "h3", "w1_bf0")
-        w2_s = tile([P, N], U8, "w2_s", "wc_raw")
         first_flat = [tile([P, 4 * PAIRS + HALF * b], F32, "first%d" % b) for b in range(2)]
         first = [first_flat[b][:, 0 : 4 * PAIRS].rearrange("p (t j) -> p t j", t=4) for b in range(2)]
         second = [tile([P, 4, PAIRS], F32, "second%d" % b) for b in range(2)]
@@ -277,7 +283,7 @@ def tile_list_flow_congestion_routing_kernel(
                     nc.tensor.matmul_mx(
                         out=y_psum(s, g, t),
                         lhsT=w2_w[:, b, cols].bitcast(FP8X4),
-                        lhsT_scale=w2_s[4 * b : P, cols],
+                        lhsT_scale=w2_s[:, g, b, P * t : P * (t + 1)],
                         rhs=z_w[b][:, HALF * s : HALF * (s + 1)].bitcast(FP8X4),
                         rhs_scale=z_s[b][:, HALF * s : HALF * (s + 1)],
                         start=(b == 0 and t % 2 == 0),

@@ -27,9 +27,9 @@ H_RING = 3
 TAB1_AT = 10240
 SCALE_ROW = 24
 PLANE_ROWS = 100
-OWN_DAMP = (0, 4, 5, 6, 7)
-ON_GPSIMD = (4, 5, 6)
-Y_BANKS = (0, 3, 1, 2)
+OWN_DAMP = (0, 3, 4, 5, 6, 7)
+ON_GPSIMD = (3, 4, 5, 7)
+Y_BANKS = (0, 1, 0, 2)
 
 
 def tile_list_flow_congestion_routing_kernel(
@@ -58,10 +58,10 @@ def tile_list_flow_congestion_routing_kernel(
         v_w = [[tile([P, BANK], U32, "v_w%d%d" % (a, s)) for s in range(2)] for a in range(2)]
         v_s_both = tile([P, 2, S], U8, "v_s")
         v_s = [v_s_both[:, a, :] for a in range(2)]
-        wc_raw = tile([P, 2, H // 2], I32, "wc_raw")
+        wc_raw = [tile([P, 2, GROUP // 2], I32, "wc_raw0", "wc_raw"), placed([P, 2, GROUP // 2], I32, "wc_raw1", 8192)]
         wcs_raw = tile([P, 2, H], U8, "wcs_raw")
         wc_w = [tile([P, 2, GROUP], U16, "wc_w%d" % b) for b in range(2)]
-        wc_s_both = placed([P, 2, 2, GROUP], U8, "wc_s", 8192)
+        wc_s_both = tile([P, 2, 2, GROUP], U8, "wc_s")
         wc_s = [wc_s_both[:, b, :, :] for b in range(2)]
         w1_raw = [
             [placed([P, 4, GROUP], F32, "w1_raw00", 0), tile([P, 4, GROUP], F32, "w1_raw01", "wc_raw")],
@@ -91,6 +91,10 @@ def tile_list_flow_congestion_routing_kernel(
         def load_table(a):
             nc.sync.dma_start(out=tab_w[a][:], in_=tab_words[a].rearrange("p t i -> p (t i)").bitcast(I32))
 
+        def load_wc(b):
+            words = wc_words.rearrange("a p c -> p a c")[:, :, 2 * GROUP * b : 2 * GROUP * (b + 1)]
+            nc.sync.dma_start(out=wc_raw[b][:], in_=words.bitcast(I32))
+
         def load_w1(b, a, lo=0, hi=GROUP):
             rows = w1[GROUP * a : GROUP * (a + 1), GROUP * b + lo : GROUP * b + hi]
             nc.sync.dma_start(out=w1_raw[b][a][:, :, lo:hi], in_=rows.rearrange("(p j) c -> p j c", j=4))
@@ -100,7 +104,7 @@ def tile_list_flow_congestion_routing_kernel(
 
         nc.sync.dma_start(offs_sb[:], offs)
         nc.sync.dma_start(out=tab_s[0:QUAD, :].bitcast(I32), in_=tab_scales.rearrange("a q t -> q a t").bitcast(I32))
-        nc.sync.dma_start(out=wc_raw[:], in_=wc_words.rearrange("a p c -> p a c").bitcast(I32))
+        load_wc(0)
         for q in range(4):
             nc.sync.dma_start(
                 out=wcs_raw[QUAD * q : QUAD * q + 4, :, :].bitcast(I32),
@@ -118,16 +122,16 @@ def tile_list_flow_congestion_routing_kernel(
                 in_=picked_s[8 * q : 8 * q + 8, :].bitcast(I32),
             )
         load_table(1)
+        load_wc(1)
 
         def gather_words(a, s):
             entries = offs_sb[:, BANK // 16 * s : BANK // 16 * (s + 1)]
             nc.vector.tensor_copy(v_w[a][s][:], tab_w[a][:].bitcast(U32).indirect(entries))
 
         def deal_wc_words(b):
-            cols = slice(GROUP * b, GROUP * (b + 1))
             nc.vector.tensor_copy(
                 out=wc_w[b][:].rearrange("p a (t m) -> p a m t", t=4),
-                in_=wc_raw[:].bitcast(U16)[:, :, cols].rearrange("p a (m t) -> p a m t", t=4),
+                in_=wc_raw[b][:].bitcast(U16).rearrange("p a (m t) -> p a m t", t=4),
             )
 
         def deal_wc_scales(b):
@@ -176,13 +180,13 @@ def tile_list_flow_congestion_routing_kernel(
         )
         deal_wc_words(0)
         deal_wc_scales(0)
-        deal_wc_words(1)
         gather_words(0, 0)
         gather_words(0, 1)
         load_w1(1, 0)
         deal_wc_scales(1)
         gather_words(1, 0)
         gather_words(1, 1)
+        deal_wc_words(1)
         load_w1(1, 1)
         round_w1(nc.vector.tensor_copy, 0, 0)
         round_w1(nc.vector.tensor_copy, 0, 1, 0, GROUP // 2)
@@ -195,7 +199,7 @@ def tile_list_flow_congestion_routing_kernel(
 
         ring = [tile([P, S], F32, "h%d" % i) for i in range(H_RING)]
         h = [ring[u % H_RING] for u in range(SLICES)]
-        h[3] = tile([P, S], F32, "h3", "w1_bf0")
+        h[2] = tile([P, S], F32, "h2_own", "w1_bf0")
         first_flat = [tile([P, 4 * PAIRS + HALF * b], F32, "first%d" % b) for b in range(2)]
         first = [first_flat[b][:, 0 : 4 * PAIRS].rearrange("p (t j) -> p t j", t=4) for b in range(2)]
         second = [tile([P, 4, PAIRS], F32, "second%d" % b) for b in range(2)]
@@ -210,7 +214,7 @@ def tile_list_flow_congestion_routing_kernel(
                 damp.append([first[b][:, t, :], second[b][:, t, :]])
         z_bf = tile([P, 4 * PAIRS], BF16, "z_bf")
         z_bf_early = first_flat[1][:, 4 * PAIRS - HALF : 4 * PAIRS + HALF].bitcast(BF16)
-        z_w = [tile([P, PAIRS], U32, "z_w0", "load_sb1"), tile([P, PAIRS], U32, "z_w1")]
+        z_w = [tile([P, PAIRS], U32, "z_w0", "damp7"), tile([P, PAIRS], U32, "z_w1")]
         z_s = [tile([P, PAIRS], U8, "z_s%d" % b) for b in range(2)]
 
         def first_product(pair, words, scales, order):
@@ -226,36 +230,62 @@ def tile_list_flow_congestion_routing_kernel(
                         stop=(a == order[1]),
                     )
 
-        def cap_stage(u):
+        def cap_product(u):
             b, t = divmod(u, 4)
             cols = slice(P * t, P * (t + 1))
-            pair = u % 4
-            first_product(pair, lambda a: wc_w[b][:, a, cols].bitcast(FP4X4), lambda a: wc_s[b][:, a, cols], (0, 1))
-            for s in range(2):
-                nc.scalar.activation(out=damp[u][s], in_=banks[2 * pair + s][:], func=ACT.Abs)
-            for s in range(2):
-                nc.scalar.activation(out=damp[u][s], in_=damp[u][s], func=ACT.Abs_reciprocal_sqrt, bias=1.0)
-            for s in range(2):
+            first_product(u % 4, lambda a: wc_w[b][:, a, cols].bitcast(FP4X4), lambda a: wc_s[b][:, a, cols], (0, 1))
+
+        def load_product(u):
+            b, t = divmod(u, 4)
+            cols = slice(P * t, P * (t + 1))
+            first_product(
+                (u - 1) % 4, lambda a: w1_w[b][a][:, cols].bitcast(FP8X4), lambda a: w1_s[b][a][:, cols], (1, 0)
+            )
+
+        def magnitude(u, s):
+            nc.scalar.activation(out=damp[u][s], in_=banks[2 * (u % 4) + s][:], func=ACT.Abs)
+
+        def inverse_root(u, s):
+            nc.scalar.activation(out=damp[u][s], in_=damp[u][s], func=ACT.Abs_reciprocal_sqrt, bias=1.0)
+
+        def square(u, s):
+            if u == 6:
+                nc.gpsimd.tensor_tensor(out=damp[u][s], in0=damp[u][s], in1=damp[u][s], op=ALU.mult)
+            else:
                 nc.scalar.activation(out=damp[u][s], in_=damp[u][s], func=ACT.Square)
 
+        def cap_stage(u):
+            cap_product(u)
+            for step in (magnitude, inverse_root, square):
+                for s in range(2):
+                    step(u, s)
+
         def load_stage(u):
-            b, t = divmod(u, 4)
-            cols = slice(P * t, P * (t + 1))
-            pair = (u - 1) % 4
-            first_product(pair, lambda a: w1_w[b][a][:, cols].bitcast(FP8X4), lambda a: w1_s[b][a][:, cols], (1, 0))
+            load_product(u)
             for s in range(2):
-                if u in ON_GPSIMD:
-                    nc.scalar.copy(out=load_sb[2 * (u % 2) + s][:], in_=banks[2 * pair + s][:])
-                    nc.gpsimd.tensor_tensor(
-                        out=h[u][:, BANK * s : BANK * (s + 1)], in0=load_sb[2 * (u % 2) + s][:], in1=damp[u][s], op=ALU.mult
-                    )
-                else:
-                    nc.vector.tensor_tensor(
-                        out=h[u][:, BANK * s : BANK * (s + 1)],
-                        in0=banks[2 * pair + s][:],
-                        in1=damp[u][s],
-                        op=ALU.mult,
-                    )
+                nc.vector.tensor_tensor(
+                    out=h[u][:, BANK * s : BANK * (s + 1)],
+                    in0=banks[2 * ((u - 1) % 4) + s][:],
+                    in1=damp[u][s],
+                    op=ALU.mult,
+                )
+
+        def gpsimd_slice(u):
+            def copy_load(u, s):
+                nc.scalar.copy(out=load_sb[2 * (ON_GPSIMD.index(u) % 2) + s][:], in_=banks[2 * ((u - 1) % 4) + s][:])
+
+            def product(u, s):
+                nc.gpsimd.tensor_tensor(
+                    out=h[u][:, BANK * s : BANK * (s + 1)], in0=load_sb[2 * (ON_GPSIMD.index(u) % 2) + s][:], in1=damp[u][s], op=ALU.mult
+                )
+
+            cap_product(u)
+            load_product(u)
+            for step, s in (
+                (magnitude, 0), (copy_load, 0), (inverse_root, 0), (magnitude, 1), (square, 0), (product, 0),
+                (inverse_root, 1), (copy_load, 1), (square, 1), (product, 1),
+            ):
+                step(u, s)
 
         def pick(u, lo=0, hi=PAIRS):
             b, t = divmod(u, 4)
@@ -276,8 +306,8 @@ def tile_list_flow_congestion_routing_kernel(
         def y_psum(s, g, t):
             return banks[2 * Y_BANKS[2 * s + g] + t // 2][:, HALF * (t % 2) : HALF * (t % 2 + 1)]
 
-        def y_passes(b, s):
-            for g in range(2):
+        def y_passes(b, s, groups=(0, 1)):
+            for g in groups:
                 for t in range(4):
                     cols = slice(GROUP * g + P * t, GROUP * g + P * (t + 1))
                     nc.tensor.matmul_mx(
@@ -293,12 +323,13 @@ def tile_list_flow_congestion_routing_kernel(
         for u in range(AHEAD):
             cap_stage(u)
         for u in range(SLICES):
-            load_stage(u)
-            if u < 2:
-                cap_stage(u + AHEAD)
             if u in ON_GPSIMD:
-                cap_stage(u + 1)
-            if u == 0:
+                gpsimd_slice(u)
+            else:
+                if u >= AHEAD:
+                    cap_stage(u)
+                load_stage(u)
+            if u == 1:
                 for a in range(2):
                     for lo in range(0, P, P // 4):
                         gpsimd_round(
@@ -308,6 +339,8 @@ def tile_list_flow_congestion_routing_kernel(
                     quantize_w1(1, a)
                 load_w2()
                 nc.sync.dma_start(out=bias[:], in_=b2.rearrange("(g p t) -> p g t", g=2, t=4))
+            if u == SLICES - 1:
+                quantize_z(0, slice(0, PAIRS), z_bf[:])
             if u not in OWN_DAMP:
                 pick(u - 1)
             if u + 1 in OWN_DAMP:
@@ -317,8 +350,6 @@ def tile_list_flow_congestion_routing_kernel(
             if u == 2:
                 deal_w2_words()
                 deal_w2_scales()
-            if u == SLICES - 2:
-                quantize_z(0, slice(0, PAIRS), z_bf[:])
 
         y = [[tile([P, 4, HALF], F32, "y%d%d" % (s, g)) for g in range(2)] for s in range(2)]
         y_bf = [[tile([P, 4 * HALF], BF16, "y_bf%d%d" % (s, g)) for g in range(2)] for s in range(2)]
@@ -347,15 +378,17 @@ def tile_list_flow_congestion_routing_kernel(
             for t in (0, 2):
                 nc.sync.dma_start(out=rows[:, t : t + 2, :], in_=y[s][g][:, t : t + 2, :])
 
-        for s in range(2):
-            y_passes(0, s)
+        y_passes(0, 0)
         for s, rounded in enumerate((z_bf_early, z_bf[:, 0 : 4 * HALF])):
             pick(SLICES - 1, HALF * s, HALF * (s + 1))
             maximum(1, slice(HALF * s, HALF * (s + 1)), rounded)
             quantize_z(1, slice(HALF * s, HALF * (s + 1)), rounded)
-            y_passes(1, s)
-        finish(0, 0, [nc.vector.tensor_copy])
-        finish(0, 1, [nc.vector.tensor_copy])
+            if s == 0:
+                y_passes(1, 0)
+        for g in range(2):
+            finish(0, g, [nc.vector.tensor_copy])
+            for b in range(2):
+                y_passes(b, 1, (g,))
         finish(1, 0, [nc.vector.tensor_copy])
         finish(1, 1, [nc.vector.tensor_copy, nc.scalar.copy])
         for g in range(2):

@@ -23,13 +23,14 @@ BANK = 512
 HALF = PAIRS // 2
 SLICES = H // P
 AHEAD = 3
-H_RING = 3
+H_RING = 4
 TAB1_AT = 10240
 SCALE_ROW = 24
 PLANE_ROWS = 100
-OWN_DAMP = (0, 3, 4, 5, 6, 7)
+OWN_DAMP = (0, 2, 3, 4, 5, 6, 7)
 ON_GPSIMD = (3, 4, 5, 7)
-Y_BANKS = (0, 1, 0, 2)
+DEFERRED = 2
+Y_BANKS = (0, 1, 3, 2)
 
 
 def tile_list_flow_congestion_routing_kernel(
@@ -199,10 +200,10 @@ def tile_list_flow_congestion_routing_kernel(
 
         ring = [tile([P, S], F32, "h%d" % i) for i in range(H_RING)]
         h = [ring[u % H_RING] for u in range(SLICES)]
-        h[2] = tile([P, S], F32, "h2_own", "w1_bf0")
-        first_flat = [tile([P, 4 * PAIRS + HALF * b], F32, "first%d" % b) for b in range(2)]
-        first = [first_flat[b][:, 0 : 4 * PAIRS].rearrange("p (t j) -> p t j", t=4) for b in range(2)]
-        second = [tile([P, 4, PAIRS], F32, "second%d" % b) for b in range(2)]
+        picked0_flat = [tile([P, 4 * PAIRS], F32, "picked0%d" % i) for i in range(2)]
+        picked0 = [picked0_flat[i][:].rearrange("p (t j) -> p t j", t=4) for i in range(2)]
+        w1_bf[1][1] = picked0_flat[0][:, PAIRS : 3 * PAIRS].bitcast(BF16)
+        picked1 = [tile([P, 8 - DEFERRED, HALF], F32, "picked1%d" % i) for i in range(2)]
         load_sb = [tile([P, BANK], F32, "load_sb%d" % s) for s in range(4)]
         damp = []
         for u in range(SLICES):
@@ -210,12 +211,14 @@ def tile_list_flow_congestion_routing_kernel(
                 own = tile([P, S], F32, "damp%d" % u)
                 damp.append([own[:, BANK * s : BANK * (s + 1)] for s in range(2)])
             else:
-                b, t = divmod(u - 1, 4)
-                damp.append([first[b][:, t, :], second[b][:, t, :]])
+                damp.append([picked0[i][:, u - 1, :] for i in range(2)])
         z_bf = tile([P, 4 * PAIRS], BF16, "z_bf")
-        z_bf_early = first_flat[1][:, 4 * PAIRS - HALF : 4 * PAIRS + HALF].bitcast(BF16)
-        z_w = [tile([P, PAIRS], U32, "z_w0", "damp7"), tile([P, PAIRS], U32, "z_w1")]
-        z_s = [tile([P, PAIRS], U8, "z_s%d" % b) for b in range(2)]
+        z_bf_early = tile([P, 4 * HALF], BF16, "z_bf_early")
+        z_w = [
+            [tile([P, HALF], U32, "z_w00", "damp7"), tile([P, HALF], U32, "z_w01", "h2")],
+            [tile([P, HALF], U32, "z_w1%d" % s) for s in range(2)],
+        ]
+        z_s = [[tile([P, HALF], U8, "z_s%d%d" % (b, s)) for s in range(2)] for b in range(2)]
 
         def first_product(pair, words, scales, order):
             for s in range(2):
@@ -281,27 +284,33 @@ def tile_list_flow_congestion_routing_kernel(
 
             cap_product(u)
             load_product(u)
-            for step, s in (
-                (magnitude, 0), (copy_load, 0), (inverse_root, 0), (magnitude, 1), (square, 0), (product, 0),
-                (inverse_root, 1), (copy_load, 1), (square, 1), (product, 1),
-            ):
-                step(u, s)
+            for step in (magnitude, inverse_root):
+                for s in range(2):
+                    step(u, s)
+            for s in range(2):
+                for step in (square, copy_load, product):
+                    step(u, s)
 
-        def pick(u, lo=0, hi=PAIRS):
-            b, t = divmod(u, 4)
-            for picked, pos in ((first, pos1_sb), (second, pos2_sb)):
-                nc.vector.tensor_copy(picked[b][:, t, lo:hi], h[u][:].indirect(pos[:, lo // 16 : hi // 16]))
+        def pick(u):
+            for i, pos in enumerate((pos1_sb, pos2_sb)):
+                nc.vector.tensor_copy(picked0[i][:, u, :], h[u][:].indirect(pos[:]))
 
-        def maximum(b, cols, rounded):
+        def pick_half(u, s):
+            slot = u - 4 + (4 - DEFERRED) * (1 - s)
+            for i, pos in enumerate((pos1_sb, pos2_sb)):
+                entries = pos[:, HALF // 16 * s : HALF // 16 * (s + 1)]
+                nc.vector.tensor_copy(picked1[i][:, slot, :], h[u][:].indirect(entries))
+
+        def maximum(picked, rounded):
             nc.vector.tensor_tensor(
                 out=rounded.rearrange("p (c i t) -> p c t i", t=4, i=4),
-                in0=first[b][:, :, cols].rearrange("p t (c i) -> p c t i", i=4),
-                in1=second[b][:, :, cols].rearrange("p t (c i) -> p c t i", i=4),
+                in0=picked[0].rearrange("p t (c i) -> p c t i", i=4),
+                in1=picked[1].rearrange("p t (c i) -> p c t i", i=4),
                 op=ALU.max,
             )
 
-        def quantize_z(b, cols, rounded):
-            nc.vector.quantize_mx(out=z_w[b][:, cols].bitcast(FP8X4), scales=z_s[b][:, cols], in_=rounded)
+        def quantize_z(b, s, rounded):
+            nc.vector.quantize_mx(out=z_w[b][s][:].bitcast(FP8X4), scales=z_s[b][s][:], in_=rounded)
 
         def y_psum(s, g, t):
             return banks[2 * Y_BANKS[2 * s + g] + t // 2][:, HALF * (t % 2) : HALF * (t % 2 + 1)]
@@ -314,8 +323,8 @@ def tile_list_flow_congestion_routing_kernel(
                         out=y_psum(s, g, t),
                         lhsT=w2_w[:, b, cols].bitcast(FP8X4),
                         lhsT_scale=w2_s[:, g, b, P * t : P * (t + 1)],
-                        rhs=z_w[b][:, HALF * s : HALF * (s + 1)].bitcast(FP8X4),
-                        rhs_scale=z_s[b][:, HALF * s : HALF * (s + 1)],
+                        rhs=z_w[b][s][:].bitcast(FP8X4),
+                        rhs_scale=z_s[b][s][:],
                         start=(b == 0 and t % 2 == 0),
                         stop=(b == 1 and t % 2 == 1),
                     )
@@ -340,20 +349,24 @@ def tile_list_flow_congestion_routing_kernel(
                 load_w2()
                 nc.sync.dma_start(out=bias[:], in_=b2.rearrange("(g p t) -> p g t", g=2, t=4))
             if u == SLICES - 1:
-                quantize_z(0, slice(0, PAIRS), z_bf[:])
+                quantize_z(0, 0, z_bf[:, 0 : 4 * HALF])
             if u not in OWN_DAMP:
                 pick(u - 1)
-            if u + 1 in OWN_DAMP:
+            if u < 4 and u + 1 in OWN_DAMP:
                 pick(u)
+            if u >= 4:
+                pick_half(u, 0)
+                if u < SLICES - DEFERRED:
+                    pick_half(u, 1)
             if u == 3:
-                maximum(0, slice(0, PAIRS), z_bf[:])
+                maximum(picked0, z_bf[:])
             if u == 2:
                 deal_w2_words()
                 deal_w2_scales()
 
         y = [[tile([P, 4, HALF], F32, "y%d%d" % (s, g)) for g in range(2)] for s in range(2)]
-        y_bf = [[tile([P, 4 * HALF], BF16, "y_bf%d%d" % (s, g)) for g in range(2)] for s in range(2)]
-        y_w = [tile([P, PAIRS], I32, "y_w%d" % g) for g in range(2)]
+        y_bf = [[tile([P, 4 * HALF], BF16, "y_bf%d%d" % (s, g), "z_bf" if (s, g) == (0, 1) else None) for g in range(2)] for s in range(2)]
+        y_w = [tile([P, 2, HALF], I32, "y_w%d" % s) for s in range(2)]
         y_s = tile([P, 2, PAIRS], U8, "y_s")
 
         def finish(s, g, round_copies):
@@ -373,26 +386,32 @@ def tile_list_flow_congestion_routing_kernel(
                     in_=y[s][g][:, :, lo : lo + width].rearrange("p t (c i) -> p c t i", i=4),
                 )
                 cols = slice(HALF * s + lo, HALF * s + lo + width)
-                nc.vector.quantize_mx(out=y_w[g][:, cols].bitcast(FP8X4), scales=y_s[:, g, cols], in_=rounded)
+                nc.vector.quantize_mx(out=y_w[s][:, g, lo : lo + width].bitcast(FP8X4), scales=y_s[:, g, cols], in_=rounded)
             rows = out_0[GROUP * g : GROUP * (g + 1), HALF * s : HALF * (s + 1)].rearrange("(p t) j -> p t j", t=4)
             for t in (0, 2):
                 nc.sync.dma_start(out=rows[:, t : t + 2, :], in_=y[s][g][:, t : t + 2, :])
 
+        def store_codes(s):
+            words = out_1.rearrange("g p m t -> p g (m t)").bitcast(I32)
+            nc.sync.dma_start(out=words[:, :, HALF * s : HALF * (s + 1)], in_=y_w[s][:])
+
         y_passes(0, 0)
-        for s, rounded in enumerate((z_bf_early, z_bf[:, 0 : 4 * HALF])):
-            pick(SLICES - 1, HALF * s, HALF * (s + 1))
-            maximum(1, slice(HALF * s, HALF * (s + 1)), rounded)
-            quantize_z(1, slice(HALF * s, HALF * (s + 1)), rounded)
-            if s == 0:
-                y_passes(1, 0)
-        for g in range(2):
-            finish(0, g, [nc.vector.tensor_copy])
-            for b in range(2):
-                y_passes(b, 1, (g,))
+        maximum([picked1[i][:, 4 - DEFERRED : 8 - DEFERRED, :] for i in range(2)], z_bf_early[:])
+        quantize_z(1, 0, z_bf_early[:])
+        y_passes(1, 0)
+        pick_half(SLICES - 2, 1)
+        quantize_z(0, 1, z_bf[:, 4 * HALF : 8 * HALF])
+        y_passes(0, 1)
+        pick_half(SLICES - 1, 1)
+        maximum([picked1[i][:, 0:4, :] for i in range(2)], z_bf[:, 0 : 4 * HALF])
+        quantize_z(1, 1, z_bf[:, 0 : 4 * HALF])
+        finish(0, 0, [nc.scalar.copy])
+        finish(0, 1, [nc.vector.tensor_copy])
+        store_codes(0)
+        y_passes(1, 1)
         finish(1, 0, [nc.vector.tensor_copy])
         finish(1, 1, [nc.vector.tensor_copy, nc.scalar.copy])
-        for g in range(2):
-            nc.sync.dma_start(out=out_1[g].rearrange("p m t -> p (m t)").bitcast(I32), in_=y_w[g][:])
+        store_codes(1)
         for q in range(4):
             queue = nc.sync if q % 2 == 0 else nc.scalar
             queue.dma_start(

@@ -28,7 +28,7 @@ TAB1_AT = 10240
 SCALE_ROW = 24
 PLANE_ROWS = 100
 OWN_DAMP = (0, 2, 3, 4, 5, 6, 7)
-ON_GPSIMD = (3, 4, 5, 7)
+ON_GPSIMD = (4, 5, 7)
 DEFERRED = 2
 Y_BANKS = (0, 1, 3, 2)
 
@@ -252,10 +252,7 @@ def tile_list_flow_congestion_routing_kernel(
             nc.scalar.activation(out=damp[u][s], in_=damp[u][s], func=ACT.Abs_reciprocal_sqrt, bias=1.0)
 
         def square(u, s):
-            if u == 6:
-                nc.gpsimd.tensor_tensor(out=damp[u][s], in0=damp[u][s], in1=damp[u][s], op=ALU.mult)
-            else:
-                nc.scalar.activation(out=damp[u][s], in_=damp[u][s], func=ACT.Square)
+            nc.scalar.activation(out=damp[u][s], in_=damp[u][s], func=ACT.Square)
 
         def cap_stage(u):
             cap_product(u)

@@ -70,13 +70,16 @@ def tile_list_flow_congestion_routing_kernel(
         ]
         w1_bf = [[tile([P, 4 * GROUP], BF16, "w1_bf%d" % a) for a in range(2)]]
         w1_bf.append(w1_bf[0][::-1])
-        w1_w = [[tile([P, GROUP], U32, "w1_w%d%d" % (b, a)) for a in range(2)] for b in range(2)]
+        w1_w = [
+            [tile([P, GROUP], U32, "w1_w0%d" % a) for a in range(2)],
+            [placed([P, GROUP], U32, "w1_w10", TAB1_AT), tile([P, GROUP], U32, "w1_w11")],
+        ]
         w1_s = [[tile([P, GROUP], U8, "w1_s%d%d" % (b, a)) for a in range(2)] for b in range(2)]
         w2_raw = tile([P, 2, N], I32, "w2_raw", "wc_raw")
         w2s_raw = tile([P, GROUP], U8, "w2s_raw")
         w2s_dealt = tile([P, GROUP], U8, "w2s_dealt")
         w2_s = tile([P, 2, 2, GROUP], U8, "w2_s")
-        w2_w = placed([P, 2, N], I32, "w2_w", TAB1_AT)
+        w2_w = placed([P, 2, N], I32, "w2_w", TAB1_AT + 4 * GROUP)
         bias = placed([P, 2, 4], F32, "bias", 0)
 
         warm = tile([P, 2], F32, "warm")
@@ -212,7 +215,7 @@ def tile_list_flow_congestion_routing_kernel(
                 damp.append([own[:, BANK * s : BANK * (s + 1)] for s in range(2)])
             else:
                 damp.append([picked0[i][:, u - 1, :] for i in range(2)])
-        z_bf = tile([P, 4 * PAIRS], BF16, "z_bf")
+        z_bf = tile([P, 4 * PAIRS], BF16, "z_bf", "damp5")
         z_bf_early = tile([P, 4 * HALF], BF16, "z_bf_early")
         z_w = [
             [tile([P, HALF], U32, "z_w00", "damp7"), tile([P, HALF], U32, "z_w01", "h2")],
@@ -342,6 +345,7 @@ def tile_list_flow_congestion_routing_kernel(
                             out=w1_bf[1][a][:].rearrange("p (t m j) -> p m t j", t=4, j=4)[:, lo : lo + P // 4, :, :],
                             in_=w1_raw[1][a][:].rearrange("p j (m t) -> p m t j", t=4)[:, lo : lo + P // 4, :, :],
                         )
+                for a in range(2):
                     quantize_w1(1, a)
                 load_w2()
                 nc.sync.dma_start(out=bias[:], in_=b2.rearrange("(g p t) -> p g t", g=2, t=4))
@@ -351,18 +355,18 @@ def tile_list_flow_congestion_routing_kernel(
                 pick(u - 1)
             if u < 4 and u + 1 in OWN_DAMP:
                 pick(u)
+            if u == 5:
+                maximum(picked0, z_bf[:])
             if u >= 4:
                 pick_half(u, 0)
                 if u < SLICES - DEFERRED:
                     pick_half(u, 1)
-            if u == 3:
-                maximum(picked0, z_bf[:])
             if u == 2:
                 deal_w2_words()
                 deal_w2_scales()
 
         y = [[tile([P, 4, HALF], F32, "y%d%d" % (s, g)) for g in range(2)] for s in range(2)]
-        y_bf = [[tile([P, 4 * HALF], BF16, "y_bf%d%d" % (s, g), "z_bf" if (s, g) == (0, 1) else None) for g in range(2)] for s in range(2)]
+        y_bf = [[tile([P, 4 * HALF], BF16, "y_bf%d%d" % (s, g), "damp5" if (s, g) == (0, 1) else None) for g in range(2)] for s in range(2)]
         y_w = [tile([P, 2, HALF], I32, "y_w%d" % s) for s in range(2)]
         y_s = tile([P, 2, PAIRS], U8, "y_s")
 

@@ -18,19 +18,22 @@ ALU = mybir.AluOpType
 
 P = 128
 QUAD = 32
+LINE = 16
 GROUP = 512
 BANK = 512
 HALF = PAIRS // 2
 SLICES = H // P
 AHEAD = 3
 H_RING = 4
-TAB1_AT = 10240
-SCALE_ROW = 24
-PLANE_ROWS = 100
-OWN_DAMP = (0, 2, 3, 4, 5, 6, 7)
+QUADRANTS = (0, 2, 1, 3)
 ON_GPSIMD = (4, 5, 7)
 DEFERRED = 2
+ROUND_PIECES = 4
 Y_BANKS = (0, 1, 3, 2)
+W1_FIRST_AT = 0
+WC_SECOND_AT = W1_FIRST_AT + 4 * 4 * GROUP
+TAB_SECOND_AT = WC_SECOND_AT + 4 * GROUP
+TAB_SCALES_AT = WC_SECOND_AT - 2 * GROUP
 
 
 def tile_list_flow_congestion_routing_kernel(
@@ -53,34 +56,34 @@ def tile_list_flow_congestion_routing_kernel(
         pos2_sb = sb.tile([P, PAIRS // 16], U16, name="pos2_sb")
         banks = [ps.tile([P, BANK], F32, name="bank%d" % i) for i in range(8)]
 
-        tab_s = placed([P, T], U8, "tab_s", 7168)
-        tab_w = [tile([P, T], I32, "tab_w0", "stage1"), placed([P, T], I32, "tab_w1", TAB1_AT)]
+        tab_s = placed([P, T], U8, "tab_s", TAB_SCALES_AT)
+        tab_w = [tile([P, T], I32, "tab_w0", "stage1"), placed([P, T], I32, "tab_w1", TAB_SECOND_AT)]
         picked_s = tile([P, S], U8, "picked_s")
         v_w = [[tile([P, BANK], U32, "v_w%d%d" % (a, s)) for s in range(2)] for a in range(2)]
-        v_s_both = tile([P, 2, S], U8, "v_s")
-        v_s = [v_s_both[:, a, :] for a in range(2)]
-        wc_raw = [tile([P, 2, GROUP // 2], I32, "wc_raw0", "wc_raw"), placed([P, 2, GROUP // 2], I32, "wc_raw1", 8192)]
+        v_s = tile([P, 2, S], U8, "v_s")
+        wc_raw = [
+            tile([P, 2, GROUP // 2], I32, "wc_raw0", "wc_raw"),
+            placed([P, 2, GROUP // 2], I32, "wc_raw1", WC_SECOND_AT),
+        ]
         wcs_raw = tile([P, 2, H], U8, "wcs_raw")
         wc_w = [tile([P, 2, GROUP], U16, "wc_w%d" % b) for b in range(2)]
-        wc_s_both = tile([P, 2, 2, GROUP], U8, "wc_s")
-        wc_s = [wc_s_both[:, b, :, :] for b in range(2)]
+        wc_s = tile([P, 2, 2, GROUP], U8, "wc_s")
         w1_raw = [
-            [placed([P, 4, GROUP], F32, "w1_raw00", 0), tile([P, 4, GROUP], F32, "w1_raw01", "wc_raw")],
-            [tile([P, 4, GROUP], F32, "w1_raw10", "stage1"), placed([P, 4, GROUP], F32, "w1_raw11", TAB1_AT)],
+            [placed([P, 4, GROUP], F32, "w1_raw00", W1_FIRST_AT), tile([P, 4, GROUP], F32, "w1_raw01", "wc_raw")],
+            [tile([P, 4, GROUP], F32, "w1_raw10", "stage1"), placed([P, 4, GROUP], F32, "w1_raw11", TAB_SECOND_AT)],
         ]
-        w1_bf = [[tile([P, 4 * GROUP], BF16, "w1_bf%d" % a) for a in range(2)]]
-        w1_bf.append(w1_bf[0][::-1])
+        w1_bf0 = [tile([P, 4 * GROUP], BF16, "w1_bf%d" % a) for a in range(2)]
         w1_w = [
             [tile([P, GROUP], U32, "w1_w0%d" % a) for a in range(2)],
-            [placed([P, GROUP], U32, "w1_w10", TAB1_AT), tile([P, GROUP], U32, "w1_w11")],
+            [placed([P, GROUP], U32, "w1_w10", TAB_SECOND_AT), tile([P, GROUP], U32, "w1_w11")],
         ]
         w1_s = [[tile([P, GROUP], U8, "w1_s%d%d" % (b, a)) for a in range(2)] for b in range(2)]
         w2_raw = tile([P, 2, N], I32, "w2_raw", "wc_raw")
         w2s_raw = tile([P, GROUP], U8, "w2s_raw")
-        w2s_dealt = tile([P, GROUP], U8, "w2s_dealt")
-        w2_s = tile([P, 2, 2, GROUP], U8, "w2_s")
-        w2_w = placed([P, 2, N], I32, "w2_w", TAB1_AT + 4 * GROUP)
-        bias = placed([P, 2, 4], F32, "bias", 0)
+        w2s_dealt = placed([P, GROUP], U8, "w2s_dealt", W1_FIRST_AT + 64)
+        w2_s = wcs_raw[:].rearrange("p g (b c) -> p g b c", b=2)
+        w2_w = placed([P, 2, N], I32, "w2_w", TAB_SECOND_AT + 4 * GROUP)
+        bias = placed([P, 2, 4], F32, "bias", W1_FIRST_AT)
 
         warm = tile([P, 2], F32, "warm")
         nc.vector.memset(warm[:, 0:1], 0.0)
@@ -88,9 +91,8 @@ def tile_list_flow_congestion_routing_kernel(
         nc.gpsimd.memset(wcs_raw[:].bitcast(I32), 0)
         nc.vector.memset(tab_s[QUAD : 2 * QUAD, :].bitcast(I32), 0)
         nc.vector.memset(tab_s[2 * QUAD : P, :].bitcast(I32), 0)
-        nc.gpsimd.memset(v_s_both[:].bitcast(I32), 0)
+        nc.gpsimd.memset(v_s[:].bitcast(I32), 0)
         nc.gpsimd.memset(w2s_raw[2 * QUAD : P, :].bitcast(I32), 0)
-        nc.gpsimd.memset(w2_s[:].bitcast(I32), 0)
 
         def load_table(a):
             nc.sync.dma_start(out=tab_w[a][:], in_=tab_words[a].rearrange("p t i -> p (t i)").bitcast(I32))
@@ -103,27 +105,22 @@ def tile_list_flow_congestion_routing_kernel(
             rows = w1[GROUP * a : GROUP * (a + 1), GROUP * b + lo : GROUP * b + hi]
             nc.sync.dma_start(out=w1_raw[b][a][:, :, lo:hi], in_=rows.rearrange("(p j) c -> p j c", j=4))
 
-        def load_w2():
-            nc.sync.dma_start(out=w2_raw[:], in_=w2_words.rearrange("b p n i -> p b (n i)").bitcast(I32))
-
         nc.sync.dma_start(offs_sb[:], offs)
         nc.sync.dma_start(out=tab_s[0:QUAD, :].bitcast(I32), in_=tab_scales.rearrange("a q t -> q a t").bitcast(I32))
         load_wc(0)
-        for q in range(4):
+        for q in QUADRANTS:
             nc.sync.dma_start(
                 out=wcs_raw[QUAD * q : QUAD * q + 4, :, :].bitcast(I32),
                 in_=wc_scales[:, 4 * q : 4 * q + 4, :].rearrange("a r c -> r a c").bitcast(I32),
             )
-
         load_table(0)
         nc.sync.dma_start(pos1_sb[:], pos1)
         nc.sync.dma_start(pos2_sb[:], pos2)
 
         nc.vector.tensor_copy(picked_s[:], tab_s[:].indirect(offs_sb[:]))
-        for q in range(4):
+        for q in QUADRANTS:
             nc.sync.dma_start(
-                out=v_s_both[QUAD * q : QUAD * q + 4, :, :].bitcast(I32),
-                in_=picked_s[8 * q : 8 * q + 8, :].bitcast(I32),
+                out=v_s[QUAD * q : QUAD * q + 4, :, :].bitcast(I32), in_=picked_s[8 * q : 8 * q + 8, :].bitcast(I32)
             )
         load_table(1)
         load_wc(1)
@@ -134,46 +131,46 @@ def tile_list_flow_congestion_routing_kernel(
 
         def deal_wc_words(b):
             nc.vector.tensor_copy(
-                out=wc_w[b][:].rearrange("p a (t m) -> p a m t", t=4),
-                in_=wc_raw[b][:].bitcast(U16).rearrange("p a (m t) -> p a m t", t=4),
+                out=wc_w[b][:].rearrange("p a (t c i) -> p a c t i", t=4, i=LINE // 2),
+                in_=wc_raw[b][:].bitcast(U16).rearrange("p a (c i t) -> p a c t i", t=4, i=LINE // 2),
             )
 
         def deal_wc_scales(b):
-            cols = slice(GROUP * b, GROUP * (b + 1))
             nc.vector.tensor_copy(
-                out=wc_s[b].rearrange("p a (t m) -> p a m t", t=4),
-                in_=wcs_raw[:, :, cols].rearrange("p a (m t) -> p a m t", t=4),
-            )
-
-        def round_w1(copy, b, a, lo=0, hi=GROUP):
-            copy(
-                out=w1_bf[b][a][:].rearrange("p (t m j) -> p m j t", t=4, j=4)[:, lo // 4 : hi // 4, :, :],
-                in_=w1_raw[b][a][:, :, lo:hi].rearrange("p j (m t) -> p m j t", t=4),
-            )
-
-        def gpsimd_round(out, in_):
-            nc.gpsimd.tensor_scalar(out=out, in0=in_, scalar1=1.0, scalar2=0.0, op0=ALU.mult, op1=ALU.add)
-
-        def quantize_w1(b, a, lo=0, hi=GROUP):
-            nc.vector.quantize_mx(
-                out=w1_w[b][a][:, lo:hi].bitcast(FP8X4), scales=w1_s[b][a][:, lo:hi], in_=w1_bf[b][a][:, 4 * lo : 4 * hi]
+                out=wc_s[:, b, :, :].rearrange("p a (t c i) -> p a c t i", t=4, i=LINE),
+                in_=wcs_raw[:, :, GROUP * b : GROUP * (b + 1)].rearrange("p a (c i t) -> p a c t i", t=4, i=LINE),
             )
 
         def deal_w2_words():
             nc.vector.tensor_copy(
-                out=w2_w[:].rearrange("p b (g t m) -> p (b g) m t", g=2, t=4),
-                in_=w2_raw[:].rearrange("p b (g m t) -> p (b g) m t", g=2, t=4),
+                out=w2_w[:].rearrange("p b (g t c i) -> p (b g) c t i", g=2, t=4, i=LINE // 4),
+                in_=w2_raw[:].rearrange("p b (g c i t) -> p (b g) c t i", g=2, t=4, i=LINE // 4),
             )
 
         def deal_w2_scales():
             nc.vector.tensor_copy(
-                out=w2s_dealt[:].rearrange("p (t m) -> p m t", t=4), in_=w2s_raw[:].rearrange("p (m t) -> p m t", t=4)
+                out=w2s_dealt[:].rearrange("p (t c i) -> p c t i", t=4, i=LINE),
+                in_=w2s_raw[:].rearrange("p (c i t) -> p c t i", t=4, i=LINE),
             )
-            for q in range(4):
+            for q in QUADRANTS:
                 nc.sync.dma_start(
                     out=w2_s[QUAD * q : QUAD * q + 4, :, :, :].rearrange("r g b c -> r (g b c)").bitcast(I32),
                     in_=w2s_dealt[16 * q : 16 * q + 16, :].bitcast(I32),
                 )
+
+        def round_w1(copy, rounded, raw, lo, hi):
+            copy(
+                out=rounded.rearrange("p (t m j) -> p m t j", t=4, j=4)[:, lo // 4 : hi // 4, :, :],
+                in_=raw[:, :, lo:hi].rearrange("p j (m t) -> p m t j", t=4),
+            )
+
+        def gpsimd_copy(out, in_):
+            nc.gpsimd.tensor_scalar(out=out, in0=in_, scalar1=1.0, scalar2=0.0, op0=ALU.mult, op1=ALU.add)
+
+        def quantize_w1(b, a, rounded, lo, hi):
+            nc.vector.quantize_mx(
+                out=w1_w[b][a][:, lo:hi].bitcast(FP8X4), scales=w1_s[b][a][:, lo:hi], in_=rounded[:, 4 * lo : 4 * hi]
+            )
 
         load_w1(0, 0)
         load_w1(0, 1, 0, GROUP // 2)
@@ -192,46 +189,52 @@ def tile_list_flow_congestion_routing_kernel(
         gather_words(1, 1)
         deal_wc_words(1)
         load_w1(1, 1)
-        round_w1(nc.vector.tensor_copy, 0, 0)
-        round_w1(nc.vector.tensor_copy, 0, 1, 0, GROUP // 2)
-        quantize_w1(0, 0, 0, P)
-        round_w1(nc.vector.tensor_copy, 0, 1, GROUP // 2, GROUP)
-        quantize_w1(0, 1, 0, P)
+        round_w1(nc.vector.tensor_copy, w1_bf0[0][:], w1_raw[0][0], 0, GROUP)
+        round_w1(nc.vector.tensor_copy, w1_bf0[1][:], w1_raw[0][1], 0, GROUP // 2)
+        quantize_w1(0, 0, w1_bf0[0], 0, P)
+        round_w1(nc.vector.tensor_copy, w1_bf0[1][:], w1_raw[0][1], GROUP // 2, GROUP)
+        quantize_w1(0, 1, w1_bf0[1], 0, P)
         for lo, hi in ((P, 2 * P), (2 * P, GROUP)):
             for a in range(2):
-                quantize_w1(0, a, lo, hi)
+                quantize_w1(0, a, w1_bf0[a], lo, hi)
 
         ring = [tile([P, S], F32, "h%d" % i) for i in range(H_RING)]
         h = [ring[u % H_RING] for u in range(SLICES)]
         picked0_flat = [tile([P, 4 * PAIRS], F32, "picked0%d" % i) for i in range(2)]
         picked0 = [picked0_flat[i][:].rearrange("p (t j) -> p t j", t=4) for i in range(2)]
-        w1_bf[1][1] = picked0_flat[0][:, PAIRS : 3 * PAIRS].bitcast(BF16)
+        w1_bf1 = [w1_bf0[1][:], picked0_flat[0][:, PAIRS : 3 * PAIRS].bitcast(BF16)]
         picked1 = [tile([P, 8 - DEFERRED, HALF], F32, "picked1%d" % i) for i in range(2)]
-        load_sb = [tile([P, BANK], F32, "load_sb%d" % s) for s in range(4)]
+        load_sb = [tile([P, BANK], F32, "load_sb%d" % i) for i in range(4)]
         damp = []
         for u in range(SLICES):
-            if u in OWN_DAMP:
+            if u == 1:
+                damp.append([picked0[i][:, 0, :] for i in range(2)])
+            else:
                 own = tile([P, S], F32, "damp%d" % u)
                 damp.append([own[:, BANK * s : BANK * (s + 1)] for s in range(2)])
-            else:
-                damp.append([picked0[i][:, u - 1, :] for i in range(2)])
         z_bf = tile([P, 4 * PAIRS], BF16, "z_bf", "damp5")
-        z_bf_early = tile([P, 4 * HALF], BF16, "z_bf_early")
+        z_bf_first = tile([P, 4 * HALF], BF16, "z_bf_first")
         z_w = [
-            [tile([P, HALF], U32, "z_w00", "damp7"), tile([P, HALF], U32, "z_w01", "h2")],
+            [tile([P, HALF], U32, "z_w00", "damp7"), tile([P, HALF], U32, "z_w01", "h%d" % (6 % H_RING))],
             [tile([P, HALF], U32, "z_w1%d" % s) for s in range(2)],
         ]
         z_s = [[tile([P, HALF], U8, "z_s%d%d" % (b, s)) for s in range(2)] for b in range(2)]
 
-        def first_product(pair, words, scales, order):
+        def cap_bank(u, s):
+            return banks[2 * (u % 4) + s]
+
+        def load_bank(u, s):
+            return banks[2 * ((u - 1) % 4) + s]
+
+        def first_product(bank, u, words, scales, order):
             for s in range(2):
                 for a in order:
                     nc.tensor.matmul_mx(
-                        out=banks[2 * pair + s][:],
+                        out=bank(u, s)[:],
                         lhsT=words(a),
                         lhsT_scale=scales(a),
                         rhs=v_w[a][s][:].bitcast(FP8X4),
-                        rhs_scale=v_s[a][:, BANK * s : BANK * (s + 1)],
+                        rhs_scale=v_s[:, a, BANK * s : BANK * (s + 1)],
                         start=(a == order[0]),
                         stop=(a == order[1]),
                     )
@@ -239,17 +242,19 @@ def tile_list_flow_congestion_routing_kernel(
         def cap_product(u):
             b, t = divmod(u, 4)
             cols = slice(P * t, P * (t + 1))
-            first_product(u % 4, lambda a: wc_w[b][:, a, cols].bitcast(FP4X4), lambda a: wc_s[b][:, a, cols], (0, 1))
+            first_product(
+                cap_bank, u, lambda a: wc_w[b][:, a, cols].bitcast(FP4X4), lambda a: wc_s[:, b, a, cols], (0, 1)
+            )
 
         def load_product(u):
             b, t = divmod(u, 4)
             cols = slice(P * t, P * (t + 1))
             first_product(
-                (u - 1) % 4, lambda a: w1_w[b][a][:, cols].bitcast(FP8X4), lambda a: w1_s[b][a][:, cols], (1, 0)
+                load_bank, u, lambda a: w1_w[b][a][:, cols].bitcast(FP8X4), lambda a: w1_s[b][a][:, cols], (1, 0)
             )
 
         def magnitude(u, s):
-            nc.scalar.activation(out=damp[u][s], in_=banks[2 * (u % 4) + s][:], func=ACT.Abs)
+            nc.scalar.activation(out=damp[u][s], in_=cap_bank(u, s)[:], func=ACT.Abs)
 
         def inverse_root(u, s):
             nc.scalar.activation(out=damp[u][s], in_=damp[u][s], func=ACT.Abs_reciprocal_sqrt, bias=1.0)
@@ -267,29 +272,22 @@ def tile_list_flow_congestion_routing_kernel(
             load_product(u)
             for s in range(2):
                 nc.vector.tensor_tensor(
-                    out=h[u][:, BANK * s : BANK * (s + 1)],
-                    in0=banks[2 * ((u - 1) % 4) + s][:],
-                    in1=damp[u][s],
-                    op=ALU.mult,
+                    out=h[u][:, BANK * s : BANK * (s + 1)], in0=load_bank(u, s)[:], in1=damp[u][s], op=ALU.mult
                 )
 
         def gpsimd_slice(u):
-            def copy_load(u, s):
-                nc.scalar.copy(out=load_sb[2 * (ON_GPSIMD.index(u) % 2) + s][:], in_=banks[2 * ((u - 1) % 4) + s][:])
-
-            def product(u, s):
-                nc.gpsimd.tensor_tensor(
-                    out=h[u][:, BANK * s : BANK * (s + 1)], in0=load_sb[2 * (ON_GPSIMD.index(u) % 2) + s][:], in1=damp[u][s], op=ALU.mult
-                )
-
             cap_product(u)
             load_product(u)
             for step in (magnitude, inverse_root):
                 for s in range(2):
                     step(u, s)
             for s in range(2):
-                for step in (square, copy_load, product):
-                    step(u, s)
+                copied = load_sb[2 * (ON_GPSIMD.index(u) % 2) + s]
+                square(u, s)
+                nc.scalar.copy(out=copied[:], in_=load_bank(u, s)[:])
+                nc.gpsimd.tensor_tensor(
+                    out=h[u][:, BANK * s : BANK * (s + 1)], in0=copied[:], in1=damp[u][s], op=ALU.mult
+                )
 
         def pick(u):
             for i, pos in enumerate((pos1_sb, pos2_sb)):
@@ -315,13 +313,12 @@ def tile_list_flow_congestion_routing_kernel(
         def y_psum(s, g, t):
             return banks[2 * Y_BANKS[2 * s + g] + t // 2][:, HALF * (t % 2) : HALF * (t % 2 + 1)]
 
-        def y_passes(b, s, groups=(0, 1)):
-            for g in groups:
+        def y_passes(b, s):
+            for g in range(2):
                 for t in range(4):
-                    cols = slice(GROUP * g + P * t, GROUP * g + P * (t + 1))
                     nc.tensor.matmul_mx(
                         out=y_psum(s, g, t),
-                        lhsT=w2_w[:, b, cols].bitcast(FP8X4),
+                        lhsT=w2_w[:, b, GROUP * g + P * t : GROUP * g + P * (t + 1)].bitcast(FP8X4),
                         lhsT_scale=w2_s[:, g, b, P * t : P * (t + 1)],
                         rhs=z_w[b][s][:].bitcast(FP8X4),
                         rhs_scale=z_s[b][s][:],
@@ -329,44 +326,50 @@ def tile_list_flow_congestion_routing_kernel(
                         stop=(b == 1 and t % 2 == 1),
                     )
 
+        def prepare_second_group():
+            width = GROUP // ROUND_PIECES
+            for a in range(2):
+                for lo in range(0, GROUP, width):
+                    round_w1(gpsimd_copy, w1_bf1[a], w1_raw[1][a], lo, lo + width)
+            for a in range(2):
+                quantize_w1(1, a, w1_bf1[a], 0, GROUP)
+            nc.sync.dma_start(out=w2_raw[:], in_=w2_words.rearrange("b p n i -> p b (n i)").bitcast(I32))
+            nc.sync.dma_start(out=bias[:], in_=b2.rearrange("(g p t) -> p g t", g=2, t=4))
+
         for u in range(AHEAD):
             cap_stage(u)
-        for u in range(SLICES):
+        load_stage(0)
+        load_stage(1)
+        prepare_second_group()
+        pick(0)
+        pick(1)
+        load_stage(2)
+        pick(2)
+        deal_w2_words()
+        deal_w2_scales()
+        cap_stage(3)
+        load_stage(3)
+        pick(3)
+
+        for u in range(4, SLICES):
             if u in ON_GPSIMD:
                 gpsimd_slice(u)
             else:
-                if u >= AHEAD:
-                    cap_stage(u)
+                cap_stage(u)
                 load_stage(u)
-            if u == 1:
-                for a in range(2):
-                    for lo in range(0, P, P // 4):
-                        gpsimd_round(
-                            out=w1_bf[1][a][:].rearrange("p (t m j) -> p m t j", t=4, j=4)[:, lo : lo + P // 4, :, :],
-                            in_=w1_raw[1][a][:].rearrange("p j (m t) -> p m t j", t=4)[:, lo : lo + P // 4, :, :],
-                        )
-                for a in range(2):
-                    quantize_w1(1, a)
-                load_w2()
-                nc.sync.dma_start(out=bias[:], in_=b2.rearrange("(g p t) -> p g t", g=2, t=4))
-            if u == SLICES - 1:
-                quantize_z(0, 0, z_bf[:, 0 : 4 * HALF])
-            if u not in OWN_DAMP:
-                pick(u - 1)
-            if u < 4 and u + 1 in OWN_DAMP:
-                pick(u)
             if u == 5:
                 maximum(picked0, z_bf[:])
-            if u >= 4:
-                pick_half(u, 0)
-                if u < SLICES - DEFERRED:
-                    pick_half(u, 1)
-            if u == 2:
-                deal_w2_words()
-                deal_w2_scales()
+            if u == 7:
+                quantize_z(0, 0, z_bf[:, 0 : 4 * HALF])
+            pick_half(u, 0)
+            if u < SLICES - DEFERRED:
+                pick_half(u, 1)
 
         y = [[tile([P, 4, HALF], F32, "y%d%d" % (s, g)) for g in range(2)] for s in range(2)]
-        y_bf = [[tile([P, 4 * HALF], BF16, "y_bf%d%d" % (s, g), "damp5" if (s, g) == (0, 1) else None) for g in range(2)] for s in range(2)]
+        y_bf = [
+            [tile([P, 4 * HALF], BF16, "y_bf00"), tile([P, 4 * HALF], BF16, "y_bf01", "damp5")],
+            [tile([P, 4 * HALF], BF16, "y_bf1%d" % g) for g in range(2)],
+        ]
         y_w = [tile([P, 2, HALF], I32, "y_w%d" % s) for s in range(2)]
         y_s = tile([P, 2, PAIRS], U8, "y_s")
 
@@ -386,8 +389,11 @@ def tile_list_flow_congestion_routing_kernel(
                     out=rounded.rearrange("p (c i t) -> p c t i", t=4, i=4),
                     in_=y[s][g][:, :, lo : lo + width].rearrange("p t (c i) -> p c t i", i=4),
                 )
-                cols = slice(HALF * s + lo, HALF * s + lo + width)
-                nc.vector.quantize_mx(out=y_w[s][:, g, lo : lo + width].bitcast(FP8X4), scales=y_s[:, g, cols], in_=rounded)
+                nc.vector.quantize_mx(
+                    out=y_w[s][:, g, lo : lo + width].bitcast(FP8X4),
+                    scales=y_s[:, g, HALF * s + lo : HALF * s + lo + width],
+                    in_=rounded,
+                )
             rows = out_0[GROUP * g : GROUP * (g + 1), HALF * s : HALF * (s + 1)].rearrange("(p t) j -> p t j", t=4)
             for t in (0, 2):
                 nc.sync.dma_start(out=rows[:, t : t + 2, :], in_=y[s][g][:, t : t + 2, :])
@@ -397,13 +403,13 @@ def tile_list_flow_congestion_routing_kernel(
             nc.sync.dma_start(out=words[:, :, HALF * s : HALF * (s + 1)], in_=y_w[s][:])
 
         y_passes(0, 0)
-        maximum([picked1[i][:, 4 - DEFERRED : 8 - DEFERRED, :] for i in range(2)], z_bf_early[:])
-        quantize_z(1, 0, z_bf_early[:])
+        maximum([picked1[i][:, 4 - DEFERRED : 8 - DEFERRED, :] for i in range(2)], z_bf_first[:])
+        quantize_z(1, 0, z_bf_first[:])
         y_passes(1, 0)
-        pick_half(SLICES - 2, 1)
+        pick_half(6, 1)
         quantize_z(0, 1, z_bf[:, 4 * HALF : 8 * HALF])
         y_passes(0, 1)
-        pick_half(SLICES - 1, 1)
+        pick_half(7, 1)
         maximum([picked1[i][:, 0:4, :] for i in range(2)], z_bf[:, 0 : 4 * HALF])
         quantize_z(1, 1, z_bf[:, 0 : 4 * HALF])
         finish(0, 0, [nc.scalar.copy])
@@ -413,8 +419,8 @@ def tile_list_flow_congestion_routing_kernel(
         finish(1, 0, [nc.vector.tensor_copy])
         finish(1, 1, [nc.vector.tensor_copy, nc.scalar.copy])
         store_codes(1)
-        for q in range(4):
-            queue = nc.sync if q % 2 == 0 else nc.scalar
+        for q in QUADRANTS:
+            queue = nc.sync if q < 2 else nc.scalar
             queue.dma_start(
                 out=out_2[:, 4 * q : 4 * q + 4, :].rearrange("g r m -> r g m").bitcast(I32),
                 in_=y_s[QUAD * q : QUAD * q + 4, :, :].bitcast(I32),

@@ -26,7 +26,7 @@ SLICES = H // P
 AHEAD = 3
 H_RING = 4
 QUADRANTS = (0, 2, 1, 3)
-ON_GPSIMD = (4, 5, 7)
+ON_GPSIMD = (3, 5, 7)
 DEFERRED = 2
 ROUND_PIECES = 4
 Y_BANKS = (0, 1, 3, 2)
@@ -73,16 +73,12 @@ def tile_list_flow_congestion_routing_kernel(
             [tile([P, 4, GROUP], F32, "w1_raw10", "stage1"), placed([P, 4, GROUP], F32, "w1_raw11", TAB_SECOND_AT)],
         ]
         w1_bf0 = [tile([P, 4 * GROUP], BF16, "w1_bf%d" % a) for a in range(2)]
-        w1_w = [
-            [tile([P, GROUP], U32, "w1_w0%d" % a) for a in range(2)],
-            [placed([P, GROUP], U32, "w1_w10", TAB_SECOND_AT), tile([P, GROUP], U32, "w1_w11")],
-        ]
+        w1_w = [[tile([P, GROUP], U32, "w1_w0%d" % a) for a in range(2)]]
         w1_s = [[tile([P, GROUP], U8, "w1_s%d%d" % (b, a)) for a in range(2)] for b in range(2)]
         w2_raw = tile([P, 2, N], I32, "w2_raw", "wc_raw")
         w2s_raw = tile([P, GROUP], U8, "w2s_raw")
         w2s_dealt = placed([P, GROUP], U8, "w2s_dealt", W1_FIRST_AT + 64)
         w2_s = wcs_raw[:].rearrange("p g (b c) -> p g b c", b=2)
-        w2_w = placed([P, 2, N], I32, "w2_w", TAB_SECOND_AT + 4 * GROUP)
         bias = placed([P, 2, 4], F32, "bias", W1_FIRST_AT)
 
         warm = tile([P, 2], F32, "warm")
@@ -202,16 +198,19 @@ def tile_list_flow_congestion_routing_kernel(
         h = [ring[u % H_RING] for u in range(SLICES)]
         picked0_flat = [tile([P, 4 * PAIRS], F32, "picked0%d" % i) for i in range(2)]
         picked0 = [picked0_flat[i][:].rearrange("p (t j) -> p t j", t=4) for i in range(2)]
-        w1_bf1 = [w1_bf0[1][:], picked0_flat[0][:, PAIRS : 3 * PAIRS].bitcast(BF16)]
+        w1_bf1 = [w1_bf0[1][:], w1_bf0[0][:]]
         picked1 = [tile([P, 8 - DEFERRED, HALF], F32, "picked1%d" % i) for i in range(2)]
-        load_sb = [tile([P, BANK], F32, "load_sb%d" % i) for i in range(4)]
+        load_sb = {u: [tile([P, BANK], F32, "load_sb%d%d" % (u, s)) for s in range(2)] for u in ON_GPSIMD}
         damp = []
         for u in range(SLICES):
-            if u == 1:
-                damp.append([picked0[i][:, 0, :] for i in range(2)])
+            if u in (1, 2):
+                damp.append([picked0[i][:, u - 1, :] for i in range(2)])
             else:
                 own = tile([P, S], F32, "damp%d" % u)
                 damp.append([own[:, BANK * s : BANK * (s + 1)] for s in range(2)])
+        w1_w1 = tile([P, 2, GROUP], U32, "w1_w1", "damp3")
+        w1_w.append([w1_w1[:, a, :] for a in range(2)])
+        w2_w = tile([P, 2, N], I32, "w2_w", "load_sb31")
         z_bf = tile([P, 4 * PAIRS], BF16, "z_bf", "damp5")
         z_bf_first = tile([P, 4 * HALF], BF16, "z_bf_first")
         z_w = [
@@ -282,7 +281,7 @@ def tile_list_flow_congestion_routing_kernel(
                 for s in range(2):
                     step(u, s)
             for s in range(2):
-                copied = load_sb[2 * (ON_GPSIMD.index(u) % 2) + s]
+                copied = load_sb[u][s]
                 square(u, s)
                 nc.scalar.copy(out=copied[:], in_=load_bank(u, s)[:])
                 nc.gpsimd.tensor_tensor(
@@ -331,8 +330,6 @@ def tile_list_flow_congestion_routing_kernel(
             for a in range(2):
                 for lo in range(0, GROUP, width):
                     round_w1(gpsimd_copy, w1_bf1[a], w1_raw[1][a], lo, lo + width)
-            for a in range(2):
-                quantize_w1(1, a, w1_bf1[a], 0, GROUP)
             nc.sync.dma_start(out=w2_raw[:], in_=w2_words.rearrange("b p n i -> p b (n i)").bitcast(I32))
             nc.sync.dma_start(out=bias[:], in_=b2.rearrange("(g p t) -> p g t", g=2, t=4))
 
@@ -342,13 +339,14 @@ def tile_list_flow_congestion_routing_kernel(
         load_stage(1)
         prepare_second_group()
         pick(0)
-        pick(1)
         load_stage(2)
+        pick(1)
         pick(2)
-        deal_w2_words()
         deal_w2_scales()
-        cap_stage(3)
-        load_stage(3)
+        gpsimd_slice(3)
+        for a in range(2):
+            quantize_w1(1, a, w1_bf1[a], 0, GROUP)
+        deal_w2_words()
         pick(3)
 
         for u in range(4, SLICES):

@@ -27,7 +27,7 @@ AHEAD = 3
 H_RING = 4
 QUADRANTS = (0, 2, 1, 3)
 ON_GPSIMD = (3, 5, 7)
-DEFERRED = 2
+DEFERRED = 1
 ROUND_PIECES = 4
 Y_BANKS = (0, 1, 3, 2)
 W1_FIRST_AT = 0
@@ -212,12 +212,17 @@ def tile_list_flow_congestion_routing_kernel(
         w1_w.append([w1_w1[:, a, :] for a in range(2)])
         w2_w = tile([P, 2, N], I32, "w2_w", "load_sb31")
         z_bf = tile([P, 4 * PAIRS], BF16, "z_bf", "damp5")
-        z_bf_first = tile([P, 4 * HALF], BF16, "z_bf_first")
+        z_bf1 = [tile([P, 4 * HALF], BF16, "z_bf1%d" % s) for s in range(2)]
+        z_w0 = tile([P, PAIRS], U32, "z_w0")
+        z_s0 = tile([P, PAIRS], U8, "z_s0")
         z_w = [
-            [tile([P, HALF], U32, "z_w00", "damp7"), tile([P, HALF], U32, "z_w01", "h%d" % (6 % H_RING))],
-            [tile([P, HALF], U32, "z_w1%d" % s) for s in range(2)],
+            [z_w0[:, HALF * s : HALF * (s + 1)] for s in range(2)],
+            [tile([P, HALF], U32, "z_w1%d" % s)[:] for s in range(2)],
         ]
-        z_s = [[tile([P, HALF], U8, "z_s%d%d" % (b, s)) for s in range(2)] for b in range(2)]
+        z_s = [
+            [z_s0[:, HALF * s : HALF * (s + 1)] for s in range(2)],
+            [tile([P, HALF], U8, "z_s1%d" % s)[:] for s in range(2)],
+        ]
 
         def cap_bank(u, s):
             return banks[2 * (u % 4) + s]
@@ -307,7 +312,7 @@ def tile_list_flow_congestion_routing_kernel(
             )
 
         def quantize_z(b, s, rounded):
-            nc.vector.quantize_mx(out=z_w[b][s][:].bitcast(FP8X4), scales=z_s[b][s][:], in_=rounded)
+            nc.vector.quantize_mx(out=z_w[b][s].bitcast(FP8X4), scales=z_s[b][s], in_=rounded)
 
         def y_psum(s, g, t):
             return banks[2 * Y_BANKS[2 * s + g] + t // 2][:, HALF * (t % 2) : HALF * (t % 2 + 1)]
@@ -319,8 +324,8 @@ def tile_list_flow_congestion_routing_kernel(
                         out=y_psum(s, g, t),
                         lhsT=w2_w[:, b, GROUP * g + P * t : GROUP * g + P * (t + 1)].bitcast(FP8X4),
                         lhsT_scale=w2_s[:, g, b, P * t : P * (t + 1)],
-                        rhs=z_w[b][s][:].bitcast(FP8X4),
-                        rhs_scale=z_s[b][s][:],
+                        rhs=z_w[b][s].bitcast(FP8X4),
+                        rhs_scale=z_s[b][s],
                         start=(b == 0 and t % 2 == 0),
                         stop=(b == 1 and t % 2 == 1),
                     )
@@ -357,15 +362,14 @@ def tile_list_flow_congestion_routing_kernel(
                 load_stage(u)
             if u == 5:
                 maximum(picked0, z_bf[:])
-            if u == 7:
-                quantize_z(0, 0, z_bf[:, 0 : 4 * HALF])
+                nc.vector.quantize_mx(out=z_w0[:].bitcast(FP8X4), scales=z_s0[:], in_=z_bf[:])
             pick_half(u, 0)
             if u < SLICES - DEFERRED:
                 pick_half(u, 1)
 
         y = [[tile([P, 4, HALF], F32, "y%d%d" % (s, g)) for g in range(2)] for s in range(2)]
         y_bf = [
-            [tile([P, 4 * HALF], BF16, "y_bf00"), tile([P, 4 * HALF], BF16, "y_bf01", "damp5")],
+            [tile([P, 4 * HALF], BF16, "y_bf00", "z_bf11"), tile([P, 4 * HALF], BF16, "y_bf01")],
             [tile([P, 4 * HALF], BF16, "y_bf1%d" % g) for g in range(2)],
         ]
         y_w = [tile([P, 2, HALF], I32, "y_w%d" % s) for s in range(2)]
@@ -401,16 +405,14 @@ def tile_list_flow_congestion_routing_kernel(
             nc.sync.dma_start(out=words[:, :, HALF * s : HALF * (s + 1)], in_=y_w[s][:])
 
         y_passes(0, 0)
-        maximum([picked1[i][:, 4 - DEFERRED : 8 - DEFERRED, :] for i in range(2)], z_bf_first[:])
-        quantize_z(1, 0, z_bf_first[:])
-        y_passes(1, 0)
-        pick_half(6, 1)
-        quantize_z(0, 1, z_bf[:, 4 * HALF : 8 * HALF])
         y_passes(0, 1)
+        maximum([picked1[i][:, 4 - DEFERRED : 8 - DEFERRED, :] for i in range(2)], z_bf1[0][:])
+        quantize_z(1, 0, z_bf1[0][:])
+        y_passes(1, 0)
         pick_half(7, 1)
-        maximum([picked1[i][:, 0:4, :] for i in range(2)], z_bf[:, 0 : 4 * HALF])
-        quantize_z(1, 1, z_bf[:, 0 : 4 * HALF])
-        finish(0, 0, [nc.scalar.copy])
+        maximum([picked1[i][:, 0:4, :] for i in range(2)], z_bf1[1][:])
+        quantize_z(1, 1, z_bf1[1][:])
+        finish(0, 0, [nc.vector.tensor_copy])
         finish(0, 1, [nc.vector.tensor_copy])
         store_codes(0)
         y_passes(1, 1)

@@ -26,7 +26,7 @@ SLICES = H // P
 AHEAD = 3
 H_RING = 4
 QUADRANTS = (0, 2, 1, 3)
-ON_GPSIMD = (3, 5, 7)
+ON_GPSIMD = (3, 5, 6, 7)
 DEFERRED = 1
 ROUND_PIECES = 4
 Y_BANKS = (0, 1, 3, 2)
@@ -72,9 +72,14 @@ def tile_list_flow_congestion_routing_kernel(
             [placed([P, 4, GROUP], F32, "w1_raw00", W1_FIRST_AT), tile([P, 4, GROUP], F32, "w1_raw01", "wc_raw")],
             [tile([P, 4, GROUP], F32, "w1_raw10", "stage1"), placed([P, 4, GROUP], F32, "w1_raw11", TAB_SECOND_AT)],
         ]
-        w1_bf0 = [tile([P, 4 * GROUP], BF16, "w1_bf%d" % a) for a in range(2)]
+        w1_bf = tile([P, 8 * GROUP], BF16, "w1_bf")
+        w1_bf0 = [w1_bf[:, 4 * GROUP * a : 4 * GROUP * (a + 1)] for a in range(2)]
         w1_w = [[tile([P, GROUP], U32, "w1_w0%d" % a) for a in range(2)]]
-        w1_s = [[tile([P, GROUP], U8, "w1_s%d%d" % (b, a)) for a in range(2)] for b in range(2)]
+        w1_s1 = tile([P, 2 * GROUP], U8, "w1_s1")
+        w1_s = [
+            [tile([P, GROUP], U8, "w1_s0%d" % a) for a in range(2)],
+            [w1_s1[:, GROUP * (1 - a) : GROUP * (2 - a)] for a in range(2)],
+        ]
         w2_raw = tile([P, 2, N], I32, "w2_raw", "wc_raw")
         w2s_raw = tile([P, GROUP], U8, "w2s_raw")
         w2s_dealt = placed([P, GROUP], U8, "w2s_dealt", W1_FIRST_AT + 64)
@@ -185,21 +190,20 @@ def tile_list_flow_congestion_routing_kernel(
         gather_words(1, 1)
         deal_wc_words(1)
         load_w1(1, 1)
-        round_w1(nc.vector.tensor_copy, w1_bf0[0][:], w1_raw[0][0], 0, GROUP)
-        round_w1(nc.vector.tensor_copy, w1_bf0[1][:], w1_raw[0][1], 0, GROUP // 2)
-        quantize_w1(0, 0, w1_bf0[0], 0, P)
-        round_w1(nc.vector.tensor_copy, w1_bf0[1][:], w1_raw[0][1], GROUP // 2, GROUP)
-        quantize_w1(0, 1, w1_bf0[1], 0, P)
-        for lo, hi in ((P, 2 * P), (2 * P, GROUP)):
-            for a in range(2):
-                quantize_w1(0, a, w1_bf0[a], lo, hi)
+        round_w1(nc.vector.tensor_copy, w1_bf0[0], w1_raw[0][0], 0, GROUP)
+        round_w1(nc.vector.tensor_copy, w1_bf0[1], w1_raw[0][1], 0, GROUP // 2)
+        quantize_w1(0, 0, w1_bf0[0], 0, GROUP)
+        round_w1(nc.vector.tensor_copy, w1_bf0[1], w1_raw[0][1], GROUP // 2, GROUP)
+        quantize_w1(0, 1, w1_bf0[1], 0, GROUP // 2)
+        quantize_w1(0, 1, w1_bf0[1], GROUP // 2, GROUP)
 
         ring = [tile([P, S], F32, "h%d" % i) for i in range(H_RING)]
         h = [ring[u % H_RING] for u in range(SLICES)]
         picked0_flat = [tile([P, 4 * PAIRS], F32, "picked0%d" % i) for i in range(2)]
         picked0 = [picked0_flat[i][:].rearrange("p (t j) -> p t j", t=4) for i in range(2)]
-        w1_bf1 = [w1_bf0[1][:], w1_bf0[0][:]]
-        picked1 = [tile([P, 8 - DEFERRED, HALF], F32, "picked1%d" % i) for i in range(2)]
+        w1_bf1 = [w1_bf0[1], w1_bf0[0]]
+        picked1_flat = [tile([P, 4 * PAIRS + HALF], F32, "picked1%d" % i) for i in range(2)]
+        picked1 = [picked1_flat[i][:, 0 : 4 * PAIRS].rearrange("p (t j) -> p t j", t=4) for i in range(2)]
         load_sb = {u: [tile([P, BANK], F32, "load_sb%d%d" % (u, s)) for s in range(2)] for u in ON_GPSIMD}
         damp = []
         for u in range(SLICES):
@@ -208,12 +212,13 @@ def tile_list_flow_congestion_routing_kernel(
             else:
                 own = tile([P, S], F32, "damp%d" % u)
                 damp.append([own[:, BANK * s : BANK * (s + 1)] for s in range(2)])
-        w1_w1 = tile([P, 2, GROUP], U32, "w1_w1", "damp3")
-        w1_w.append([w1_w1[:, a, :] for a in range(2)])
+        damp[4][1] = picked0[1][:, 3, :]
+        w1_w1 = tile([P, 2 * GROUP], U32, "w1_w1", "damp3")
+        w1_w.append([w1_w1[:, GROUP * (1 - a) : GROUP * (2 - a)] for a in range(2)])
         w2_w = tile([P, 2, N], I32, "w2_w", "load_sb31")
         z_bf = tile([P, 4 * PAIRS], BF16, "z_bf", "damp5")
-        z_bf1 = [tile([P, 4 * HALF], BF16, "z_bf1%d" % s) for s in range(2)]
-        z_w0 = tile([P, PAIRS], U32, "z_w0")
+        z_bf1 = [picked1_flat[0][:, 7 * HALF : 9 * HALF].bitcast(BF16), tile([P, 4 * HALF], BF16, "z_bf11")[:]]
+        z_w0 = tile([P, PAIRS], U32, "z_w0", "damp6")
         z_s0 = tile([P, PAIRS], U8, "z_s0")
         z_w = [
             [z_w0[:, HALF * s : HALF * (s + 1)] for s in range(2)],
@@ -293,15 +298,10 @@ def tile_list_flow_congestion_routing_kernel(
                     out=h[u][:, BANK * s : BANK * (s + 1)], in0=copied[:], in1=damp[u][s], op=ALU.mult
                 )
 
-        def pick(u):
-            for i, pos in enumerate((pos1_sb, pos2_sb)):
-                nc.vector.tensor_copy(picked0[i][:, u, :], h[u][:].indirect(pos[:]))
-
-        def pick_half(u, s):
-            slot = u - 4 + (4 - DEFERRED) * (1 - s)
-            for i, pos in enumerate((pos1_sb, pos2_sb)):
-                entries = pos[:, HALF // 16 * s : HALF // 16 * (s + 1)]
-                nc.vector.tensor_copy(picked1[i][:, slot, :], h[u][:].indirect(entries))
+        def pick(u, i, lo=0, hi=PAIRS):
+            b, t = divmod(u, 4)
+            entries = (pos1_sb, pos2_sb)[i][:, lo // 16 : hi // 16]
+            nc.vector.tensor_copy((picked0, picked1)[b][i][:, t, lo:hi], h[u][:].indirect(entries))
 
         def maximum(picked, rounded):
             nc.vector.tensor_tensor(
@@ -343,62 +343,66 @@ def tile_list_flow_congestion_routing_kernel(
         load_stage(0)
         load_stage(1)
         prepare_second_group()
-        pick(0)
+        pick(0, 0)
+        pick(0, 1)
         load_stage(2)
-        pick(1)
-        pick(2)
+        for u in (1, 2):
+            pick(u, 0)
+            pick(u, 1)
         deal_w2_scales()
         gpsimd_slice(3)
-        for a in range(2):
-            quantize_w1(1, a, w1_bf1[a], 0, GROUP)
+        nc.vector.quantize_mx(out=w1_w1[:].bitcast(FP8X4), scales=w1_s1[:], in_=w1_bf[:])
         deal_w2_words()
-        pick(3)
+        pick(3, 0)
 
-        for u in range(4, SLICES):
-            if u in ON_GPSIMD:
-                gpsimd_slice(u)
-            else:
-                cap_stage(u)
-                load_stage(u)
-            if u == 5:
-                maximum(picked0, z_bf[:])
-                nc.vector.quantize_mx(out=z_w0[:].bitcast(FP8X4), scales=z_s0[:], in_=z_bf[:])
-            pick_half(u, 0)
-            if u < SLICES - DEFERRED:
-                pick_half(u, 1)
+        cap_stage(4)
+        load_stage(4)
+        pick(3, 1)
+        pick(4, 0)
+        pick(4, 1)
+        gpsimd_slice(5)
+        maximum(picked0, z_bf[:])
+        pick(5, 0)
+        pick(5, 1)
+        gpsimd_slice(6)
+        nc.vector.quantize_mx(out=z_w0[:].bitcast(FP8X4), scales=z_s0[:], in_=z_bf[:])
+        pick(6, 0)
+        pick(6, 1)
+        gpsimd_slice(7)
+        pick(7, 0, 0, HALF)
+        pick(7, 1, 0, HALF)
 
-        y = [[tile([P, 4, HALF], F32, "y%d%d" % (s, g)) for g in range(2)] for s in range(2)]
-        y_bf = [
-            [tile([P, 4 * HALF], BF16, "y_bf00", "z_bf11"), tile([P, 4 * HALF], BF16, "y_bf01")],
-            [tile([P, 4 * HALF], BF16, "y_bf1%d" % g) for g in range(2)],
-        ]
+        y = [tile([P, 2, 4, HALF], F32, "y%d" % s) for s in range(2)]
+        y_bf = [tile([P, 2, 4 * HALF], BF16, "y_bf0", "z_bf11"), tile([P, 2, 4 * HALF], BF16, "y_bf1")]
         y_w = [tile([P, 2, HALF], I32, "y_w%d" % s) for s in range(2)]
         y_s = tile([P, 2, PAIRS], U8, "y_s")
 
-        def finish(s, g, round_copies):
-            width = HALF // len(round_copies)
-            for piece, round_copy in enumerate(round_copies):
-                lo = width * piece
-                for t in range(4):
-                    nc.scalar.activation(
-                        out=y[s][g][:, t, lo : lo + width],
-                        in_=y_psum(s, g, t)[:, lo : lo + width],
-                        func=ACT.Identity,
-                        bias=bias[:, g, t : t + 1],
-                    )
-                rounded = y_bf[s][g][:, 4 * lo : 4 * (lo + width)]
-                round_copy(
-                    out=rounded.rearrange("p (c i t) -> p c t i", t=4, i=4),
-                    in_=y[s][g][:, :, lo : lo + width].rearrange("p t (c i) -> p c t i", i=4),
+        def add_bias(s, g, lo=0, hi=HALF):
+            for t in range(4):
+                nc.scalar.activation(
+                    out=y[s][:, g, t, lo:hi],
+                    in_=y_psum(s, g, t)[:, lo:hi],
+                    func=ACT.Identity,
+                    bias=bias[:, g, t : t + 1],
                 )
-                nc.vector.quantize_mx(
-                    out=y_w[s][:, g, lo : lo + width].bitcast(FP8X4),
-                    scales=y_s[:, g, HALF * s + lo : HALF * s + lo + width],
-                    in_=rounded,
-                )
+
+        def store_y(s, g):
             rows = out_0[GROUP * g : GROUP * (g + 1), HALF * s : HALF * (s + 1)].rearrange("(p t) j -> p t j", t=4)
             for t in (0, 2):
-                nc.sync.dma_start(out=rows[:, t : t + 2, :], in_=y[s][g][:, t : t + 2, :])
+                nc.sync.dma_start(out=rows[:, t : t + 2, :], in_=y[s][:, g, t : t + 2, :])
+
+        def round_y(copy, s, g, lo=0, hi=HALF):
+            copy(
+                out=y_bf[s][:, g, 4 * lo : 4 * hi].rearrange("p (c i t) -> p c t i", t=4, i=4),
+                in_=y[s][:, g, :, lo:hi].rearrange("p t (c i) -> p c t i", i=4),
+            )
+
+        def quantize_y(s, g, lo=0, hi=HALF):
+            nc.vector.quantize_mx(
+                out=y_w[s][:, g, lo:hi].bitcast(FP8X4),
+                scales=y_s[:, g, HALF * s + lo : HALF * s + hi],
+                in_=y_bf[s][:, g, 4 * lo : 4 * hi],
+            )
 
         def store_codes(s):
             words = out_1.rearrange("g p m t -> p g (m t)").bitcast(I32)
@@ -406,18 +410,33 @@ def tile_list_flow_congestion_routing_kernel(
 
         y_passes(0, 0)
         y_passes(0, 1)
-        maximum([picked1[i][:, 4 - DEFERRED : 8 - DEFERRED, :] for i in range(2)], z_bf1[0][:])
-        quantize_z(1, 0, z_bf1[0][:])
+        maximum([picked1[i][:, :, 0:HALF] for i in range(2)], z_bf1[0])
+        pick(7, 1, HALF, PAIRS)
+        quantize_z(1, 0, z_bf1[0])
         y_passes(1, 0)
-        pick_half(7, 1)
-        maximum([picked1[i][:, 0:4, :] for i in range(2)], z_bf1[1][:])
-        quantize_z(1, 1, z_bf1[1][:])
-        finish(0, 0, [nc.vector.tensor_copy])
-        finish(0, 1, [nc.vector.tensor_copy])
+        pick(7, 0, HALF, PAIRS)
+        maximum([picked1[i][:, :, HALF:PAIRS] for i in range(2)], z_bf1[1])
+        quantize_z(1, 1, z_bf1[1])
+        for g in range(2):
+            add_bias(0, g)
+            store_y(0, g)
+        for g in range(2):
+            round_y(nc.vector.tensor_copy, 0, g)
+        for g in range(2):
+            quantize_y(0, g)
         store_codes(0)
         y_passes(1, 1)
-        finish(1, 0, [nc.vector.tensor_copy])
-        finish(1, 1, [nc.vector.tensor_copy, nc.scalar.copy])
+        add_bias(1, 0)
+        store_y(1, 0)
+        round_y(nc.vector.tensor_copy, 1, 0)
+        add_bias(1, 1, 0, HALF // 2)
+        round_y(nc.vector.tensor_copy, 1, 1, 0, HALF // 2)
+        quantize_y(1, 0)
+        quantize_y(1, 1, 0, HALF // 2)
+        add_bias(1, 1, HALF // 2, HALF)
+        store_y(1, 1)
+        round_y(nc.scalar.copy, 1, 1, HALF // 2, HALF)
+        quantize_y(1, 1, HALF // 2, HALF)
         store_codes(1)
         for q in QUADRANTS:
             queue = nc.sync if q < 2 else nc.scalar

@@ -27,6 +27,7 @@ AHEAD = 3
 H_RING = 4
 QUADRANTS = (0, 2, 1, 3)
 ON_GPSIMD = (3, 5, 6, 7)
+SQUARED_ON_GPSIMD = 4
 DEFERRED = 1
 ROUND_PIECES = 4
 Y_BANKS = (0, 1, 3, 2)
@@ -198,12 +199,14 @@ def tile_list_flow_congestion_routing_kernel(
         quantize_w1(0, 1, w1_bf0[1], GROUP // 2, GROUP)
 
         ring = [tile([P, S], F32, "h%d" % i) for i in range(H_RING)]
-        h = [ring[u % H_RING] for u in range(SLICES)]
-        picked0_flat = [tile([P, 4 * PAIRS], F32, "picked0%d" % i) for i in range(2)]
-        picked0 = [picked0_flat[i][:].rearrange("p (t j) -> p t j", t=4) for i in range(2)]
+        h = [ring[u % H_RING][:] for u in range(SLICES)]
+        picked = [tile([P, 17 * HALF], F32, "picked0"), tile([P, 14 * HALF], F32, "picked1")]
+        picked0 = [picked[i][:, 0 : 4 * PAIRS].rearrange("p (t j) -> p t j", t=4) for i in range(2)]
+        h[6] = picked[0][:, 0:S]
         w1_bf1 = [w1_bf0[1], w1_bf0[0]]
-        picked1_flat = [tile([P, 4 * PAIRS + HALF], F32, "picked1%d" % i) for i in range(2)]
-        picked1 = [picked1_flat[i][:, 0 : 4 * PAIRS].rearrange("p (t j) -> p t j", t=4) for i in range(2)]
+        picked1 = [
+            picked[i][:, (4 - i) * PAIRS : (8 - i) * PAIRS].rearrange("p (t j) -> p t j", t=4) for i in range(2)
+        ]
         load_sb = {u: [tile([P, BANK], F32, "load_sb%d%d" % (u, s)) for s in range(2)] for u in ON_GPSIMD}
         damp = []
         for u in range(SLICES):
@@ -212,22 +215,18 @@ def tile_list_flow_congestion_routing_kernel(
             else:
                 own = tile([P, S], F32, "damp%d" % u)
                 damp.append([own[:, BANK * s : BANK * (s + 1)] for s in range(2)])
-        damp[4][1] = picked0[1][:, 3, :]
+        root = list(damp)
+        damp[4] = [tile([P, BANK], F32, "damp40", "wc_raw")[:], picked0[1][:, 3, :]]
         w1_w1 = tile([P, 2 * GROUP], U32, "w1_w1", "damp3")
         w1_w.append([w1_w1[:, GROUP * (1 - a) : GROUP * (2 - a)] for a in range(2)])
         w2_w = tile([P, 2, N], I32, "w2_w", "load_sb31")
         z_bf = tile([P, 4 * PAIRS], BF16, "z_bf", "damp5")
-        z_bf1 = [picked1_flat[0][:, 7 * HALF : 9 * HALF].bitcast(BF16), tile([P, 4 * HALF], BF16, "z_bf11")[:]]
-        z_w0 = tile([P, PAIRS], U32, "z_w0", "damp6")
-        z_s0 = tile([P, PAIRS], U8, "z_s0")
+        z_bf1 = [picked[0][:, 15 * HALF : 17 * HALF].bitcast(BF16), tile([P, 4 * HALF], BF16, "z_bf11")[:]]
         z_w = [
-            [z_w0[:, HALF * s : HALF * (s + 1)] for s in range(2)],
+            [tile([P, HALF], U32, "z_w00", "damp7")[:], tile([P, HALF], U32, "z_w01", "h%d" % (7 % H_RING))[:]],
             [tile([P, HALF], U32, "z_w1%d" % s)[:] for s in range(2)],
         ]
-        z_s = [
-            [z_s0[:, HALF * s : HALF * (s + 1)] for s in range(2)],
-            [tile([P, HALF], U8, "z_s1%d" % s)[:] for s in range(2)],
-        ]
+        z_s = [[tile([P, HALF], U8, "z_s%d%d" % (b, s))[:] for s in range(2)] for b in range(2)]
 
         def cap_bank(u, s):
             return banks[2 * (u % 4) + s]
@@ -263,13 +262,16 @@ def tile_list_flow_congestion_routing_kernel(
             )
 
         def magnitude(u, s):
-            nc.scalar.activation(out=damp[u][s], in_=cap_bank(u, s)[:], func=ACT.Abs)
+            nc.scalar.activation(out=root[u][s], in_=cap_bank(u, s)[:], func=ACT.Abs)
 
         def inverse_root(u, s):
-            nc.scalar.activation(out=damp[u][s], in_=damp[u][s], func=ACT.Abs_reciprocal_sqrt, bias=1.0)
+            nc.scalar.activation(out=root[u][s], in_=root[u][s], func=ACT.Abs_reciprocal_sqrt, bias=1.0)
 
         def square(u, s):
-            nc.scalar.activation(out=damp[u][s], in_=damp[u][s], func=ACT.Square)
+            if u == SQUARED_ON_GPSIMD:
+                nc.gpsimd.tensor_tensor(out=damp[u][s], in0=root[u][s], in1=root[u][s], op=ALU.mult)
+            else:
+                nc.scalar.activation(out=damp[u][s], in_=root[u][s], func=ACT.Square)
 
         def cap_stage(u):
             cap_product(u)
@@ -278,15 +280,12 @@ def tile_list_flow_congestion_routing_kernel(
                     step(u, s)
 
         def load_stage(u):
-            load_product(u)
             for s in range(2):
                 nc.vector.tensor_tensor(
                     out=h[u][:, BANK * s : BANK * (s + 1)], in0=load_bank(u, s)[:], in1=damp[u][s], op=ALU.mult
                 )
 
         def gpsimd_slice(u):
-            cap_product(u)
-            load_product(u)
             for step in (magnitude, inverse_root):
                 for s in range(2):
                     step(u, s)
@@ -301,7 +300,7 @@ def tile_list_flow_congestion_routing_kernel(
         def pick(u, i, lo=0, hi=PAIRS):
             b, t = divmod(u, 4)
             entries = (pos1_sb, pos2_sb)[i][:, lo // 16 : hi // 16]
-            nc.vector.tensor_copy((picked0, picked1)[b][i][:, t, lo:hi], h[u][:].indirect(entries))
+            nc.vector.tensor_copy((picked0, picked1)[b][i][:, t, lo:hi], h[u].indirect(entries))
 
         def maximum(picked, rounded):
             nc.vector.tensor_tensor(
@@ -340,37 +339,48 @@ def tile_list_flow_congestion_routing_kernel(
 
         for u in range(AHEAD):
             cap_stage(u)
-        load_stage(0)
-        load_stage(1)
+        for u in range(2):
+            load_product(u)
+            load_stage(u)
         prepare_second_group()
         pick(0, 0)
         pick(0, 1)
+        load_product(2)
         load_stage(2)
         for u in (1, 2):
             pick(u, 0)
             pick(u, 1)
         deal_w2_scales()
+        cap_product(3)
+        load_product(3)
         gpsimd_slice(3)
         nc.vector.quantize_mx(out=w1_w1[:].bitcast(FP8X4), scales=w1_s1[:], in_=w1_bf[:])
         deal_w2_words()
         pick(3, 0)
 
         cap_stage(4)
+        cap_product(5)
+        load_product(5)
+        load_product(4)
         load_stage(4)
         pick(3, 1)
         pick(4, 0)
-        pick(4, 1)
         gpsimd_slice(5)
         maximum(picked0, z_bf[:])
+        pick(4, 1)
         pick(5, 0)
         pick(5, 1)
+        cap_product(6)
+        load_product(6)
         gpsimd_slice(6)
-        nc.vector.quantize_mx(out=z_w0[:].bitcast(FP8X4), scales=z_s0[:], in_=z_bf[:])
         pick(6, 0)
         pick(6, 1)
+        cap_product(7)
+        load_product(7)
         gpsimd_slice(7)
         pick(7, 0, 0, HALF)
         pick(7, 1, 0, HALF)
+        quantize_z(0, 0, z_bf[:, 0 : 4 * HALF])
 
         y = [tile([P, 2, 4, HALF], F32, "y%d" % s) for s in range(2)]
         y_bf = [tile([P, 2, 4 * HALF], BF16, "y_bf0", "z_bf11"), tile([P, 2, 4 * HALF], BF16, "y_bf1")]
@@ -409,12 +419,13 @@ def tile_list_flow_congestion_routing_kernel(
             nc.sync.dma_start(out=words[:, :, HALF * s : HALF * (s + 1)], in_=y_w[s][:])
 
         y_passes(0, 0)
-        y_passes(0, 1)
         maximum([picked1[i][:, :, 0:HALF] for i in range(2)], z_bf1[0])
         pick(7, 1, HALF, PAIRS)
         quantize_z(1, 0, z_bf1[0])
         y_passes(1, 0)
         pick(7, 0, HALF, PAIRS)
+        quantize_z(0, 1, z_bf[:, 4 * HALF : 8 * HALF])
+        y_passes(0, 1)
         maximum([picked1[i][:, :, HALF:PAIRS] for i in range(2)], z_bf1[1])
         quantize_z(1, 1, z_bf1[1])
         for g in range(2):

@@ -26,9 +26,7 @@ SLICES = H // P
 AHEAD = 3
 H_RING = 4
 QUADRANTS = (0, 2, 1, 3)
-ON_GPSIMD = (3, 5, 6, 7)
-SQUARED_ON_GPSIMD = 4
-DEFERRED = 1
+ON_GPSIMD = ((3, 0), (3, 1), (5, 0), (5, 1), (6, 0), (6, 1), (7, 0))
 ROUND_PIECES = 4
 Y_BANKS = (0, 1, 3, 2)
 W1_FIRST_AT = 0
@@ -200,33 +198,33 @@ def tile_list_flow_congestion_routing_kernel(
 
         ring = [tile([P, S], F32, "h%d" % i) for i in range(H_RING)]
         h = [ring[u % H_RING][:] for u in range(SLICES)]
-        picked = [tile([P, 17 * HALF], F32, "picked0"), tile([P, 14 * HALF], F32, "picked1")]
-        picked0 = [picked[i][:, 0 : 4 * PAIRS].rearrange("p (t j) -> p t j", t=4) for i in range(2)]
+        picked = [tile([P, 8 * PAIRS + HALF], F32, "picked0"), tile([P, 7 * PAIRS], F32, "picked1")]
+        slots = [
+            [picked[i][:, first * PAIRS : (first + 4) * PAIRS].rearrange("p (t j) -> p t j", t=4) for i, first in pair]
+            for pair in (((0, 0), (1, 0)), ((0, 4), (1, 3)))
+        ]
         h[6] = picked[0][:, 0:S]
         w1_bf1 = [w1_bf0[1], w1_bf0[0]]
-        picked1 = [
-            picked[i][:, (4 - i) * PAIRS : (8 - i) * PAIRS].rearrange("p (t j) -> p t j", t=4) for i in range(2)
-        ]
-        load_sb = {u: [tile([P, BANK], F32, "load_sb%d%d" % (u, s)) for s in range(2)] for u in ON_GPSIMD}
+        load_sb = {(u, s): tile([P, BANK], F32, "load_sb%d%d" % (u, s)) for u, s in ON_GPSIMD}
         damp = []
         for u in range(SLICES):
             if u in (1, 2):
-                damp.append([picked0[i][:, u - 1, :] for i in range(2)])
+                damp.append([slots[0][i][:, u - 1, :] for i in range(2)])
+            elif u == 4:
+                damp.append([tile([P, BANK], F32, "damp4")[:], slots[0][1][:, 3, :]])
             else:
                 own = tile([P, S], F32, "damp%d" % u)
                 damp.append([own[:, BANK * s : BANK * (s + 1)] for s in range(2)])
-        root = list(damp)
-        damp[4] = [tile([P, BANK], F32, "damp40", "wc_raw")[:], picked0[1][:, 3, :]]
         w1_w1 = tile([P, 2 * GROUP], U32, "w1_w1", "damp3")
         w1_w.append([w1_w1[:, GROUP * (1 - a) : GROUP * (2 - a)] for a in range(2)])
         w2_w = tile([P, 2, N], I32, "w2_w", "load_sb31")
-        z_bf = tile([P, 4 * PAIRS], BF16, "z_bf", "damp5")
-        z_bf1 = [picked[0][:, 15 * HALF : 17 * HALF].bitcast(BF16), tile([P, 4 * HALF], BF16, "z_bf11")[:]]
+        z_bf0 = tile([P, 4 * PAIRS], BF16, "z_bf0", "damp5")
+        z_bf1 = [picked[0][:, 8 * PAIRS - HALF :].bitcast(BF16), tile([P, 4 * HALF], BF16, "z_bf11")[:]]
         z_w = [
-            [tile([P, HALF], U32, "z_w00", "damp7")[:], tile([P, HALF], U32, "z_w01", "h%d" % (7 % H_RING))[:]],
-            [tile([P, HALF], U32, "z_w1%d" % s)[:] for s in range(2)],
+            [tile([P, HALF], U32, "z_w00", "load_sb70"), tile([P, HALF], U32, "z_w01", "h%d" % (7 % H_RING))],
+            [tile([P, HALF], U32, "z_w1%d" % s) for s in range(2)],
         ]
-        z_s = [[tile([P, HALF], U8, "z_s%d%d" % (b, s))[:] for s in range(2)] for b in range(2)]
+        z_s = [[tile([P, HALF], U8, "z_s%d%d" % (b, s)) for s in range(2)] for b in range(2)]
 
         def cap_bank(u, s):
             return banks[2 * (u % 4) + s]
@@ -262,16 +260,13 @@ def tile_list_flow_congestion_routing_kernel(
             )
 
         def magnitude(u, s):
-            nc.scalar.activation(out=root[u][s], in_=cap_bank(u, s)[:], func=ACT.Abs)
+            nc.scalar.activation(out=damp[u][s], in_=cap_bank(u, s)[:], func=ACT.Abs)
 
         def inverse_root(u, s):
-            nc.scalar.activation(out=root[u][s], in_=root[u][s], func=ACT.Abs_reciprocal_sqrt, bias=1.0)
+            nc.scalar.activation(out=damp[u][s], in_=damp[u][s], func=ACT.Abs_reciprocal_sqrt, bias=1.0)
 
         def square(u, s):
-            if u == SQUARED_ON_GPSIMD:
-                nc.gpsimd.tensor_tensor(out=damp[u][s], in0=root[u][s], in1=root[u][s], op=ALU.mult)
-            else:
-                nc.scalar.activation(out=damp[u][s], in_=root[u][s], func=ACT.Square)
+            nc.scalar.activation(out=damp[u][s], in_=damp[u][s], func=ACT.Square)
 
         def cap_stage(u):
             cap_product(u)
@@ -279,39 +274,44 @@ def tile_list_flow_congestion_routing_kernel(
                 for s in range(2):
                     step(u, s)
 
-        def load_stage(u):
-            for s in range(2):
-                nc.vector.tensor_tensor(
-                    out=h[u][:, BANK * s : BANK * (s + 1)], in0=load_bank(u, s)[:], in1=damp[u][s], op=ALU.mult
-                )
+        def multiply(u, s):
+            half = h[u][:, BANK * s : BANK * (s + 1)]
+            if (u, s) in ON_GPSIMD:
+                nc.scalar.copy(out=load_sb[u, s][:], in_=load_bank(u, s)[:])
+                nc.gpsimd.tensor_tensor(out=half, in0=load_sb[u, s][:], in1=damp[u][s], op=ALU.mult)
+            else:
+                nc.vector.tensor_tensor(out=half, in0=load_bank(u, s)[:], in1=damp[u][s], op=ALU.mult)
 
-        def gpsimd_slice(u):
+        def load_stage(u):
+            load_product(u)
+            for s in range(2):
+                multiply(u, s)
+
+        def whole_slice(u):
+            cap_product(u)
+            load_product(u)
             for step in (magnitude, inverse_root):
                 for s in range(2):
                     step(u, s)
             for s in range(2):
-                copied = load_sb[u][s]
                 square(u, s)
-                nc.scalar.copy(out=copied[:], in_=load_bank(u, s)[:])
-                nc.gpsimd.tensor_tensor(
-                    out=h[u][:, BANK * s : BANK * (s + 1)], in0=copied[:], in1=damp[u][s], op=ALU.mult
-                )
+                multiply(u, s)
 
         def pick(u, i, lo=0, hi=PAIRS):
             b, t = divmod(u, 4)
             entries = (pos1_sb, pos2_sb)[i][:, lo // 16 : hi // 16]
-            nc.vector.tensor_copy((picked0, picked1)[b][i][:, t, lo:hi], h[u].indirect(entries))
+            nc.vector.tensor_copy(slots[b][i][:, t, lo:hi], h[u].indirect(entries))
 
-        def maximum(picked, rounded):
+        def maximum(b, lo, hi, rounded):
             nc.vector.tensor_tensor(
                 out=rounded.rearrange("p (c i t) -> p c t i", t=4, i=4),
-                in0=picked[0].rearrange("p t (c i) -> p c t i", i=4),
-                in1=picked[1].rearrange("p t (c i) -> p c t i", i=4),
+                in0=slots[b][0][:, :, lo:hi].rearrange("p t (c i) -> p c t i", i=4),
+                in1=slots[b][1][:, :, lo:hi].rearrange("p t (c i) -> p c t i", i=4),
                 op=ALU.max,
             )
 
         def quantize_z(b, s, rounded):
-            nc.vector.quantize_mx(out=z_w[b][s].bitcast(FP8X4), scales=z_s[b][s], in_=rounded)
+            nc.vector.quantize_mx(out=z_w[b][s][:].bitcast(FP8X4), scales=z_s[b][s][:], in_=rounded)
 
         def y_psum(s, g, t):
             return banks[2 * Y_BANKS[2 * s + g] + t // 2][:, HALF * (t % 2) : HALF * (t % 2 + 1)]
@@ -323,8 +323,8 @@ def tile_list_flow_congestion_routing_kernel(
                         out=y_psum(s, g, t),
                         lhsT=w2_w[:, b, GROUP * g + P * t : GROUP * g + P * (t + 1)].bitcast(FP8X4),
                         lhsT_scale=w2_s[:, g, b, P * t : P * (t + 1)],
-                        rhs=z_w[b][s].bitcast(FP8X4),
-                        rhs_scale=z_s[b][s],
+                        rhs=z_w[b][s][:].bitcast(FP8X4),
+                        rhs_scale=z_s[b][s][:],
                         start=(b == 0 and t % 2 == 0),
                         stop=(b == 1 and t % 2 == 1),
                     )
@@ -339,48 +339,37 @@ def tile_list_flow_congestion_routing_kernel(
 
         for u in range(AHEAD):
             cap_stage(u)
-        for u in range(2):
-            load_product(u)
-            load_stage(u)
+        load_stage(0)
+        load_stage(1)
         prepare_second_group()
         pick(0, 0)
         pick(0, 1)
-        load_product(2)
         load_stage(2)
         for u in (1, 2):
             pick(u, 0)
             pick(u, 1)
         deal_w2_scales()
-        cap_product(3)
-        load_product(3)
-        gpsimd_slice(3)
+        whole_slice(3)
         nc.vector.quantize_mx(out=w1_w1[:].bitcast(FP8X4), scales=w1_s1[:], in_=w1_bf[:])
         deal_w2_words()
         pick(3, 0)
 
         cap_stage(4)
-        cap_product(5)
-        load_product(5)
-        load_product(4)
         load_stage(4)
         pick(3, 1)
         pick(4, 0)
-        gpsimd_slice(5)
-        maximum(picked0, z_bf[:])
+        whole_slice(5)
+        maximum(0, 0, PAIRS, z_bf0[:])
         pick(4, 1)
         pick(5, 0)
         pick(5, 1)
-        cap_product(6)
-        load_product(6)
-        gpsimd_slice(6)
+        whole_slice(6)
         pick(6, 0)
         pick(6, 1)
-        cap_product(7)
-        load_product(7)
-        gpsimd_slice(7)
+        whole_slice(7)
         pick(7, 0, 0, HALF)
         pick(7, 1, 0, HALF)
-        quantize_z(0, 0, z_bf[:, 0 : 4 * HALF])
+        quantize_z(0, 0, z_bf0[:, 0 : 4 * HALF])
 
         y = [tile([P, 2, 4, HALF], F32, "y%d" % s) for s in range(2)]
         y_bf = [tile([P, 2, 4 * HALF], BF16, "y_bf0", "z_bf11"), tile([P, 2, 4 * HALF], BF16, "y_bf1")]
@@ -419,14 +408,14 @@ def tile_list_flow_congestion_routing_kernel(
             nc.sync.dma_start(out=words[:, :, HALF * s : HALF * (s + 1)], in_=y_w[s][:])
 
         y_passes(0, 0)
-        maximum([picked1[i][:, :, 0:HALF] for i in range(2)], z_bf1[0])
+        maximum(1, 0, HALF, z_bf1[0])
         pick(7, 1, HALF, PAIRS)
         quantize_z(1, 0, z_bf1[0])
         y_passes(1, 0)
         pick(7, 0, HALF, PAIRS)
-        quantize_z(0, 1, z_bf[:, 4 * HALF : 8 * HALF])
+        quantize_z(0, 1, z_bf0[:, 4 * HALF : 8 * HALF])
         y_passes(0, 1)
-        maximum([picked1[i][:, :, HALF:PAIRS] for i in range(2)], z_bf1[1])
+        maximum(1, HALF, PAIRS, z_bf1[1])
         quantize_z(1, 1, z_bf1[1])
         for g in range(2):
             add_bias(0, g)

@@ -198,27 +198,25 @@ def tile_list_flow_congestion_routing_kernel(
 
         ring = [tile([P, S], F32, "h%d" % i) for i in range(H_RING)]
         h = [ring[u % H_RING][:] for u in range(SLICES)]
-        picked = [tile([P, 8 * PAIRS + HALF], F32, "picked0"), tile([P, 7 * PAIRS], F32, "picked1")]
+        picked = [tile([P, 8 * PAIRS + HALF], F32, "picked0"), tile([P, 8 * PAIRS], F32, "picked1")]
         slots = [
-            [picked[i][:, first * PAIRS : (first + 4) * PAIRS].rearrange("p (t j) -> p t j", t=4) for i, first in pair]
-            for pair in (((0, 0), (1, 0)), ((0, 4), (1, 3)))
+            [picked[i][:, 4 * PAIRS * b : 4 * PAIRS * (b + 1)].rearrange("p (t j) -> p t j", t=4) for i in range(2)]
+            for b in range(2)
         ]
-        h[6] = picked[0][:, 0:S]
+        h[5] = picked[0][:, 0:S]
         w1_bf1 = [w1_bf0[1], w1_bf0[0]]
         load_sb = {(u, s): tile([P, BANK], F32, "load_sb%d%d" % (u, s)) for u, s in ON_GPSIMD}
         damp = []
         for u in range(SLICES):
             if u in (1, 2):
                 damp.append([slots[0][i][:, u - 1, :] for i in range(2)])
-            elif u == 4:
-                damp.append([tile([P, BANK], F32, "damp4")[:], slots[0][1][:, 3, :]])
             else:
                 own = tile([P, S], F32, "damp%d" % u)
                 damp.append([own[:, BANK * s : BANK * (s + 1)] for s in range(2)])
         w1_w1 = tile([P, 2 * GROUP], U32, "w1_w1", "damp3")
         w1_w.append([w1_w1[:, GROUP * (1 - a) : GROUP * (2 - a)] for a in range(2)])
         w2_w = tile([P, 2, N], I32, "w2_w", "load_sb31")
-        z_bf0 = tile([P, 4 * PAIRS], BF16, "z_bf0", "damp5")
+        z_bf0 = tile([P, 4 * PAIRS], BF16, "z_bf0")
         z_bf1 = [picked[0][:, 8 * PAIRS - HALF :].bitcast(BF16), tile([P, 4 * HALF], BF16, "z_bf11")[:]]
         z_w = [
             [tile([P, HALF], U32, "z_w00", "load_sb70"), tile([P, HALF], U32, "z_w01", "h%d" % (7 % H_RING))],
@@ -353,19 +351,17 @@ def tile_list_flow_congestion_routing_kernel(
         nc.vector.quantize_mx(out=w1_w1[:].bitcast(FP8X4), scales=w1_s1[:], in_=w1_bf[:])
         deal_w2_words()
         pick(3, 0)
+        pick(3, 1)
+        maximum(0, 0, PAIRS, z_bf0[:])
 
         cap_stage(4)
         load_stage(4)
-        pick(3, 1)
         pick(4, 0)
-        whole_slice(5)
-        maximum(0, 0, PAIRS, z_bf0[:])
         pick(4, 1)
-        pick(5, 0)
-        pick(5, 1)
-        whole_slice(6)
-        pick(6, 0)
-        pick(6, 1)
+        for u in (5, 6):
+            whole_slice(u)
+            pick(u, 0)
+            pick(u, 1)
         whole_slice(7)
         pick(7, 0, 0, HALF)
         pick(7, 1, 0, HALF)

@@ -141,10 +141,11 @@ def tile_list_flow_congestion_routing_kernel(
                 in_=wcs_raw[:, :, GROUP * b : GROUP * (b + 1)].rearrange("p a (c i t) -> p a c t i", t=4, i=LINE),
             )
 
-        def deal_w2_words():
-            nc.vector.tensor_copy(
-                out=w2_w[:].rearrange("p b (g t c i) -> p (b g) c t i", g=2, t=4, i=LINE // 4),
-                in_=w2_raw[:].rearrange("p b (g c i t) -> p (b g) c t i", g=2, t=4, i=LINE // 4),
+        def deal_w2_words(b, g):
+            cols = slice(GROUP * g, GROUP * (g + 1))
+            nc.scalar.copy(
+                out=w2_w[:, b, cols].rearrange("p (t c i) -> p c t i", t=4, i=LINE // 4),
+                in_=w2_raw[:, b, cols].bitcast(U32).rearrange("p (c i t) -> p c t i", t=4, i=LINE // 4),
             )
 
         def deal_w2_scales():
@@ -215,7 +216,8 @@ def tile_list_flow_congestion_routing_kernel(
                 damp.append([own[:, BANK * s : BANK * (s + 1)] for s in range(2)])
         w1_w1 = tile([P, 2 * GROUP], U32, "w1_w1", "damp3")
         w1_w.append([w1_w1[:, GROUP * (1 - a) : GROUP * (2 - a)] for a in range(2)])
-        w2_w = tile([P, 2, N], I32, "w2_w", "load_sb31")
+        last_root = tile([P, BANK], F32, "last_root")
+        w2_w = tile([P, 2, N], U32, "w2_w", "last_root")
         z_bf0 = tile([P, 4 * PAIRS], BF16, "z_bf0")
         z_bf1 = [picked[0][:, 8 * PAIRS - HALF :].bitcast(BF16), tile([P, 4 * HALF], BF16, "z_bf11")[:]]
         z_w = [
@@ -257,14 +259,17 @@ def tile_list_flow_congestion_routing_kernel(
                 load_bank, u, lambda a: w1_w[b][a][:, cols].bitcast(FP8X4), lambda a: w1_s[b][a][:, cols], (1, 0)
             )
 
+        def root_of(u, s):
+            return last_root[:] if (u, s) == (SLICES - 1, 1) else damp[u][s]
+
         def magnitude(u, s):
-            nc.scalar.activation(out=damp[u][s], in_=cap_bank(u, s)[:], func=ACT.Abs)
+            nc.scalar.activation(out=root_of(u, s), in_=cap_bank(u, s)[:], func=ACT.Abs)
 
         def inverse_root(u, s):
-            nc.scalar.activation(out=damp[u][s], in_=damp[u][s], func=ACT.Abs_reciprocal_sqrt, bias=1.0)
+            nc.scalar.activation(out=root_of(u, s), in_=root_of(u, s), func=ACT.Abs_reciprocal_sqrt, bias=1.0)
 
         def square(u, s):
-            nc.scalar.activation(out=damp[u][s], in_=damp[u][s], func=ACT.Square)
+            nc.scalar.activation(out=damp[u][s], in_=root_of(u, s), func=ACT.Square)
 
         def cap_stage(u):
             cap_product(u)
@@ -349,7 +354,6 @@ def tile_list_flow_congestion_routing_kernel(
         deal_w2_scales()
         whole_slice(3)
         nc.vector.quantize_mx(out=w1_w1[:].bitcast(FP8X4), scales=w1_s1[:], in_=w1_bf[:])
-        deal_w2_words()
         pick(3, 0)
         pick(3, 1)
         maximum(0, 0, PAIRS, z_bf0[:])
@@ -363,6 +367,9 @@ def tile_list_flow_congestion_routing_kernel(
             pick(u, 0)
             pick(u, 1)
         whole_slice(7)
+        for b in range(2):
+            for g in range(2):
+                deal_w2_words(b, g)
         pick(7, 0, 0, HALF)
         pick(7, 1, 0, HALF)
         quantize_z(0, 0, z_bf0[:, 0 : 4 * HALF])

@@ -24,6 +24,7 @@ BANK = 512
 HALF = PAIRS // 2
 SLICES = H // P
 AHEAD = 3
+QUARTER = BANK // 2
 H_RING = 4
 QUADRANTS = (0, 2, 1, 3)
 ON_GPSIMD = ((3, 0), (3, 1), (5, 0), (5, 1), (6, 0), (6, 1), (7, 0))
@@ -125,12 +126,12 @@ def tile_list_flow_congestion_routing_kernel(
         load_table(1)
         load_wc(1)
 
-        def gather_words(a, s):
-            entries = offs_sb[:, BANK // 16 * s : BANK // 16 * (s + 1)]
-            nc.vector.tensor_copy(v_w[a][s][:], tab_w[a][:].bitcast(U32).indirect(entries))
+        def gather_words(a, s, lo=0, hi=BANK):
+            entries = offs_sb[:, (BANK * s + lo) // 16 : (BANK * s + hi) // 16]
+            nc.vector.tensor_copy(v_w[a][s][:, lo:hi], tab_w[a][:].bitcast(U32).indirect(entries))
 
-        def deal_wc_words(b):
-            nc.vector.tensor_copy(
+        def deal_wc_words(copy, b):
+            copy(
                 out=wc_w[b][:].rearrange("p a (t c i) -> p a c t i", t=4, i=LINE // 2),
                 in_=wc_raw[b][:].bitcast(U16).rearrange("p a (c i t) -> p a c t i", t=4, i=LINE // 2),
             )
@@ -180,15 +181,16 @@ def tile_list_flow_congestion_routing_kernel(
             out=w2s_raw[0 : 2 * QUAD, :].bitcast(I32),
             in_=w2_scales.rearrange("b q (g c) -> (q g) b c", g=2).bitcast(I32),
         )
-        deal_wc_words(0)
+        deal_wc_words(nc.vector.tensor_copy, 0)
         deal_wc_scales(0)
         gather_words(0, 0)
         gather_words(0, 1)
         load_w1(1, 0)
         deal_wc_scales(1)
-        gather_words(1, 0)
+        gather_words(1, 0, 0, QUARTER)
+        gather_words(1, 0, QUARTER, BANK)
         gather_words(1, 1)
-        deal_wc_words(1)
+        deal_wc_words(nc.scalar.copy, 1)
         load_w1(1, 1)
         round_w1(nc.vector.tensor_copy, w1_bf0[0], w1_raw[0][0], 0, GROUP)
         round_w1(nc.vector.tensor_copy, w1_bf0[1], w1_raw[0][1], 0, GROUP // 2)
@@ -208,8 +210,12 @@ def tile_list_flow_congestion_routing_kernel(
         w1_bf1 = [w1_bf0[1], w1_bf0[0]]
         load_sb = {(u, s): tile([P, BANK], F32, "load_sb%d%d" % (u, s)) for u, s in ON_GPSIMD}
         damp = []
+        root4 = tile([P, S], F32, "root4")
+        damp4 = tile([P, S], F32, "damp4", "w1_bf")
         for u in range(SLICES):
-            if u in (1, 2):
+            if u == 4:
+                damp.append([damp4[:, BANK * s : BANK * (s + 1)] for s in range(2)])
+            elif u in (1, 2):
                 damp.append([slots[0][i][:, u - 1, :] for i in range(2)])
             else:
                 own = tile([P, S], F32, "damp%d" % u)
@@ -218,7 +224,7 @@ def tile_list_flow_congestion_routing_kernel(
         w1_w.append([w1_w1[:, GROUP * (1 - a) : GROUP * (2 - a)] for a in range(2)])
         last_root = tile([P, BANK], F32, "last_root")
         w2_w = tile([P, 2, N], U32, "w2_w", "last_root")
-        z_bf0 = tile([P, 4 * PAIRS], BF16, "z_bf0")
+        z_bf0 = tile([P, 4 * PAIRS], BF16, "z_bf0", "root4")
         z_bf1 = [picked[0][:, 8 * PAIRS - HALF :].bitcast(BF16), tile([P, 4 * HALF], BF16, "z_bf11")[:]]
         z_w = [
             [tile([P, HALF], U32, "z_w00", "load_sb70"), tile([P, HALF], U32, "z_w01", "h%d" % (7 % H_RING))],
@@ -255,11 +261,14 @@ def tile_list_flow_congestion_routing_kernel(
         def load_product(u):
             b, t = divmod(u, 4)
             cols = slice(P * t, P * (t + 1))
+            order = (0, 1) if u == 0 else (1, 0)
             first_product(
-                load_bank, u, lambda a: w1_w[b][a][:, cols].bitcast(FP8X4), lambda a: w1_s[b][a][:, cols], (1, 0)
+                load_bank, u, lambda a: w1_w[b][a][:, cols].bitcast(FP8X4), lambda a: w1_s[b][a][:, cols], order
             )
 
         def root_of(u, s):
+            if u == 4:
+                return root4[:, BANK * s : BANK * (s + 1)]
             return last_root[:] if (u, s) == (SLICES - 1, 1) else damp[u][s]
 
         def magnitude(u, s):
@@ -276,6 +285,36 @@ def tile_list_flow_congestion_routing_kernel(
             for step in (magnitude, inverse_root, square):
                 for s in range(2):
                     step(u, s)
+
+        def cap_stage_square_on_gpsimd(u):
+            cap_product(u)
+            for step in (magnitude, inverse_root):
+                for s in range(2):
+                    step(u, s)
+            nc.gpsimd.tensor_tensor(out=damp4[:], in0=root4[:], in1=root4[:], op=ALU.mult)
+
+        def first_cap_stage():
+            parts = (
+                (load_bank(0, 0)[:, 0:QUARTER], 0, 0, QUARTER),
+                (cap_bank(0, 0)[:, 0:QUARTER], 0, QUARTER, BANK),
+                (cap_bank(0, 1)[:], 1, 0, BANK),
+            )
+            for bank, s, lo, hi in parts:
+                for a in range(2):
+                    nc.tensor.matmul_mx(
+                        out=bank,
+                        lhsT=wc_w[0][:, a, 0:P].bitcast(FP4X4),
+                        lhsT_scale=wc_s[:, 0, a, 0:P],
+                        rhs=v_w[a][s][:, lo:hi].bitcast(FP8X4),
+                        rhs_scale=v_s[:, a, BANK * s + lo : BANK * s + hi],
+                        start=(a == 0),
+                        stop=(a == 1),
+                    )
+            for bank, s, lo, hi in parts:
+                part = damp[0][s][:, lo:hi]
+                nc.scalar.activation(out=part, in_=bank, func=ACT.Abs)
+                nc.scalar.activation(out=part, in_=part, func=ACT.Abs_reciprocal_sqrt, bias=1.0)
+                nc.scalar.activation(out=part, in_=part, func=ACT.Square)
 
         def multiply(u, s):
             half = h[u][:, BANK * s : BANK * (s + 1)]
@@ -340,7 +379,8 @@ def tile_list_flow_congestion_routing_kernel(
             nc.sync.dma_start(out=w2_raw[:], in_=w2_words.rearrange("b p n i -> p b (n i)").bitcast(I32))
             nc.sync.dma_start(out=bias[:], in_=b2.rearrange("(g p t) -> p g t", g=2, t=4))
 
-        for u in range(AHEAD):
+        first_cap_stage()
+        for u in range(1, AHEAD):
             cap_stage(u)
         load_stage(0)
         load_stage(1)
@@ -356,9 +396,9 @@ def tile_list_flow_congestion_routing_kernel(
         nc.vector.quantize_mx(out=w1_w1[:].bitcast(FP8X4), scales=w1_s1[:], in_=w1_bf[:])
         pick(3, 0)
         pick(3, 1)
+        cap_stage_square_on_gpsimd(4)
         maximum(0, 0, PAIRS, z_bf0[:])
 
-        cap_stage(4)
         load_stage(4)
         pick(4, 0)
         pick(4, 1)

@@ -28,12 +28,13 @@ QUARTER = BANK // 2
 H_RING = 4
 QUADRANTS = (0, 2, 1, 3)
 ON_GPSIMD = ((3, 0), (3, 1), (5, 0), (5, 1), (6, 0), (6, 1), (7, 0))
-ROUND_PIECES = 4
+ROUND_PIECES = 1
 Y_BANKS = (0, 1, 3, 2)
 W1_FIRST_AT = 0
 WC_SECOND_AT = W1_FIRST_AT + 4 * 4 * GROUP
 TAB_SECOND_AT = WC_SECOND_AT + 4 * GROUP
 TAB_SCALES_AT = WC_SECOND_AT - 2 * GROUP
+TAB_FIRST_AT = TAB_SECOND_AT + 4 * T
 
 
 def tile_list_flow_congestion_routing_kernel(
@@ -57,7 +58,7 @@ def tile_list_flow_congestion_routing_kernel(
         banks = [ps.tile([P, BANK], F32, name="bank%d" % i) for i in range(8)]
 
         tab_s = placed([P, T], U8, "tab_s", TAB_SCALES_AT)
-        tab_w = [tile([P, T], I32, "tab_w0", "stage1"), placed([P, T], I32, "tab_w1", TAB_SECOND_AT)]
+        tab_w = [placed([P, T], I32, "tab_w0", TAB_FIRST_AT), placed([P, T], I32, "tab_w1", TAB_SECOND_AT)]
         picked_s = tile([P, S], U8, "picked_s")
         v_w = [[tile([P, BANK], U32, "v_w%d%d" % (a, s)) for s in range(2)] for a in range(2)]
         v_s = tile([P, 2, S], U8, "v_s")
@@ -70,7 +71,10 @@ def tile_list_flow_congestion_routing_kernel(
         wc_s = tile([P, 2, 2, GROUP], U8, "wc_s")
         w1_raw = [
             [placed([P, 4, GROUP], F32, "w1_raw00", W1_FIRST_AT), tile([P, 4, GROUP], F32, "w1_raw01", "wc_raw")],
-            [tile([P, 4, GROUP], F32, "w1_raw10", "stage1"), placed([P, 4, GROUP], F32, "w1_raw11", TAB_SECOND_AT)],
+            [
+                placed([P, 4, GROUP], F32, "w1_raw10", TAB_FIRST_AT),
+                placed([P, 4, GROUP], F32, "w1_raw11", TAB_SECOND_AT),
+            ],
         ]
         w1_bf = tile([P, 8 * GROUP], BF16, "w1_bf")
         w1_bf0 = [w1_bf[:, 4 * GROUP * a : 4 * GROUP * (a + 1)] for a in range(2)]
@@ -82,7 +86,7 @@ def tile_list_flow_congestion_routing_kernel(
         ]
         w2_raw = tile([P, 2, N], I32, "w2_raw", "wc_raw")
         w2s_raw = tile([P, GROUP], U8, "w2s_raw")
-        w2s_dealt = placed([P, GROUP], U8, "w2s_dealt", W1_FIRST_AT + 64)
+        w2s_dealt = placed([P, GROUP], U8, "w2s_dealt", TAB_FIRST_AT + 4 * 4 * GROUP)
         w2_s = wcs_raw[:].rearrange("p g (b c) -> p g b c", b=2)
         bias = placed([P, 2, 4], F32, "bias", W1_FIRST_AT)
 
@@ -94,6 +98,10 @@ def tile_list_flow_congestion_routing_kernel(
         nc.vector.memset(tab_s[2 * QUAD : P, :].bitcast(I32), 0)
         nc.gpsimd.memset(v_s[:].bitcast(I32), 0)
         nc.gpsimd.memset(w2s_raw[2 * QUAD : P, :].bitcast(I32), 0)
+        nc.gpsimd.dma_start(
+            out=w2s_raw[0 : 2 * QUAD, :].bitcast(I32),
+            in_=w2_scales.rearrange("b q (g c) -> (q g) b c", g=2).bitcast(I32),
+        )
 
         def load_table(a):
             nc.sync.dma_start(out=tab_w[a][:], in_=tab_words[a].rearrange("p t i -> p (t i)").bitcast(I32))
@@ -155,7 +163,7 @@ def tile_list_flow_congestion_routing_kernel(
                 in_=w2s_raw[:].rearrange("p (c i t) -> p c t i", t=4, i=LINE),
             )
             for q in QUADRANTS:
-                nc.sync.dma_start(
+                nc.gpsimd.dma_start(
                     out=w2_s[QUAD * q : QUAD * q + 4, :, :, :].rearrange("r g b c -> r (g b c)").bitcast(I32),
                     in_=w2s_dealt[16 * q : 16 * q + 16, :].bitcast(I32),
                 )
@@ -177,16 +185,13 @@ def tile_list_flow_congestion_routing_kernel(
         load_w1(0, 0)
         load_w1(0, 1, 0, GROUP // 2)
         load_w1(0, 1, GROUP // 2, GROUP)
-        nc.sync.dma_start(
-            out=w2s_raw[0 : 2 * QUAD, :].bitcast(I32),
-            in_=w2_scales.rearrange("b q (g c) -> (q g) b c", g=2).bitcast(I32),
-        )
         deal_wc_words(nc.vector.tensor_copy, 0)
         deal_wc_scales(0)
         gather_words(0, 0)
         gather_words(0, 1)
         load_w1(1, 0)
         deal_wc_scales(1)
+        deal_w2_scales()
         gather_words(1, 0, 0, QUARTER)
         gather_words(1, 0, QUARTER, BANK)
         gather_words(1, 1)
@@ -331,7 +336,8 @@ def tile_list_flow_congestion_routing_kernel(
 
         def whole_slice(u):
             cap_product(u)
-            load_product(u)
+            if u != 5:
+                load_product(u)
             for step in (magnitude, inverse_root):
                 for s in range(2):
                     step(u, s)
@@ -391,7 +397,6 @@ def tile_list_flow_congestion_routing_kernel(
         for u in (1, 2):
             pick(u, 0)
             pick(u, 1)
-        deal_w2_scales()
         whole_slice(3)
         nc.vector.quantize_mx(out=w1_w1[:].bitcast(FP8X4), scales=w1_s1[:], in_=w1_bf[:])
         pick(3, 0)
@@ -399,6 +404,7 @@ def tile_list_flow_congestion_routing_kernel(
         cap_stage_square_on_gpsimd(4)
         maximum(0, 0, PAIRS, z_bf0[:])
 
+        load_product(5)
         load_stage(4)
         pick(4, 0)
         pick(4, 1)

@@ -28,13 +28,13 @@ QUARTER = BANK // 2
 H_RING = 4
 QUADRANTS = (0, 2, 1, 3)
 ON_GPSIMD = ((3, 0), (3, 1), (5, 0), (5, 1), (6, 0), (6, 1), (7, 0))
-ROUND_PIECES = 1
 Y_BANKS = (0, 1, 3, 2)
 W1_FIRST_AT = 0
 WC_SECOND_AT = W1_FIRST_AT + 4 * 4 * GROUP
 TAB_SECOND_AT = WC_SECOND_AT + 4 * GROUP
 TAB_SCALES_AT = WC_SECOND_AT - 2 * GROUP
 TAB_FIRST_AT = TAB_SECOND_AT + 4 * T
+W2_SCALES_AT = TAB_FIRST_AT + 4 * 4 * GROUP
 
 
 def tile_list_flow_congestion_routing_kernel(
@@ -86,7 +86,7 @@ def tile_list_flow_congestion_routing_kernel(
         ]
         w2_raw = tile([P, 2, N], I32, "w2_raw", "wc_raw")
         w2s_raw = tile([P, GROUP], U8, "w2s_raw")
-        w2s_dealt = placed([P, GROUP], U8, "w2s_dealt", TAB_FIRST_AT + 4 * 4 * GROUP)
+        w2s_dealt = placed([P, GROUP], U8, "w2s_dealt", W2_SCALES_AT)
         w2_s = wcs_raw[:].rearrange("p g (b c) -> p g b c", b=2)
         bias = placed([P, 2, 4], F32, "bias", W1_FIRST_AT)
 
@@ -215,12 +215,8 @@ def tile_list_flow_congestion_routing_kernel(
         w1_bf1 = [w1_bf0[1], w1_bf0[0]]
         load_sb = {(u, s): tile([P, BANK], F32, "load_sb%d%d" % (u, s)) for u, s in ON_GPSIMD}
         damp = []
-        root4 = tile([P, S], F32, "root4")
-        damp4 = tile([P, S], F32, "damp4", "w1_bf")
         for u in range(SLICES):
-            if u == 4:
-                damp.append([damp4[:, BANK * s : BANK * (s + 1)] for s in range(2)])
-            elif u in (1, 2):
+            if u in (1, 2):
                 damp.append([slots[0][i][:, u - 1, :] for i in range(2)])
             else:
                 own = tile([P, S], F32, "damp%d" % u)
@@ -229,7 +225,7 @@ def tile_list_flow_congestion_routing_kernel(
         w1_w.append([w1_w1[:, GROUP * (1 - a) : GROUP * (2 - a)] for a in range(2)])
         last_root = tile([P, BANK], F32, "last_root")
         w2_w = tile([P, 2, N], U32, "w2_w", "last_root")
-        z_bf0 = tile([P, 4 * PAIRS], BF16, "z_bf0", "root4")
+        z_bf0 = tile([P, 4 * PAIRS], BF16, "z_bf0")
         z_bf1 = [picked[0][:, 8 * PAIRS - HALF :].bitcast(BF16), tile([P, 4 * HALF], BF16, "z_bf11")[:]]
         z_w = [
             [tile([P, HALF], U32, "z_w00", "load_sb70"), tile([P, HALF], U32, "z_w01", "h%d" % (7 % H_RING))],
@@ -272,8 +268,6 @@ def tile_list_flow_congestion_routing_kernel(
             )
 
         def root_of(u, s):
-            if u == 4:
-                return root4[:, BANK * s : BANK * (s + 1)]
             return last_root[:] if (u, s) == (SLICES - 1, 1) else damp[u][s]
 
         def magnitude(u, s):
@@ -290,13 +284,6 @@ def tile_list_flow_congestion_routing_kernel(
             for step in (magnitude, inverse_root, square):
                 for s in range(2):
                     step(u, s)
-
-        def cap_stage_square_on_gpsimd(u):
-            cap_product(u)
-            for step in (magnitude, inverse_root):
-                for s in range(2):
-                    step(u, s)
-            nc.gpsimd.tensor_tensor(out=damp4[:], in0=root4[:], in1=root4[:], op=ALU.mult)
 
         def first_cap_stage():
             parts = (
@@ -334,16 +321,18 @@ def tile_list_flow_congestion_routing_kernel(
             for s in range(2):
                 multiply(u, s)
 
-        def whole_slice(u):
-            cap_product(u)
-            if u != 5:
-                load_product(u)
+        def finish_slice(u):
             for step in (magnitude, inverse_root):
                 for s in range(2):
                     step(u, s)
             for s in range(2):
                 square(u, s)
                 multiply(u, s)
+
+        def whole_slice(u):
+            cap_product(u)
+            load_product(u)
+            finish_slice(u)
 
         def pick(u, i, lo=0, hi=PAIRS):
             b, t = divmod(u, 4)
@@ -378,10 +367,8 @@ def tile_list_flow_congestion_routing_kernel(
                     )
 
         def prepare_second_group():
-            width = GROUP // ROUND_PIECES
             for a in range(2):
-                for lo in range(0, GROUP, width):
-                    round_w1(gpsimd_copy, w1_bf1[a], w1_raw[1][a], lo, lo + width)
+                round_w1(gpsimd_copy, w1_bf1[a], w1_raw[1][a], 0, GROUP)
             nc.sync.dma_start(out=w2_raw[:], in_=w2_words.rearrange("b p n i -> p b (n i)").bitcast(I32))
             nc.sync.dma_start(out=bias[:], in_=b2.rearrange("(g p t) -> p g t", g=2, t=4))
 
@@ -401,17 +388,20 @@ def tile_list_flow_congestion_routing_kernel(
         nc.vector.quantize_mx(out=w1_w1[:].bitcast(FP8X4), scales=w1_s1[:], in_=w1_bf[:])
         pick(3, 0)
         pick(3, 1)
-        cap_stage_square_on_gpsimd(4)
+        cap_stage(4)
         maximum(0, 0, PAIRS, z_bf0[:])
 
         load_product(5)
         load_stage(4)
         pick(4, 0)
         pick(4, 1)
-        for u in (5, 6):
-            whole_slice(u)
-            pick(u, 0)
-            pick(u, 1)
+        cap_product(5)
+        finish_slice(5)
+        pick(5, 0)
+        pick(5, 1)
+        whole_slice(6)
+        pick(6, 0)
+        pick(6, 1)
         whole_slice(7)
         for b in range(2):
             for g in range(2):

@@ -87,7 +87,7 @@ def tile_list_flow_congestion_routing_kernel(
         w2_raw = tile([P, 2, N], I32, "w2_raw", "wc_raw")
         w2s_raw = tile([P, GROUP], U8, "w2s_raw")
         w2s_dealt = placed([P, GROUP], U8, "w2s_dealt", W2_SCALES_AT)
-        w2_s = wcs_raw[:].rearrange("p g (b c) -> p g b c", b=2)
+        w2_s = wc_s
         bias = placed([P, 2, 4], F32, "bias", W1_FIRST_AT)
 
         warm = tile([P, 2], F32, "warm")
@@ -162,8 +162,10 @@ def tile_list_flow_congestion_routing_kernel(
                 out=w2s_dealt[:].rearrange("p (t c i) -> p c t i", t=4, i=LINE),
                 in_=w2s_raw[:].rearrange("p (c i t) -> p c t i", t=4, i=LINE),
             )
+
+        def move_w2_scales():
             for q in QUADRANTS:
-                nc.gpsimd.dma_start(
+                nc.sync.dma_start(
                     out=w2_s[QUAD * q : QUAD * q + 4, :, :, :].rearrange("r g b c -> r (g b c)").bitcast(I32),
                     in_=w2s_dealt[16 * q : 16 * q + 16, :].bitcast(I32),
                 )
@@ -172,6 +174,12 @@ def tile_list_flow_congestion_routing_kernel(
             copy(
                 out=rounded.rearrange("p (t m j) -> p m t j", t=4, j=4)[:, lo // 4 : hi // 4, :, :],
                 in_=raw[:, :, lo:hi].rearrange("p j (m t) -> p m t j", t=4),
+            )
+
+        def round_w1_by_lines(rounded, raw, lo, hi):
+            nc.vector.tensor_copy(
+                out=rounded.rearrange("p (t m j) -> p m j t", t=4, j=4)[:, lo // 4 : hi // 4, :, :],
+                in_=raw[:, :, lo:hi].rearrange("p j (m t) -> p m j t", t=4),
             )
 
         def gpsimd_copy(out, in_):
@@ -197,10 +205,10 @@ def tile_list_flow_congestion_routing_kernel(
         gather_words(1, 1)
         deal_wc_words(nc.scalar.copy, 1)
         load_w1(1, 1)
-        round_w1(nc.vector.tensor_copy, w1_bf0[0], w1_raw[0][0], 0, GROUP)
-        round_w1(nc.vector.tensor_copy, w1_bf0[1], w1_raw[0][1], 0, GROUP // 2)
+        round_w1_by_lines(w1_bf0[0], w1_raw[0][0], 0, GROUP)
+        round_w1_by_lines(w1_bf0[1], w1_raw[0][1], 0, GROUP // 2)
         quantize_w1(0, 0, w1_bf0[0], 0, GROUP)
-        round_w1(nc.vector.tensor_copy, w1_bf0[1], w1_raw[0][1], GROUP // 2, GROUP)
+        round_w1_by_lines(w1_bf0[1], w1_raw[0][1], GROUP // 2, GROUP)
         quantize_w1(0, 1, w1_bf0[1], 0, GROUP // 2)
         quantize_w1(0, 1, w1_bf0[1], GROUP // 2, GROUP)
 
@@ -403,6 +411,7 @@ def tile_list_flow_congestion_routing_kernel(
         pick(6, 0)
         pick(6, 1)
         whole_slice(7)
+        move_w2_scales()
         for b in range(2):
             for g in range(2):
                 deal_w2_words(b, g)

@@ -27,8 +27,8 @@ AHEAD = 3
 QUARTER = BANK // 2
 H_RING = 4
 QUADRANTS = (0, 2, 1, 3)
-ON_GPSIMD = ((3, 0), (3, 1), (5, 0), (5, 1), (6, 0), (6, 1), (7, 0))
-Y_BANKS = (0, 1, 3, 2)
+ON_GPSIMD = ((3, 0), (5, 0), (5, 1), (6, 0), (6, 1), (7, 0), (7, 1))
+Y_BANKS = (3, 1, 0, 2)
 W1_FIRST_AT = 0
 WC_SECOND_AT = W1_FIRST_AT + 4 * 4 * GROUP
 TAB_SECOND_AT = WC_SECOND_AT + 4 * GROUP
@@ -64,7 +64,6 @@ def tile_list_flow_congestion_routing_kernel(
         v_s = tile([P, 2, S], U8, "v_s")
         wc_raw = [
             tile([P, 2, GROUP // 2], I32, "wc_raw0", "wc_raw"),
-            placed([P, 2, GROUP // 2], I32, "wc_raw1", WC_SECOND_AT),
         ]
         wcs_raw = tile([P, 2, H], U8, "wcs_raw")
         wc_w = [tile([P, 2, GROUP], U16, "wc_w%d" % b) for b in range(2)]
@@ -132,7 +131,6 @@ def tile_list_flow_congestion_routing_kernel(
                 out=v_s[QUAD * q : QUAD * q + 4, :, :].bitcast(I32), in_=picked_s[8 * q : 8 * q + 8, :].bitcast(I32)
             )
         load_table(1)
-        load_wc(1)
 
         def gather_words(a, s, lo=0, hi=BANK):
             entries = offs_sb[:, (BANK * s + lo) // 16 : (BANK * s + hi) // 16]
@@ -193,6 +191,8 @@ def tile_list_flow_congestion_routing_kernel(
         load_w1(0, 0)
         load_w1(0, 1, 0, GROUP // 2)
         load_w1(0, 1, GROUP // 2, GROUP)
+        wc_raw.append(tile([P, 2, GROUP // 2], I32, "wc_raw1", "picked_s"))
+        load_wc(1)
         deal_wc_words(nc.vector.tensor_copy, 0)
         deal_wc_scales(0)
         gather_words(0, 0)
@@ -203,14 +203,17 @@ def tile_list_flow_congestion_routing_kernel(
         gather_words(1, 0, 0, QUARTER)
         gather_words(1, 0, QUARTER, BANK)
         gather_words(1, 1)
-        deal_wc_words(nc.scalar.copy, 1)
         load_w1(1, 1)
         round_w1_by_lines(w1_bf0[0], w1_raw[0][0], 0, GROUP)
         round_w1_by_lines(w1_bf0[1], w1_raw[0][1], 0, GROUP // 2)
         quantize_w1(0, 0, w1_bf0[0], 0, GROUP)
         round_w1_by_lines(w1_bf0[1], w1_raw[0][1], GROUP // 2, GROUP)
         quantize_w1(0, 1, w1_bf0[1], 0, GROUP // 2)
-        quantize_w1(0, 1, w1_bf0[1], GROUP // 2, GROUP)
+        deal_wc_words(nc.vector.tensor_copy, 1)
+        w1_last = tile([P, GROUP // 2], U32, "w1_last", "picked_s")
+        nc.vector.quantize_mx(
+            out=w1_last[:].bitcast(FP8X4), scales=w1_s[0][1][:, GROUP // 2 :], in_=w1_bf0[1][:, 2 * GROUP :]
+        )
 
         ring = [tile([P, S], F32, "h%d" % i) for i in range(H_RING)]
         h = [ring[u % H_RING][:] for u in range(SLICES)]
@@ -226,6 +229,8 @@ def tile_list_flow_congestion_routing_kernel(
         for u in range(SLICES):
             if u in (1, 2):
                 damp.append([slots[0][i][:, u - 1, :] for i in range(2)])
+            elif u == 4:
+                damp.append([w1_bf[:, 2 * BANK * s : 2 * BANK * (s + 1)].bitcast(F32) for s in range(2)])
             else:
                 own = tile([P, S], F32, "damp%d" % u)
                 damp.append([own[:, BANK * s : BANK * (s + 1)] for s in range(2)])
@@ -233,16 +238,15 @@ def tile_list_flow_congestion_routing_kernel(
         w1_w.append([w1_w1[:, GROUP * (1 - a) : GROUP * (2 - a)] for a in range(2)])
         last_root = tile([P, BANK], F32, "last_root")
         w2_w = tile([P, 2, N], U32, "w2_w", "last_root")
-        z_bf0 = tile([P, 4 * PAIRS], BF16, "z_bf0")
         z_bf1 = [picked[0][:, 8 * PAIRS - HALF :].bitcast(BF16), tile([P, 4 * HALF], BF16, "z_bf11")[:]]
         z_w = [
-            [tile([P, HALF], U32, "z_w00", "load_sb70"), tile([P, HALF], U32, "z_w01", "h%d" % (7 % H_RING))],
+            [tile([P, HALF], U32, "z_w00", "load_sb71"), tile([P, HALF], U32, "z_w01", "h%d" % (7 % H_RING))],
             [tile([P, HALF], U32, "z_w1%d" % s) for s in range(2)],
         ]
         z_s = [[tile([P, HALF], U8, "z_s%d%d" % (b, s)) for s in range(2)] for b in range(2)]
 
         def cap_bank(u, s):
-            return banks[2 * (u % 4) + s]
+            return banks[2 * (u % 4 if u < SLICES - 1 else 0) + s]
 
         def load_bank(u, s):
             return banks[2 * ((u - 1) % 4) + s]
@@ -271,9 +275,13 @@ def tile_list_flow_congestion_routing_kernel(
             b, t = divmod(u, 4)
             cols = slice(P * t, P * (t + 1))
             order = (0, 1) if u == 0 else (1, 0)
-            first_product(
-                load_bank, u, lambda a: w1_w[b][a][:, cols].bitcast(FP8X4), lambda a: w1_s[b][a][:, cols], order
-            )
+
+            def words(a):
+                if (b, a) == (0, 1) and t >= 2:
+                    return w1_last[:, P * (t - 2) : P * (t - 1)].bitcast(FP8X4)
+                return w1_w[b][a][:, cols].bitcast(FP8X4)
+
+            first_product(load_bank, u, words, lambda a: w1_s[b][a][:, cols], order)
 
         def root_of(u, s):
             return last_root[:] if (u, s) == (SLICES - 1, 1) else damp[u][s]
@@ -292,6 +300,15 @@ def tile_list_flow_congestion_routing_kernel(
             for step in (magnitude, inverse_root, square):
                 for s in range(2):
                     step(u, s)
+
+        def gpsimd_squares(u, root):
+            halves = [root[:, BANK * s : BANK * (s + 1)] for s in range(2)]
+            for s in range(2):
+                nc.scalar.activation(out=halves[s], in_=cap_bank(u, s)[:], func=ACT.Abs)
+            for s in range(2):
+                nc.scalar.activation(out=halves[s], in_=halves[s], func=ACT.Abs_reciprocal_sqrt, bias=1.0)
+            for s in range(2):
+                nc.gpsimd.tensor_tensor(out=damp[u][s], in0=halves[s], in1=halves[s], op=ALU.mult)
 
         def first_cap_stage():
             parts = (
@@ -396,7 +413,10 @@ def tile_list_flow_congestion_routing_kernel(
         nc.vector.quantize_mx(out=w1_w1[:].bitcast(FP8X4), scales=w1_s1[:], in_=w1_bf[:])
         pick(3, 0)
         pick(3, 1)
-        cap_stage(4)
+        cap_product(4)
+        root4 = tile([P, S], F32, "root4")
+        gpsimd_squares(4, root4)
+        z_bf0 = tile([P, 4 * PAIRS], BF16, "z_bf0", "root4")
         maximum(0, 0, PAIRS, z_bf0[:])
 
         load_product(5)

@@ -27,7 +27,7 @@ AHEAD = 3
 QUARTER = BANK // 2
 H_RING = 4
 QUADRANTS = (0, 2, 1, 3)
-ON_GPSIMD = ((3, 0), (5, 0), (5, 1), (6, 0), (6, 1), (7, 0), (7, 1))
+ON_GPSIMD = ((3, 0), (3, 1), (5, 0), (5, 1), (6, 0), (6, 1), (7, 0))
 Y_BANKS = (3, 1, 0, 2)
 W1_FIRST_AT = 0
 WC_SECOND_AT = W1_FIRST_AT + 4 * 4 * GROUP
@@ -229,8 +229,6 @@ def tile_list_flow_congestion_routing_kernel(
         for u in range(SLICES):
             if u in (1, 2):
                 damp.append([slots[0][i][:, u - 1, :] for i in range(2)])
-            elif u == 4:
-                damp.append([w1_bf[:, 2 * BANK * s : 2 * BANK * (s + 1)].bitcast(F32) for s in range(2)])
             else:
                 own = tile([P, S], F32, "damp%d" % u)
                 damp.append([own[:, BANK * s : BANK * (s + 1)] for s in range(2)])
@@ -240,7 +238,7 @@ def tile_list_flow_congestion_routing_kernel(
         w2_w = tile([P, 2, N], U32, "w2_w", "last_root")
         z_bf1 = [picked[0][:, 8 * PAIRS - HALF :].bitcast(BF16), tile([P, 4 * HALF], BF16, "z_bf11")[:]]
         z_w = [
-            [tile([P, HALF], U32, "z_w00", "load_sb71"), tile([P, HALF], U32, "z_w01", "h%d" % (7 % H_RING))],
+            [tile([P, HALF], U32, "z_w00", "load_sb70"), tile([P, HALF], U32, "z_w01", "h%d" % (7 % H_RING))],
             [tile([P, HALF], U32, "z_w1%d" % s) for s in range(2)],
         ]
         z_s = [[tile([P, HALF], U8, "z_s%d%d" % (b, s)) for s in range(2)] for b in range(2)]
@@ -300,15 +298,6 @@ def tile_list_flow_congestion_routing_kernel(
             for step in (magnitude, inverse_root, square):
                 for s in range(2):
                     step(u, s)
-
-        def gpsimd_squares(u, root):
-            halves = [root[:, BANK * s : BANK * (s + 1)] for s in range(2)]
-            for s in range(2):
-                nc.scalar.activation(out=halves[s], in_=cap_bank(u, s)[:], func=ACT.Abs)
-            for s in range(2):
-                nc.scalar.activation(out=halves[s], in_=halves[s], func=ACT.Abs_reciprocal_sqrt, bias=1.0)
-            for s in range(2):
-                nc.gpsimd.tensor_tensor(out=damp[u][s], in0=halves[s], in1=halves[s], op=ALU.mult)
 
         def first_cap_stage():
             parts = (
@@ -413,10 +402,8 @@ def tile_list_flow_congestion_routing_kernel(
         nc.vector.quantize_mx(out=w1_w1[:].bitcast(FP8X4), scales=w1_s1[:], in_=w1_bf[:])
         pick(3, 0)
         pick(3, 1)
-        cap_product(4)
-        root4 = tile([P, S], F32, "root4")
-        gpsimd_squares(4, root4)
-        z_bf0 = tile([P, 4 * PAIRS], BF16, "z_bf0", "root4")
+        cap_stage(4)
+        z_bf0 = tile([P, 4 * PAIRS], BF16, "z_bf0")
         maximum(0, 0, PAIRS, z_bf0[:])
 
         load_product(5)

@@ -65,7 +65,7 @@ def tile_list_flow_congestion_routing_kernel(
         wc_raw = [
             tile([P, 2, GROUP // 2], I32, "wc_raw0", "wc_raw"),
         ]
-        wcs_raw = tile([P, 2, H], U8, "wcs_raw")
+        wcs_raw = tile([P, 2, GROUP], U8, "wcs_raw")
         wc_w = [tile([P, 2, GROUP], U16, "wc_w%d" % b) for b in range(2)]
         wc_s = tile([P, 2, 2, GROUP], U8, "wc_s")
         w1_raw = [
@@ -96,7 +96,12 @@ def tile_list_flow_congestion_routing_kernel(
         nc.vector.memset(tab_s[QUAD : 2 * QUAD, :].bitcast(I32), 0)
         nc.vector.memset(tab_s[2 * QUAD : P, :].bitcast(I32), 0)
         nc.gpsimd.memset(v_s[:].bitcast(I32), 0)
-        nc.gpsimd.memset(w2s_raw[2 * QUAD : P, :].bitcast(I32), 0)
+        nc.gpsimd.memset(w2s_raw[3 * QUAD : P, :].bitcast(I32), 0)
+        nc.gpsimd.memset(wc_s[:, 1, :, :].bitcast(I32), 0)
+        nc.gpsimd.dma_start(
+            out=w2s_raw[2 * QUAD : 3 * QUAD, :].bitcast(I32),
+            in_=wc_scales[:, :, GROUP:].rearrange("a q c -> q a c").bitcast(I32),
+        )
         nc.gpsimd.dma_start(
             out=w2s_raw[0 : 2 * QUAD, :].bitcast(I32),
             in_=w2_scales.rearrange("b q (g c) -> (q g) b c", g=2).bitcast(I32),
@@ -119,7 +124,7 @@ def tile_list_flow_congestion_routing_kernel(
         for q in QUADRANTS:
             nc.sync.dma_start(
                 out=wcs_raw[QUAD * q : QUAD * q + 4, :, :].bitcast(I32),
-                in_=wc_scales[:, 4 * q : 4 * q + 4, :].rearrange("a r c -> r a c").bitcast(I32),
+                in_=wc_scales[:, 4 * q : 4 * q + 4, 0:GROUP].rearrange("a r c -> r a c").bitcast(I32),
             )
         load_table(0)
         nc.sync.dma_start(pos1_sb[:], pos1)
@@ -142,11 +147,18 @@ def tile_list_flow_congestion_routing_kernel(
                 in_=wc_raw[b][:].bitcast(U16).rearrange("p a (c i t) -> p a c t i", t=4, i=LINE // 2),
             )
 
-        def deal_wc_scales(b):
+        def deal_wc_scales():
             nc.vector.tensor_copy(
-                out=wc_s[:, b, :, :].rearrange("p a (t c i) -> p a c t i", t=4, i=LINE),
-                in_=wcs_raw[:, :, GROUP * b : GROUP * (b + 1)].rearrange("p a (c i t) -> p a c t i", t=4, i=LINE),
+                out=wc_s[:, 0, :, :].rearrange("p a (t c i) -> p a c t i", t=4, i=LINE),
+                in_=wcs_raw[:].rearrange("p a (c i t) -> p a c t i", t=4, i=LINE),
             )
+
+        def move_wc_scales():
+            for q in QUADRANTS:
+                nc.sync.dma_start(
+                    out=wc_s[QUAD * q : QUAD * q + 4, 1, :, :].bitcast(I32),
+                    in_=w2s_dealt[2 * QUAD + 8 * q : 2 * QUAD + 8 * q + 8, :].bitcast(I32),
+                )
 
         def deal_w2_words(b, g):
             cols = slice(GROUP * g, GROUP * (g + 1))
@@ -194,12 +206,12 @@ def tile_list_flow_congestion_routing_kernel(
         wc_raw.append(tile([P, 2, GROUP // 2], I32, "wc_raw1", "picked_s"))
         load_wc(1)
         deal_wc_words(nc.vector.tensor_copy, 0)
-        deal_wc_scales(0)
+        deal_wc_scales()
         gather_words(0, 0)
         gather_words(0, 1)
         load_w1(1, 0)
-        deal_wc_scales(1)
         deal_w2_scales()
+        move_wc_scales()
         gather_words(1, 0, 0, QUARTER)
         gather_words(1, 0, QUARTER, BANK)
         gather_words(1, 1)

@@ -27,7 +27,7 @@ AHEAD = 3
 QUARTER = BANK // 2
 H_RING = 4
 QUADRANTS = (0, 2, 1, 3)
-ON_GPSIMD = ((3, 0), (3, 1), (5, 0), (5, 1), (6, 0), (6, 1), (7, 0))
+ON_GPSIMD = ((3, 0), (3, 1), (5, 0), (5, 1), (6, 0), (6, 1), (7, 0), (7, 1))
 Y_BANKS = (3, 1, 0, 2)
 W1_FIRST_AT = 0
 WC_SECOND_AT = W1_FIRST_AT + 4 * 4 * GROUP
@@ -236,21 +236,28 @@ def tile_list_flow_congestion_routing_kernel(
         ]
         h[5] = picked[0][:, 0:S]
         w1_bf1 = [w1_bf0[1], w1_bf0[0]]
-        load_sb = {(u, s): tile([P, BANK], F32, "load_sb%d%d" % (u, s)) for u, s in ON_GPSIMD}
+        load_sb = {(u, s): tile([P, BANK], F32, "load_sb%d%d" % (u, s)) for u, s in ON_GPSIMD if u != 5}
+        load_sb5 = tile([P, S], F32, "load_sb5")
+        damp5 = tile([P, S], F32, "damp5")
         damp = []
         for u in range(SLICES):
             if u in (1, 2):
                 damp.append([slots[0][i][:, u - 1, :] for i in range(2)])
+            elif u == 5:
+                damp.append([damp5[:, BANK * s : BANK * (s + 1)] for s in range(2)])
+            elif u == 4:
+                damp.append([w1_bf[:, 2 * BANK * s : 2 * BANK * (s + 1)].bitcast(F32) for s in range(2)])
             else:
                 own = tile([P, S], F32, "damp%d" % u)
                 damp.append([own[:, BANK * s : BANK * (s + 1)] for s in range(2)])
         w1_w1 = tile([P, 2 * GROUP], U32, "w1_w1", "damp3")
         w1_w.append([w1_w1[:, GROUP * (1 - a) : GROUP * (2 - a)] for a in range(2)])
+        root4 = tile([P, S], F32, "root4")
         last_root = tile([P, BANK], F32, "last_root")
         w2_w = tile([P, 2, N], U32, "w2_w", "last_root")
         z_bf1 = [picked[0][:, 8 * PAIRS - HALF :].bitcast(BF16), tile([P, 4 * HALF], BF16, "z_bf11")[:]]
         z_w = [
-            [tile([P, HALF], U32, "z_w00", "load_sb70"), tile([P, HALF], U32, "z_w01", "h%d" % (7 % H_RING))],
+            [tile([P, HALF], U32, "z_w00", "load_sb71"), tile([P, HALF], U32, "z_w01", "h%d" % (7 % H_RING))],
             [tile([P, HALF], U32, "z_w1%d" % s) for s in range(2)],
         ]
         z_s = [[tile([P, HALF], U8, "z_s%d%d" % (b, s)) for s in range(2)] for b in range(2)]
@@ -294,6 +301,8 @@ def tile_list_flow_congestion_routing_kernel(
             first_product(load_bank, u, words, lambda a: w1_s[b][a][:, cols], order)
 
         def root_of(u, s):
+            if u == 4:
+                return root4[:, BANK * s : BANK * (s + 1)]
             return last_root[:] if (u, s) == (SLICES - 1, 1) else damp[u][s]
 
         def magnitude(u, s):
@@ -414,8 +423,12 @@ def tile_list_flow_congestion_routing_kernel(
         nc.vector.quantize_mx(out=w1_w1[:].bitcast(FP8X4), scales=w1_s1[:], in_=w1_bf[:])
         pick(3, 0)
         pick(3, 1)
-        cap_stage(4)
-        z_bf0 = tile([P, 4 * PAIRS], BF16, "z_bf0")
+        cap_product(4)
+        for step in (magnitude, inverse_root):
+            for s in range(2):
+                step(4, s)
+        nc.gpsimd.tensor_tensor(out=w1_bf[:, 0 : 2 * S].bitcast(F32), in0=root4[:], in1=root4[:], op=ALU.mult)
+        z_bf0 = tile([P, 4 * PAIRS], BF16, "z_bf0", "root4")
         maximum(0, 0, PAIRS, z_bf0[:])
 
         load_product(5)
@@ -423,7 +436,13 @@ def tile_list_flow_congestion_routing_kernel(
         pick(4, 0)
         pick(4, 1)
         cap_product(5)
-        finish_slice(5)
+        for step in (magnitude, inverse_root):
+            for s in range(2):
+                step(5, s)
+        for s in range(2):
+            square(5, s)
+            nc.scalar.copy(out=load_sb5[:, BANK * s : BANK * (s + 1)], in_=load_bank(5, s)[:])
+        nc.gpsimd.tensor_tensor(out=h[5], in0=load_sb5[:], in1=damp5[:], op=ALU.mult)
         pick(5, 0)
         pick(5, 1)
         whole_slice(6)

from contextlib import ExitStack

import concourse.mybir as mybir

K, T, S, H, PAIRS, N = 1024, 4096, 1024, 1024, 512, 1024
FLOPS = 2 * K * H * S * 2 + 2 * H * N * PAIRS

F32 = mybir.dt.float32
BF16 = mybir.dt.bfloat16
I32 = mybir.dt.int32
U32 = mybir.dt.uint32
U16 = mybir.dt.uint16
U8 = mybir.dt.uint8
FP8X4 = mybir.dt.float8_e4m3fn_x4
FP4X4 = mybir.dt.float4_e2m1fn_x4
ACT = mybir.ActivationFunctionType
ALU = mybir.AluOpType

P = 128
QUAD = 32
LINE = 16
GROUP = 512
BANK = 512
HALF = PAIRS // 2
SLICES = H // P
AHEAD = 3
QUARTER = BANK // 2
H_RING = 4
QUADRANTS = (0, 2, 1, 3)
ON_GPSIMD = ((3, 0), (3, 1), (5, 0), (5, 1), (6, 0), (6, 1), (7, 0), (7, 1))
Y_BANKS = (3, 1, 0, 2)
W1_FIRST_AT = 0
WC_SECOND_AT = W1_FIRST_AT + 4 * 4 * GROUP
TAB_SECOND_AT = WC_SECOND_AT + 4 * GROUP
TAB_SCALES_AT = WC_SECOND_AT - 2 * GROUP
TAB_FIRST_AT = TAB_SECOND_AT + 4 * T
W2_SCALES_AT = TAB_FIRST_AT + 4 * 4 * GROUP


def tile_list_flow_congestion_routing_kernel(
    tc, tab_words, tab_scales, offs, pos1, pos2, w1, wc_words, wc_scales, w2_words, w2_scales, b2, out_0, out_1, out_2
):
    nc = tc.nc
    with ExitStack() as ctx:
        sb = ctx.enter_context(tc.tile_pool(name="sb", bufs=1))
        shared = ctx.enter_context(tc.tile_pool(name="shared", bufs=1))
        ps = ctx.enter_context(tc.psum_pool(name="ps", bufs=1))

        def tile(shape, dtype, name, buffer=None):
            return sb.tile(shape, dtype, name=name, tag=buffer or name, align_bytes=64)

        def placed(shape, dtype, name, offset):
            return shared.tile(shape, dtype, name=name, align_bytes=64, offset=offset)

        offs_sb = sb.tile([P, S // 16], U16, name="offs_sb")
        pos1_sb = sb.tile([P, PAIRS // 16], U16, name="pos1_sb")
        pos2_sb = sb.tile([P, PAIRS // 16], U16, name="pos2_sb")
        banks = [ps.tile([P, BANK], F32, name="bank%d" % i) for i in range(8)]

        tab_s = placed([P, T], U8, "tab_s", TAB_SCALES_AT)
        tab_w = [placed([P, T], I32, "tab_w0", TAB_FIRST_AT), placed([P, T], I32, "tab_w1", TAB_SECOND_AT)]
        picked_s = tile([P, S], U8, "picked_s")
        v_w = [[tile([P, BANK], U32, "v_w%d%d" % (a, s)) for s in range(2)] for a in range(2)]
        v_s = tile([P, 2, S], U8, "v_s")
        wc_raw = [
            tile([P, 2, GROUP // 2], I32, "wc_raw0", "wc_raw"),
        ]
        wcs_raw = tile([P, 2, GROUP], U8, "wcs_raw")
        wc_w = [tile([P, 2, GROUP], U16, "wc_w%d" % b) for b in range(2)]
        wc_s = tile([P, 2, 2, GROUP], U8, "wc_s")
        w1_raw = [
            [placed([P, 4, GROUP], F32, "w1_raw00", W1_FIRST_AT), tile([P, 4, GROUP], F32, "w1_raw01", "wc_raw")],
            [
                placed([P, 4, GROUP], F32, "w1_raw10", TAB_FIRST_AT),
                placed([P, 4, GROUP], F32, "w1_raw11", TAB_SECOND_AT),
            ],
        ]
        w1_bf = tile([P, 8 * GROUP], BF16, "w1_bf")
        w1_bf0 = [w1_bf[:, 4 * GROUP * a : 4 * GROUP * (a + 1)] for a in range(2)]
        w1_w = [[tile([P, GROUP], U32, "w1_w0%d" % a) for a in range(2)]]
        w1_s1 = tile([P, 2 * GROUP], U8, "w1_s1")
        w1_s = [
            [tile([P, GROUP], U8, "w1_s0%d" % a) for a in range(2)],
            [w1_s1[:, GROUP * (1 - a) : GROUP * (2 - a)] for a in range(2)],
        ]
        w2_raw = tile([P, 2, N], I32, "w2_raw", "wc_raw")
        w2s_raw = tile([P, GROUP], U8, "w2s_raw")
        w2s_dealt = placed([P, GROUP], U8, "w2s_dealt", W2_SCALES_AT)
        w2_s = wc_s
        bias = placed([P, 2, 4], F32, "bias", W1_FIRST_AT)

        warm = tile([P, 2], F32, "warm")
        nc.vector.memset(warm[:, 0:1], 0.0)
        nc.scalar.activation(out=warm[:, 1:2], in_=warm[:, 0:1], func=ACT.Abs_reciprocal_sqrt, bias=1.0)
        nc.gpsimd.memset(wcs_raw[:].bitcast(I32), 0)
        nc.vector.memset(tab_s[QUAD : 2 * QUAD, :].bitcast(I32), 0)
        nc.vector.memset(tab_s[2 * QUAD : P, :].bitcast(I32), 0)
        nc.gpsimd.memset(v_s[:].bitcast(I32), 0)
        nc.gpsimd.memset(w2s_raw[3 * QUAD : P, :].bitcast(I32), 0)
        nc.gpsimd.memset(wc_s[:, 1, :, :].bitcast(I32), 0)
        nc.gpsimd.dma_start(
            out=w2s_raw[2 * QUAD : 3 * QUAD, :].bitcast(I32),
            in_=wc_scales[:, :, GROUP:].rearrange("a q c -> q a c").bitcast(I32),
        )
        nc.gpsimd.dma_start(
            out=w2s_raw[0 : 2 * QUAD, :].bitcast(I32),
            in_=w2_scales.rearrange("b q (g c) -> (q g) b c", g=2).bitcast(I32),
        )

        def load_table(a):
            nc.sync.dma_start(out=tab_w[a][:], in_=tab_words[a].rearrange("p t i -> p (t i)").bitcast(I32))

        def load_wc(b):
            words = wc_words.rearrange("a p c -> p a c")[:, :, 2 * GROUP * b : 2 * GROUP * (b + 1)]
            nc.sync.dma_start(out=wc_raw[b][:], in_=words.bitcast(I32))

        def load_w1(b, a, lo=0, hi=GROUP):
            rows = w1[GROUP * a : GROUP * (a + 1), GROUP * b + lo : GROUP * b + hi]
            nc.sync.dma_start(out=w1_raw[b][a][:, :, lo:hi], in_=rows.rearrange("(p j) c -> p j c", j=4))

        nc.sync.dma_start(offs_sb[:], offs)
        nc.sync.dma_start(out=tab_s[0:QUAD, :].bitcast(I32), in_=tab_scales.rearrange("a q t -> q a t").bitcast(I32))
        load_wc(0)
        for q in QUADRANTS:
            nc.sync.dma_start(
                out=wcs_raw[QUAD * q : QUAD * q + 4, :, :].bitcast(I32),
                in_=wc_scales[:, 4 * q : 4 * q + 4, 0:GROUP].rearrange("a r c -> r a c").bitcast(I32),
            )
        load_table(0)
        nc.sync.dma_start(pos1_sb[:], pos1)
        nc.sync.dma_start(pos2_sb[:], pos2)

        nc.vector.tensor_copy(picked_s[:], tab_s[:].indirect(offs_sb[:]))
        for q in QUADRANTS:
            nc.sync.dma_start(
                out=v_s[QUAD * q : QUAD * q + 4, :, :].bitcast(I32), in_=picked_s[8 * q : 8 * q + 8, :].bitcast(I32)
            )
        load_table(1)

        def gather_words(a, s, lo=0, hi=BANK):
            entries = offs_sb[:, (BANK * s + lo) // 16 : (BANK * s + hi) // 16]
            nc.vector.tensor_copy(v_w[a][s][:, lo:hi], tab_w[a][:].bitcast(U32).indirect(entries))

        def deal_wc_words(copy, b):
            copy(
                out=wc_w[b][:].rearrange("p a (t c i) -> p a c t i", t=4, i=LINE // 2),
                in_=wc_raw[b][:].bitcast(U16).rearrange("p a (c i t) -> p a c t i", t=4, i=LINE // 2),
            )

        def deal_wc_scales():
            nc.vector.tensor_copy(
                out=wc_s[:, 0, :, :].rearrange("p a (t c i) -> p a c t i", t=4, i=LINE),
                in_=wcs_raw[:].rearrange("p a (c i t) -> p a c t i", t=4, i=LINE),
            )

        def move_wc_scales():
            for q in QUADRANTS:
                nc.sync.dma_start(
                    out=wc_s[QUAD * q : QUAD * q + 4, 1, :, :].bitcast(I32),
                    in_=w2s_dealt[2 * QUAD + 8 * q : 2 * QUAD + 8 * q + 8, :].bitcast(I32),
                )

        def deal_w2_words(b, g):
            cols = slice(GROUP * g, GROUP * (g + 1))
            nc.scalar.copy(
                out=w2_w[:, b, cols].rearrange("p (t c i) -> p c t i", t=4, i=LINE // 4),
                in_=w2_raw[:, b, cols].bitcast(U32).rearrange("p (c i t) -> p c t i", t=4, i=LINE // 4),
            )

        def deal_w2_scales():
            nc.vector.tensor_copy(
                out=w2s_dealt[:].rearrange("p (t c i) -> p c t i", t=4, i=LINE),
                in_=w2s_raw[:].rearrange("p (c i t) -> p c t i", t=4, i=LINE),
            )

        def move_w2_scales():
            for q in QUADRANTS:
                nc.sync.dma_start(
                    out=w2_s[QUAD * q : QUAD * q + 4, :, :, :].rearrange("r g b c -> r (g b c)").bitcast(I32),
                    in_=w2s_dealt[16 * q : 16 * q + 16, :].bitcast(I32),
                )

        def round_w1(copy, rounded, raw, lo, hi):
            copy(
                out=rounded.rearrange("p (t m j) -> p m t j", t=4, j=4)[:, lo // 4 : hi // 4, :, :],
                in_=raw[:, :, lo:hi].rearrange("p j (m t) -> p m t j", t=4),
            )

        def round_w1_by_lines(rounded, raw, lo, hi):
            nc.vector.tensor_copy(
                out=rounded.rearrange("p (t m j) -> p m j t", t=4, j=4)[:, lo // 4 : hi // 4, :, :],
                in_=raw[:, :, lo:hi].rearrange("p j (m t) -> p m j t", t=4),
            )

        def gpsimd_copy(out, in_):
            nc.gpsimd.tensor_scalar(out=out, in0=in_, scalar1=1.0, scalar2=0.0, op0=ALU.mult, op1=ALU.add)

        def quantize_w1(b, a, rounded, lo, hi):
            nc.vector.quantize_mx(
                out=w1_w[b][a][:, lo:hi].bitcast(FP8X4), scales=w1_s[b][a][:, lo:hi], in_=rounded[:, 4 * lo : 4 * hi]
            )

        load_w1(0, 0)
        load_w1(0, 1, 0, GROUP // 2)
        load_w1(0, 1, GROUP // 2, GROUP)
        wc_raw.append(tile([P, 2, GROUP // 2], I32, "wc_raw1", "picked_s"))
        load_wc(1)
        deal_wc_words(nc.vector.tensor_copy, 0)
        deal_wc_scales()
        gather_words(0, 0)
        gather_words(0, 1)
        load_w1(1, 0)
        deal_w2_scales()
        move_wc_scales()
        gather_words(1, 0, 0, QUARTER)
        gather_words(1, 0, QUARTER, BANK)
        gather_words(1, 1)
        load_w1(1, 1)
        round_w1_by_lines(w1_bf0[0], w1_raw[0][0], 0, GROUP)
        round_w1_by_lines(w1_bf0[1], w1_raw[0][1], 0, GROUP // 2)
        quantize_w1(0, 0, w1_bf0[0], 0, GROUP)
        round_w1_by_lines(w1_bf0[1], w1_raw[0][1], GROUP // 2, GROUP)
        quantize_w1(0, 1, w1_bf0[1], 0, GROUP // 2)
        deal_wc_words(nc.vector.tensor_copy, 1)
        w1_last = tile([P, GROUP // 2], U32, "w1_last", "picked_s")
        nc.vector.quantize_mx(
            out=w1_last[:].bitcast(FP8X4), scales=w1_s[0][1][:, GROUP // 2 :], in_=w1_bf0[1][:, 2 * GROUP :]
        )

        ring = [tile([P, S], F32, "h%d" % i) for i in range(H_RING)]
        h = [ring[u % H_RING][:] for u in range(SLICES)]
        picked = [tile([P, 8 * PAIRS + HALF], F32, "picked0"), tile([P, 8 * PAIRS], F32, "picked1")]
        slots = [
            [picked[i][:, 4 * PAIRS * b : 4 * PAIRS * (b + 1)].rearrange("p (t j) -> p t j", t=4) for i in range(2)]
            for b in range(2)
        ]
        h[5] = picked[0][:, 0:S]
        w1_bf1 = [w1_bf0[1], w1_bf0[0]]
        load_sb = {(u, s): tile([P, BANK], F32, "load_sb%d%d" % (u, s)) for u, s in ON_GPSIMD if u != 5}
        load_sb5 = tile([P, S], F32, "load_sb5")
        damp5 = tile([P, S], F32, "damp5")
        damp = []
        for u in range(SLICES):
            if u in (1, 2):
                damp.append([slots[0][i][:, u - 1, :] for i in range(2)])
            elif u == 5:
                damp.append([damp5[:, BANK * s : BANK * (s + 1)] for s in range(2)])
            elif u == 4:
                damp.append([w1_bf[:, 2 * BANK * s : 2 * BANK * (s + 1)].bitcast(F32) for s in range(2)])
            else:
                own = tile([P, S], F32, "damp%d" % u)
                damp.append([own[:, BANK * s : BANK * (s + 1)] for s in range(2)])
        w1_w1 = tile([P, 2 * GROUP], U32, "w1_w1", "damp3")
        w1_w.append([w1_w1[:, GROUP * (1 - a) : GROUP * (2 - a)] for a in range(2)])
        root4 = tile([P, S], F32, "root4")
        last_root = tile([P, BANK], F32, "last_root")
        w2_w = tile([P, 2, N], U32, "w2_w", "last_root")
        z_bf1 = [picked[0][:, 8 * PAIRS - HALF :].bitcast(BF16), tile([P, 4 * HALF], BF16, "z_bf11")[:]]
        z_w = [
            [tile([P, HALF], U32, "z_w00", "load_sb71"), tile([P, HALF], U32, "z_w01", "h%d" % (7 % H_RING))],
            [tile([P, HALF], U32, "z_w1%d" % s) for s in range(2)],
        ]
        z_s = [[tile([P, HALF], U8, "z_s%d%d" % (b, s)) for s in range(2)] for b in range(2)]

        def cap_bank(u, s):
            return banks[2 * (u % 4 if u < SLICES - 1 else 0) + s]

        def load_bank(u, s):
            return banks[2 * ((u - 1) % 4) + s]

        def first_product(bank, u, words, scales, order):
            for s in range(2):
                for a in order:
                    nc.tensor.matmul_mx(
                        out=bank(u, s)[:],
                        lhsT=words(a),
                        lhsT_scale=scales(a),
                        rhs=v_w[a][s][:].bitcast(FP8X4),
                        rhs_scale=v_s[:, a, BANK * s : BANK * (s + 1)],
                        start=(a == order[0]),
                        stop=(a == order[1]),
                    )

        def cap_product(u):
            b, t = divmod(u, 4)
            cols = slice(P * t, P * (t + 1))
            first_product(
                cap_bank, u, lambda a: wc_w[b][:, a, cols].bitcast(FP4X4), lambda a: wc_s[:, b, a, cols], (0, 1)
            )

        def load_product(u):
            b, t = divmod(u, 4)
            cols = slice(P * t, P * (t + 1))
            order = (0, 1) if u == 0 else (1, 0)

            def words(a):
                if (b, a) == (0, 1) and t >= 2:
                    return w1_last[:, P * (t - 2) : P * (t - 1)].bitcast(FP8X4)
                return w1_w[b][a][:, cols].bitcast(FP8X4)

            first_product(load_bank, u, words, lambda a: w1_s[b][a][:, cols], order)

        def root_of(u, s):
            if u == 4:
                return root4[:, BANK * s : BANK * (s + 1)]
            return last_root[:] if (u, s) == (SLICES - 1, 1) else damp[u][s]

        def magnitude(u, s):
            nc.scalar.activation(out=root_of(u, s), in_=cap_bank(u, s)[:], func=ACT.Abs)

        def inverse_root(u, s):
            nc.scalar.activation(out=root_of(u, s), in_=root_of(u, s), func=ACT.Abs_reciprocal_sqrt, bias=1.0)

        def square(u, s):
            nc.scalar.activation(out=damp[u][s], in_=root_of(u, s), func=ACT.Square)

        def cap_stage(u):
            cap_product(u)
            for step in (magnitude, inverse_root, square):
                for s in range(2):
                    step(u, s)

        def first_cap_stage():
            parts = (
                (load_bank(0, 0)[:, 0:QUARTER], 0, 0, QUARTER),
                (cap_bank(0, 0)[:, 0:QUARTER], 0, QUARTER, BANK),
                (cap_bank(0, 1)[:], 1, 0, BANK),
            )
            for bank, s, lo, hi in parts:
                for a in range(2):
                    nc.tensor.matmul_mx(
                        out=bank,
                        lhsT=wc_w[0][:, a, 0:P].bitcast(FP4X4),
                        lhsT_scale=wc_s[:, 0, a, 0:P],
                        rhs=v_w[a][s][:, lo:hi].bitcast(FP8X4),
                        rhs_scale=v_s[:, a, BANK * s + lo : BANK * s + hi],
                        start=(a == 0),
                        stop=(a == 1),
                    )
            for bank, s, lo, hi in parts:
                part = damp[0][s][:, lo:hi]
                nc.scalar.activation(out=part, in_=bank, func=ACT.Abs)
                nc.scalar.activation(out=part, in_=part, func=ACT.Abs_reciprocal_sqrt, bias=1.0)
                nc.scalar.activation(out=part, in_=part, func=ACT.Square)

        def multiply(u, s):
            half = h[u][:, BANK * s : BANK * (s + 1)]
            if (u, s) in ON_GPSIMD:
                nc.scalar.copy(out=load_sb[u, s][:], in_=load_bank(u, s)[:])
                nc.gpsimd.tensor_tensor(out=half, in0=load_sb[u, s][:], in1=damp[u][s], op=ALU.mult)
            else:
                nc.vector.tensor_tensor(out=half, in0=load_bank(u, s)[:], in1=damp[u][s], op=ALU.mult)

        def load_stage(u):
            load_product(u)
            for s in range(2):
                multiply(u, s)

        def finish_slice(u):
            for step in (magnitude, inverse_root):
                for s in range(2):
                    step(u, s)
            for s in range(2):
                square(u, s)
                multiply(u, s)

        def whole_slice(u):
            cap_product(u)
            load_product(u)
            finish_slice(u)

        def pick(u, i, lo=0, hi=PAIRS):
            b, t = divmod(u, 4)
            entries = (pos1_sb, pos2_sb)[i][:, lo // 16 : hi // 16]
            nc.vector.tensor_copy(slots[b][i][:, t, lo:hi], h[u].indirect(entries))

        def maximum(b, lo, hi, rounded):
            nc.vector.tensor_tensor(
                out=rounded.rearrange("p (c i t) -> p c t i", t=4, i=4),
                in0=slots[b][0][:, :, lo:hi].rearrange("p t (c i) -> p c t i", i=4),
                in1=slots[b][1][:, :, lo:hi].rearrange("p t (c i) -> p c t i", i=4),
                op=ALU.max,
            )

        def quantize_z(b, s, rounded):
            nc.vector.quantize_mx(out=z_w[b][s][:].bitcast(FP8X4), scales=z_s[b][s][:], in_=rounded)

        def y_psum(s, g, t):
            return banks[2 * Y_BANKS[2 * s + g] + t // 2][:, HALF * (t % 2) : HALF * (t % 2 + 1)]

        def y_passes(b, s):
            for g in range(2):
                for t in range(4):
                    nc.tensor.matmul_mx(
                        out=y_psum(s, g, t),
                        lhsT=w2_w[:, b, GROUP * g + P * t : GROUP * g + P * (t + 1)].bitcast(FP8X4),
                        lhsT_scale=w2_s[:, g, b, P * t : P * (t + 1)],
                        rhs=z_w[b][s][:].bitcast(FP8X4),
                        rhs_scale=z_s[b][s][:],
                        start=(b == 0 and t % 2 == 0),
                        stop=(b == 1 and t % 2 == 1),
                    )

        def prepare_second_group():
            for a in range(2):
                round_w1(gpsimd_copy, w1_bf1[a], w1_raw[1][a], 0, GROUP)
            nc.sync.dma_start(out=w2_raw[:], in_=w2_words.rearrange("b p n i -> p b (n i)").bitcast(I32))
            nc.sync.dma_start(out=bias[:], in_=b2.rearrange("(g p t) -> p g t", g=2, t=4))

        first_cap_stage()
        for u in range(1, AHEAD):
            cap_stage(u)
        load_stage(0)
        load_stage(1)
        prepare_second_group()
        pick(0, 0)
        pick(0, 1)
        load_stage(2)
        for u in (1, 2):
            pick(u, 0)
            pick(u, 1)
        whole_slice(3)
        nc.vector.quantize_mx(out=w1_w1[:].bitcast(FP8X4), scales=w1_s1[:], in_=w1_bf[:])
        pick(3, 0)
        pick(3, 1)
        cap_product(4)
        for step in (magnitude, inverse_root):
            for s in range(2):
                step(4, s)
        nc.gpsimd.tensor_tensor(out=w1_bf[:, 0 : 2 * S].bitcast(F32), in0=root4[:], in1=root4[:], op=ALU.mult)
        z_bf0 = tile([P, 4 * PAIRS], BF16, "z_bf0", "root4")
        maximum(0, 0, PAIRS, z_bf0[:])

        load_product(5)
        load_stage(4)
        pick(4, 0)
        pick(4, 1)
        cap_product(5)
        for step in (magnitude, inverse_root):
            for s in range(2):
                step(5, s)
        for s in range(2):
            square(5, s)
            nc.scalar.copy(out=load_sb5[:, BANK * s : BANK * (s + 1)], in_=load_bank(5, s)[:])
        nc.gpsimd.tensor_tensor(out=h[5], in0=load_sb5[:], in1=damp5[:], op=ALU.mult)
        pick(5, 0)
        pick(5, 1)
        whole_slice(6)
        pick(6, 0)
        pick(6, 1)
        whole_slice(7)
        move_w2_scales()
        for b in range(2):
            for g in range(2):
                deal_w2_words(b, g)
        pick(7, 0, 0, HALF)
        pick(7, 1, 0, HALF)
        quantize_z(0, 0, z_bf0[:, 0 : 4 * HALF])

        y = [tile([P, 2, 4, HALF], F32, "y%d" % s) for s in range(2)]
        y_bf = [tile([P, 2, 4 * HALF], BF16, "y_bf0", "z_bf11"), tile([P, 2, 4 * HALF], BF16, "y_bf1")]
        y_w = [tile([P, 2, HALF], I32, "y_w%d" % s) for s in range(2)]
        y_s = tile([P, 2, PAIRS], U8, "y_s")

        def add_bias(s, g, lo=0, hi=HALF):
            for t in range(4):
                nc.scalar.activation(
                    out=y[s][:, g, t, lo:hi],
                    in_=y_psum(s, g, t)[:, lo:hi],
                    func=ACT.Identity,
                    bias=bias[:, g, t : t + 1],
                )

        def store_y(s, g):
            rows = out_0[GROUP * g : GROUP * (g + 1), HALF * s : HALF * (s + 1)].rearrange("(p t) j -> p t j", t=4)
            for t in (0, 2):
                nc.sync.dma_start(out=rows[:, t : t + 2, :], in_=y[s][:, g, t : t + 2, :])

        def round_y(copy, s, g, lo=0, hi=HALF):
            copy(
                out=y_bf[s][:, g, 4 * lo : 4 * hi].rearrange("p (c i t) -> p c t i", t=4, i=4),
                in_=y[s][:, g, :, lo:hi].rearrange("p t (c i) -> p c t i", i=4),
            )

        def quantize_y(s, g, lo=0, hi=HALF):
            nc.vector.quantize_mx(
                out=y_w[s][:, g, lo:hi].bitcast(FP8X4),
                scales=y_s[:, g, HALF * s + lo : HALF * s + hi],
                in_=y_bf[s][:, g, 4 * lo : 4 * hi],
            )

        def store_codes(s):
            words = out_1.rearrange("g p m t -> p g (m t)").bitcast(I32)
            nc.sync.dma_start(out=words[:, :, HALF * s : HALF * (s + 1)], in_=y_w[s][:])

        y_passes(0, 0)
        maximum(1, 0, HALF, z_bf1[0])
        pick(7, 1, HALF, PAIRS)
        quantize_z(1, 0, z_bf1[0])
        y_passes(1, 0)
        pick(7, 0, HALF, PAIRS)
        quantize_z(0, 1, z_bf0[:, 4 * HALF : 8 * HALF])
        y_passes(0, 1)
        maximum(1, HALF, PAIRS, z_bf1[1])
        quantize_z(1, 1, z_bf1[1])
        for g in range(2):
            add_bias(0, g)
            store_y(0, g)
        for g in range(2):
            round_y(nc.vector.tensor_copy, 0, g)
        for g in range(2):
            quantize_y(0, g)
        store_codes(0)
        y_passes(1, 1)
        add_bias(1, 0)
        store_y(1, 0)
        round_y(nc.vector.tensor_copy, 1, 0)
        add_bias(1, 1, 0, HALF // 2)
        round_y(nc.vector.tensor_copy, 1, 1, 0, HALF // 2)
        quantize_y(1, 0)
        quantize_y(1, 1, 0, HALF // 2)
        add_bias(1, 1, HALF // 2, HALF)
        store_y(1, 1)
        round_y(nc.scalar.copy, 1, 1, HALF // 2, HALF)
        quantize_y(1, 1, HALF // 2, HALF)
        store_codes(1)
        for q in QUADRANTS:
            queue = nc.sync if q < 2 else nc.scalar
            queue.dma_start(
                out=out_2[:, 4 * q : 4 * q + 4, :].rearrange("g r m -> r g m").bitcast(I32),
                in_=y_s[QUAD * q : QUAD * q + 4, :, :].bitcast(I32),
            )
